import numpy as np, ml_dtypes
CORES = [40,41,42,43,44,45,46,47]
N = 8
import mx_ref
BF = ml_dtypes.bfloat16
def gcols(t, e):
    v = np.concatenate([t.reshape(8, 16, -1, 4), np.zeros((8, 16, 1, 4), BF)], axis=2)
    return np.ascontiguousarray(np.stack([v[g][:, e[g]] for g in range(8)])).reshape(128, -1)
def tile(rs):
    return np.stack(rs, axis=2).reshape(128, -1).astype(BF)
def cut(t, i, w=512):
    return t[:, w * i:w * i + w]
def pick(q, e):
    c = np.concatenate([q[0].reshape(128, -1, 4), np.zeros((128, 1, 4), np.uint8)], axis=1); s = np.concatenate([q[1], np.ones((16, 1), np.uint8)], axis=1)
    return (np.ascontiguousarray(c[:, e].reshape(128, -1)), np.ascontiguousarray(s[:, e]))
def join(*qs):
    return (np.concatenate([q[0] for q in qs], axis=1), np.concatenate([q[1] for q in qs], axis=1))
def put(q, e, v):
    c, s = q[0].reshape(128, -1, 4).copy(), q[1].copy(); c[:, e] = v[0].reshape(128, -1, 4); s[:, e] = v[1]
    return (c.reshape(128, -1), s)
def pk(c, s):
    return (np.ascontiguousarray(c), mx_ref.live(s))
def emit(q):
    return q[0], q[1]
def packed(v, rng):
    q = [mx_ref.quantize(np.ascontiguousarray(v[r])) for r in range(N)]
    return np.stack([a for a, b in q]), np.stack([mx_ref.plane(b, rng) for a, b in q])
def values_of_codes():
    e, c = np.zeros((128, 128, 4), np.float32), np.zeros((128, 2, 4), np.uint8)
    e[np.arange(128), np.arange(128), 0] = 1
    c[:127, :, 0] = np.arange(256).reshape(2, 128).T[:127]
    return mx_ref.matmul(mx_ref.quantize(e.reshape(128, 512).astype(BF)), (c.reshape(128, 8), np.full((16, 2), 127, np.uint8))).T.reshape(-1).astype(np.float64)
CODE_VALUE, SCALE_VALUE = values_of_codes(), 2.0 ** (np.arange(256) - 127.0)
def decode(q):
    return (CODE_VALUE[q[0]].reshape(16, 8, -1, 4) * SCALE_VALUE[q[1]][:, None, :, None] + 0.0).reshape(128, -1).astype(np.float32)
def f(rng, *shape):
    return mx_ref.flush((rng.standard_normal(shape, dtype=np.float32) * np.exp2(rng.integers(-2, 3, shape[:-1] + (1,)))).astype(BF))
def wide(rng, *shape, cols=0):
    v = rng.standard_normal(shape, dtype=np.float32) * np.exp2(rng.integers(-12, 13, shape)).astype(np.float32)
    if cols: v *= np.repeat(np.exp2(rng.integers(-cols, cols + 1, shape[:-2] + (1, shape[-1] // 4))) * (rng.random(shape[:-2] + (1, shape[-1] // 4)) > 0.0625), 4, axis=-1).astype(np.float32)
    return mx_ref.flush(v.astype(BF))
C, K, R = 448, 128, 2
def turned(s, t):
    s = s + np.float32(0.0)
    k, g = np.arange(C), np.arange(8)
    above = (s[:, None, :] > s[:, :, None]) | (s[:, None, :] == s[:, :, None]) & (k[None, :] < k[:, None])
    low = np.max(np.where(above & (k[None, :] < k[:, None]), k, -1), axis=2) + 1
    high = np.min(np.where(above & (k[None, :] > k[:, None]), k, C), axis=2) - 1
    at = np.tile(k, (8, 1))
    for c in np.argsort(high - low, axis=1, kind="stable").T:
        a, b = low[g, c][:, None], high[g, c][:, None]
        at = np.where((t[g, c][:, None] > 0) & (at >= a) & (at <= b), a + b - at, at)
    return np.argsort(at, axis=1)
def numbers_of(rng):
    return {"x": np.array(f(rng, N, 128, 4 * C)), "u": np.array(f(rng, N, 128, 512)), "v": np.array(f(rng, N, 128, 512))}
def weights(rng, w):
    c, p = packed(w, rng)
    return {"wc": c, "ws": p}
def still(rng):
    return weights(rng, np.zeros((N, 128, 2048), np.float32).astype(BF))
def apart(rng):
    w = np.array(f(rng, N, 128, 2048)).reshape(N, 8, 16, 4, 8, 16, 4)
    w[:, :, :8] = 0
    w[:, :, :, :, :, :8] = 0
    return weights(rng, w.reshape(N, 128, 2048))
def signs(rng):
    return np.stack([rng.permutation(8) % 2 * 2.0 - 1.0 for r in range(N)])
def small(rng):
    return np.where(rng.permutation(N) < N // 2, 2.0 ** -30, 1.0).astype(np.float32)
def planted(rng, s, t):
    d, k = numbers_of(rng), small(rng)
    neg = rng.permutation(N) % 2
    b = ((np.where(neg[:, None, None] == 1, 511 - s, s)[..., None] >> np.arange(9)) & 1) * k[:, None, None, None]
    x = d["x"].astype(np.float32).reshape(N, 8, 16, C, 4)
    x[:, :, :8] = 0
    x[:, :, 0] = b[..., :4]
    x[:, :, 1] = 16 * b[..., 4:8]
    x[:, :, 2, :, 0] = 16 * b[..., 8]
    x[:, :, 4, :, 0] = t * k[:, None, None]
    u = d["u"].astype(np.float32).reshape(N, 128, 128, 4)
    u[:, :, ::16] = 0
    u[:, :, 1::16] = 0
    m = (1 - 2 * neg) * k
    for h in range(0, 128, 16):
        u[:, h:h + 2, h] = m[:, None, None] * np.array([1.0, 2.0, 4.0, 8.0])
        u[:, h + 2, h, 0] = 16 * m
        u[:, h + 4, h + 1, 0] = k
    return {"x": x.reshape(N, 128, 4 * C).astype(BF), "u": u.reshape(N, 128, 512).astype(BF), "v": d["v"], **apart(rng)}
def setup_inputs(rng):
    return {**numbers_of(rng), **weights(rng, f(rng, N, 128, 2048))}
def setup_inputs_ties(rng):
    s, t = rng.integers(0, 3, (N, 8, C)), rng.integers(-1, 2, (N, 8, C))
    e = rng.permutation(N)
    s[e[0]] = 1
    t[e[1]] = 0
    return planted(rng, s, t)
def setup_inputs_chains(rng):
    c = np.arange(C)
    one = np.ones(C, np.int64)
    zig = np.where(c < C // 2, C - 1 - 2 * c, 2 * c - C)
    halves = np.sum((c[:, None] + 1) % 2 ** np.arange(1, 9) == 0, axis=1)
    s, t = np.zeros((N, 8, C), np.int64), np.zeros((N, 8, C), np.int64)
    for r in range(N):
        g, m, n = rng.permutation(8), rng.permutation(C), rng.permutation(C)
        s[r, g] = np.stack([c, C - 1 - c, zig, c, 7 * one, halves, m, n])
        t[r, g] = np.stack([one, one, one, rng.integers(-1, 2, C), one, one, (m == C - 1) * 2 - 1, -(n % 2)])
    return planted(rng, s, t)
def setup_inputs_near(rng):
    d = numbers_of(rng)
    x = d["x"].astype(np.float32).reshape(N, 8, 16, C, 4)
    i = np.array([[np.arange(C) // 2 if a > 0 else rng.permutation(C) // 2 for a in e] for e in signs(rng)])
    b = ((i[..., None] >> np.arange(8)) & 1) * np.exp2(np.arange(8) - 23.0)
    x[:, :, 0] = 0
    x[:, :, 0, :, 0] = signs(rng)[:, :, None]
    x[:, :, 8] = b[..., :4]
    x[:, :, 9] = b[..., 4:]
    x[:, :, 10] = 0
    x[:, :, 10, :, 0] = rng.integers(-1, 2, (N, 8, C)) * 2.0 ** -20
    x[:, :, 11:] = rng.integers(4, 8, (N, 8, 5, C, 4)) * rng.choice([-1.0, 1.0], (N, 8, 5, C, 4)) * 2.0 ** -20
    u = d["u"].astype(np.float32).reshape(N, 128, 128, 4)
    k = small(rng)
    u[:, :, ::16] = 0
    u[:, :, 1::16] = 0
    for h in range(0, 128, 16):
        u[:, h, h, 0] = k
        u[:, h + 8:h + 10, h] = k[:, None, None]
        u[:, h + 10, h + 1, 0] = k
    return {"x": x.reshape(N, 128, 4 * C).astype(BF), "u": u.reshape(N, 128, 512).astype(BF), "v": d["v"], **still(rng)}
def setup_inputs_huge(rng):
    d = numbers_of(rng)
    x = 2.0 ** 30 * (0.6 + 0.4 * rng.random((N, 8, 16, C, 4)))
    c = np.stack([rng.permutation(C) % 2 * 2.0 - 1.0 for r in range(N)])
    e = rng.permutation(N)
    c[e < N // 2] = 1
    x[..., :2] *= c[:, None, None, :, None]
    x[..., 2:] *= rng.choice([-1.0, 1.0], (N, 8, 1, C, 1))
    g = signs(rng)
    u = d["u"].astype(np.float32).reshape(N, 128, 128, 4)
    u[:, :, ::16] = 0
    u[:, :, 1::16] = 0
    u[:, :, ::16, :2] = 2.0 ** 30 * (1 - 0.25 * rng.random((N, 128, 8, 2))) * g[:, None, :, None]
    for h in range(0, 128, 16):
        u[:, h:h + 16, h + 1, 2:] = 2.0 ** 30
    r = int(np.argmin(e))
    x[r] = np.abs(x[r])
    x[r, :, :, C // 2:] = 2.0 ** 30
    u[r, :, ::16] = 2.0 ** 30 * g[r][None, :, None]
    return {"x": x.astype(np.float32).reshape(N, 128, 4 * C).astype(BF), "u": u.reshape(N, 128, 512).astype(BF), "v": d["v"], **still(rng)}
def setup_inputs_spread(rng):
    d = setup_inputs(rng)
    d["x"] = wide(rng, N, 128, 4 * C, cols=6)
    return d
def check_inputs(d):
    b = []
    for k in ("x", "u", "v"):
        a = np.abs(d[k].astype(np.float32))
        if not (np.isfinite(a).all() and ((a == 0) | (a >= 2.0 ** -30) & (a <= 2.0 ** 30)).all()): b.append("a value of " + k)
    return b
def reference(x, u, v, wc, ws):
    qu = [mx_ref.quantize(u[r]) for r in range(N)]
    lay = [pk(wc[r], ws[r]) for r in range(N)]
    now = [x[r] for r in range(N)]
    for t in range(R):
        o, border = [], []
        for r in range(N):
            p = mx_ref.matmul(qu[r], mx_ref.quantize(now[r]))
            o.append(turned(p[::16], p[1::16]))
            border.append(mx_ref.quantize(gcols(now[r], o[r][:, C - K:])))
        came = decode(join(*border)).astype(BF)
        for r in range(N):
            z = np.ascontiguousarray(np.concatenate([cut(came, (r - 1) % N, 4 * K), gcols(now[r], o[r][:, :C - K])], axis=1))
            q = mx_ref.quantize(z)
            now[r] = tile([z[:, b::4].astype(np.float32) + mx_ref.matmul(pick(lay[r], np.arange(128 * b, 128 * b + 128)), q) * np.float32(0.015625) for b in range(4)])
    y, ol = np.zeros((N, 128, C), np.float32), np.zeros((N, 8, C), np.float32)
    oc, osc = np.zeros((N, 128, 4 * C), np.uint8), np.zeros((N, 16, C), np.uint8)
    for r in range(N):
        q = mx_ref.quantize(now[r])
        y[r] = mx_ref.matmul(mx_ref.quantize(v[r]), q)
        ol[r] = o[r]
        oc[r], osc[r] = emit(q)
    return {"y": y, "ol": ol, "oc": oc, "osc": osc}

@@ -1,0 +1,507 @@
+from concourse.mybir import dt, AluOpType as A, ActivationFunctionType as F
+
+C, K, ROUNDS = 448, 128, 2
+HUGE = 2.0 ** 90
+CODE, PLANE = "float8_e4m3fn_x4", "uint8"
+
+
+def _sb(n, d):
+    return ("sbuf", [128, n], d)
+
+
+SCRATCH = {"ps": ("psum", [128, 4096], "float32")}
+for _n, _w in (("x0", 1792), ("xs", 1792), ("x64", 1792), ("z", 1792), ("z64", 1792), ("dec", 1792), ("ut", 512), ("vt", 512),
+               ("t1", 1792), ("tb", 896), ("kd8", 224), ("k8a", 224), ("i16", 464), ("tz", 464), ("msk", 464), ("kml", 448),
+               ("kmr", 448), ("klev", 464), ("k01", 464), ("kc", 464), ("k16", 480), ("kdb", 448), ("kl", 896), ("dgi", 528),
+               ("dga", 528), ("dg", 528), ("dv", 520), ("cn", 512), ("cp", 512), ("blk", 128), ("sg", 448),
+               ("nrr", 448), ("nrl", 448), ("v1r", 448), ("v1l", 448), ("vr", 448), ("c1r", 480), ("c1l", 480), ("b1r", 448),
+               ("b1l", 448), ("g1l", 448), ("nf", 896)):
+    SCRATCH[_n] = _sb(_w, "bfloat16")
+for _n, _w in (("w2r", 448), ("w2l", 448), ("g2r", 448), ("g2l", 448), ("h2r", 448), ("h2l", 448), ("hh", 480), ("tt", 928),
+               ("run", 896)):
+    SCRATCH[_n] = _sb(_w, "float16")
+for _n, _w in (("win", 968), ("sm", 448), ("sw", 448), ("smr", 456), ("sml", 456), ("thr", 896), ("ssb", 448), ("nd", 448),
+               ("c2r", 480), ("c2l", 480), ("ts", 928), ("ord", 448), ("iw", 464), ("ga", 448), ("gb", 448), ("gw", 448),
+               ("ysb", 448), ("col", 16), ("tab", 320), ("wk", 512), ("sma", 256)):
+    SCRATCH[_n] = _sb(_w, "float32")
+for _n, _w in (("pi", 8), ("ni", 384)):
+    SCRATCH[_n] = _sb(_w, "int32")
+for _n, _w in (("lu", 128), ("upk", 16), ("off", 272), ("came0", 8), ("came1", 8)):
+    SCRATCH[_n] = _sb(_w, "uint16")
+for _n, _w in (("x", 448), ("z", 448), ("u", 128), ("p", 256), ("v", 128), ("w", 512), ("c", 1024), ("1", 448), ("b", 224),
+               ("l0", 448), ("l1", 448)):
+    SCRATCH["q" + _n] = _sb(_w, CODE)
+    SCRATCH["s" + _n + "_"] = _sb(_w, PLANE)
+
+NSEM, NDMA = 112, 20
+SEMAPHORES = (["c%d" % i for i in range(NSEM)] + ["d%d" % i for i in range(NDMA)]
+              + [n + str(t) for n in ("arr", "out", "larr", "lout") for t in range(ROUNDS)])
+
+
+def emit(g, T, ops):
+    queue = {"v": g.vector, "a": g.scalar, "p": g.tensor, "g": g, "s": g.sync}
+    writer, readers, known, at_issue, waits, needed = {}, {}, {}, [], [], set()
+    for i, (e, fn, rd, wr, kind) in enumerate(ops):
+        deps = set()
+        for key in rd:
+            if key in writer:
+                deps.add(writer[key])
+            if key.startswith("ps"):
+                deps.update(j for j in readers.get(key, []) if ops[j][0] != e)
+        implied = 0
+        for key in wr:
+            if key in writer:
+                if kind == "acc":
+                    implied |= 1 << writer[key]
+                else:
+                    deps.add(writer[key])
+            deps.update(readers.get(key, []))
+        kn, mine = known.get(e, 0), []
+        for j in sorted(deps, reverse=True):
+            if not kn >> j & 1:
+                mine.append(j)
+                needed.add(j)
+                kn |= 1 << j | at_issue[j]
+        known[e] = kn
+        at_issue.append(kn | implied)
+        waits.append(mine)
+        for key in rd:
+            readers.setdefault(key, []).append(i)
+        for key in wr:
+            writer[key] = i
+            readers[key] = []
+    user, count, mark, ndma = {}, {}, {}, 0
+    for i, (e, fn, rd, wr, kind) in enumerate(ops):
+        for j in reversed(waits[i]):
+            queue[e].wait_ge(T.sem[mark[j][0]], mark[j][1])
+        if isinstance(kind, tuple):
+            if fn is not None:
+                fn()
+            mark[i] = kind
+            continue
+        if fn is None:
+            continue
+        ins = fn()
+        if i not in needed:
+            continue
+        if kind == "dma":
+            name = "d%d" % ndma
+            ndma += 1
+            ins.then_inc(T.sem[name], 16)
+            mark[i] = (name, 16)
+            continue
+        n = [n for n in range(NSEM) if n not in user or at_issue[i] >> user[n] & 1][0]
+        user[n] = i
+        count[n] = count.get(n, 0) + 1
+        ins.then_inc(T.sem["c%d" % n], 1)
+        mark[i] = ("c%d" % n, count[n])
+
+
+def rank_program(g, core, T, topo):
+    rank = T.rank_of(core)
+    if rank is None:
+        return
+    nxt = T.cores[(rank + 1) % len(T.cores)]
+    prv = T.cores[(rank - 1) % len(T.cores)]
+    rid, pid = topo.addr(nxt)[:2]
+    mask = topo.mask(core, nxt)
+    nout, nin = len(topo.engines(core, nxt)), len(topo.engines(prv, core))
+    ops = []
+    V, S, P = g.vector, g.scalar, g.tensor
+
+    def op(e, fn, rd, wr, kind=None):
+        ops.append((e, fn, rd.split(), wr.split(), kind))
+
+    def tt(out, a, b, o, rd, wr):
+        op("v", lambda: V.tensor_tensor(out, a, b, o), rd, wr)
+
+    def ts(out, a, s1, o1, rd, wr, s2=None, o2=None):
+        if o2 is None:
+            op("v", lambda: V.tensor_scalar(out, a, s1, None, o1), rd, wr)
+        else:
+            op("v", lambda: V.tensor_scalar(out, a, s1, s2, o1, o2), rd, wr)
+
+    def cp(out, a, rd, wr):
+        op("v", lambda: V.tensor_copy(out, a), rd, wr)
+
+    def scan(out, d0, d1, init, o0, o1, rd, wr):
+        op("v", lambda: V.tensor_tensor_scan(out, d0, d1, init, o0, o1), rd, wr)
+
+    def ms(out, val, wr):
+        op("v", lambda: V.memset(out, val), "", wr)
+
+    def act(out, a, f, rd, wr, scale=None, bias=None):
+        kw = {}
+        if scale is not None:
+            kw["scale"] = scale
+        if bias is not None:
+            kw["bias"] = bias
+        op("a", lambda: S.activation(out, a, f, **kw), rd, wr)
+
+    def quant(name, a, b, src, rd, wr):
+        op("v", lambda: V.quantize_mx(T["q" + name][:, a:b], T["s" + name + "_"][:, a:b], src), rd, wr)
+
+    def bank(k, n=C):
+        return T.ps[:, 512 * k:512 * k + n]
+
+    def mm(k, ln, la, rn, a, b, rd, start=True, stop=True):
+        op("p", lambda: P.matmul_mx(bank(k, b - a), T["q" + ln][:, la:la + 128], T["s" + ln + "_"][:, la:la + 128],
+                                    T["q" + rn][:, a:b], T["s" + rn + "_"][:, a:b], start, stop),
+           rd, "ps%d" % k, None if start else "acc")
+
+    def iota(out, pat, base, cm, wr):
+        op("g", lambda: g.iota(out, pat, base, cm, allow_small_or_imprecise_dtypes=True), "", wr)
+
+    def pick(out, src, pat, cmp, fill, base, cm, rd, wr):
+        op("g", lambda: g.affine_select(out, src, pat, cmp, fill, base, cm), rd, wr)
+
+    def dma(e, out, src, rd, wr):
+        q = g.sync if e == "s" else g.scalar
+        op(e, lambda: q.dma_start(out, src), rd, wr, "dma")
+
+    def send(dst, src, there, here, total, rd, wr):
+        op("g", lambda: g.remote_dma(dst, src, T.sem[there], T.sem[here], pid, rid, mask), rd, wr, (here, total))
+
+    def rev(t, a, n=C):
+        return t[:, a + n - 1:(a - 1 if a else None):-1]
+
+    def rbank(k):
+        return rev(T.ps, 512 * k)
+
+    col = lambda j: T.col[:, j:j + 1]
+    R_, NR, R15, H1, H2, NB, R16, PAR, RH, M15, NM15 = range(11)
+    MRB, MLW, MLB, BMB = 16, 464, 480, 937
+    CL, CR, TL, TR, PK = 0, 28, 56, 84, 112
+    O_L2, O_LR, O_W, O_AT, O_O = 0, 56, 112, 168, 200
+    VR, VL, CN, CP = 512, 640, 768, 896
+    HALF = C // 2
+    tab = lambda a, n=56: T.tab[:, a:a + n]
+    wk = lambda j, a=0, n=56: T.wk[:, 64 * j + a:64 * j + n]
+    plane = lambda t, b, a=0, n=C: t[:, C * b + a:C * b + n]
+
+    dma("a", T.ut[:], T.u[:], "", "ut")
+    dma("s", T.x0[:, 0:896], T.x[:, 0:896], "", "x0a")
+    dma("s", T.x0[:, 896:], T.x[:, 896:], "", "x0b")
+
+    op("g", lambda: g.iota(T.pi[:, 0:1], [[0, 1]], 0, 1), "", "pi0")
+    iota(T.tab[:, 296:312], [[1, 2], [16, 8]], 0, 0, "upl")
+    iota(T.i16[:], [[0, 29], [1, 16]], 0, 0, "i16")
+    iota(tab(0), [[0, 28], [16, 2]], 1, 0, "c0")
+    iota(tab(56, 28), [[-1, 14], [0, 2]], 15, 0, "ta")
+    iota(tab(84, 28), [[1, 14], [0, 2]], 2, 0, "tb_")
+    iota(T.dgi[:], [[1, 528]], 0, -4, "dgi")
+    iota(tab(168), [[2, 2], [16, 28]], 15, 0, "ck")
+    iota(tab(224, 28), [[16, 28]], 16, 0, "ck1")
+    iota(T.blk[:], [[0, 128]], 1, 0, "blk")
+    pick(T.blk[:], T.blk[:], [[-16, 8], [0, 16]], A.is_ge, 0.0, 0, 1, "blk", "blk")
+    pick(T.blk[:], T.blk[:], [[16, 8], [0, 16]], A.is_ge, 0.0, 15, -1, "blk", "blk")
+    iota(T.t1[:, 3::4], [[0, C]], 0, 0, "t13")
+
+    ms(T.tz[:], 0.0, "tz")
+    ms(T.k16[:], 1.0, "k16")
+    ts(T.pi[:, 1:2], T.pi[:, 0:1], 15, A.bitwise_and, "pi0", "pi1")
+    fill = [lambda: cp(col(R_), T.pi[:, 1:2], "pi1", "r"), lambda: ms(T.k16[:, 0::16], 0.0, "k16"),
+            lambda: cp(T.upk[:], T.tab[:, 296:312], "upl", "upk"), lambda: ms(T.win[:, 0:15], HUGE, "wino"),
+            lambda: ms(T.win[:, 464:480], HUGE, "winp"), lambda: ms(T.win[:, 929:968], HUGE, "winq"),
+            lambda: ms(T.smr[:, 448:456], -HUGE, "smrp"), lambda: ms(T.sml[:, 0:8], -HUGE, "smlp")]
+    for j in range(1, 9):
+        ms(T.tz[:, 0::2 ** j], float(j), "tz")
+        fill[j - 1]()
+    ms(T.tz[:, 0:1], 15.0, "tz")
+    ms(T.kl[:, 0:C], -16.0, "kll")
+    ms(T.kl[:, C:], 16.0, "klr")
+    ts(T.msk[:], T.i16[:], col(R_), A.is_equal, "i16 r", "msk")
+    act(col(H1), col(R_), F.Identity, "r", "h1", -HUGE, HUGE)
+    act(col(H2), col(R_), F.Identity, "r", "h2", HUGE, HUGE)
+    act(T.kml[:], T.i16[:, 0:C], F.Relu, "i16 h1", "kml", HUGE, col(H1))
+    act(T.kmr[:], T.i16[:, 0:C], F.Relu, "i16 h2", "kmr", -HUGE, col(H2))
+    act(wk(0), tab(0), F.Identity, "c0 r", "w0", 1.0, col(R_))
+    act(tab(112), tab(56), F.Identity, "ta tb_", "tc", -2.0, 31.0)
+    quant("u", 0, 128, T.ut[:], "ut", "qu")
+    op("v", lambda: V.tensor_copy(T.qp[:, 0:256].bitcast(dt.uint32), T.qu[:, 0:128].bitcast(dt.uint32).indirect(T.upk[:, 0:16])),
+       "qu upk", "qp")
+    act(T["sp_"][:, 0:256], T["su_"][:, 0:128].indirect(T.upk[:, 0:16]), F.Copy, "qu upk", "sp")
+    act(T.klev[:], T.tz[:], F.Relu, "tz h1", "klev", HUGE, col(H1))
+    tt(wk(1), wk(0), tab(56), A.is_gt, "w0 ta tb_", "w1")
+    quant("x", 0, HALF, T.x0[:, 0:896], "x0a", "qxa")
+    tt(wk(2), wk(1), tab(112), A.mult, "w1 tc", "w2")
+    tt(wk(3), wk(1), tab(56), A.mult, "w1", "w3")
+    quant("x", HALF, C, T.x0[:, 896:], "x0b", "qxb")
+    dma("s", T.qw[:].bitcast(dt.uint8), T.wc[:], "x0a x0b", "qw")
+    dma("s", T["sw_"][:], T.ws[:], "", "sw_")
+    dma("s", T.vt[:], T.v[:], "", "vt")
+    tt(wk(4), wk(2), tab(56), A.add, "w2", "w4")
+    tt(wk(5), wk(0), wk(3), A.subtract, "w0 w3", "w5")
+    act(T.dga[:], T.dgi[:], F.Abs, "dgi", "dga", 1.0, -3.0)
+    act(T.win[:, 15:16], T.msk[:, 16:17], F.Identity, "msk", "winr", -2 * HUGE, HUGE)
+    act(T.win[:, 928:929], T.msk[:, 16:17], F.Identity, "msk", "wins", -2 * HUGE, HUGE)
+    act(wk(7, 0, 28), wk(4, 0, 28), F.Identity, "w4", "w7a", 15.0, float(MLB - BMB - 30))
+    act(wk(7, 28), wk(4, 28), F.Identity, "w4", "w7b", -15.0, float(466 - BMB))
+    act(wk(1, 0, 28), wk(5, 0, 28), F.Identity, "w5", "w1a w1", 1.0, float(BMB - 2))
+    act(wk(1, 28), wk(5, 28), F.Identity, "w5 w1", "w1b", -1.0, float(BMB + 29))
+    ts(T.lu[:, TL:TL + 28], wk(4, 0, 28), 16.0, A.mult, "w4", "ltl", -17.0, A.add)
+    ts(T.lu[:, TR:TR + 28], wk(4, 28), -16.0, A.mult, "w4", "ltr", 479.0, A.add)
+    tt(wk(6), wk(5), wk(4), A.is_equal, "w5 w4", "w6")
+
+    def setup_0():
+        act(T.dg[:], T.dga[:], F.Relu, "dga", "dg", -1.0, 1.0)
+        pick(T.dv[:], T.dg[:, 0:520], [[1, 520]], A.not_equal, -1.0, 1, -4, "dg", "dv")
+        iota(T.dv[:, 63::64], [[0, 8]], 0, 0, "dv")
+        pick(T.dv[:, 64::64], T.dv[:, 64::64], [[-16, 8]], A.not_equal, 2.0, -15, 1, "dv", "dv")
+        for n, v in (("c1r", 2), ("c2r", 0)):
+            iota(T[n][:, 0:17], [[0, 17]], v, 0, n + "p")
+            iota(T[n][:, 465:480], [[0, 15]], v, 0, n + "q")
+        for n, v in (("c1l", -1), ("c2l", 0), ("hh", 0)):
+            iota(T[n][:, 0:16], [[0, 16]], v, 0, n + "p")
+            iota(T[n][:, 464:480], [[0, 16]], v, 0, n + "q")
+        iota(T.iw[:], [[1, 464]], 0, 0, "iw")
+        iota(tab(260, 2), [[256, 2]], 15, 0, "kp")
+        iota(T.sma[:, 156:160], [[0, 4]], 0, 0, "ownp")
+        act(col(NR), col(R_), F.Copy, "r", "nr_", -1.0)
+        act(col(R15), col(R_), F.Identity, "r", "r15", -1.0, 15.0)
+
+    def setup_1():
+        tt(wk(6), wk(6), wk(7), A.mult, "w6 w7a w7b", "w6")
+        for b in range(3):
+            quant("c", 128 * b, 128 * b + 128, T.dg[:, 3 - b:515 - b], "dg", "e%d" % b)
+        tt(wk(6), wk(6), wk(1), A.add, "w6 w1a w1b", "w6")
+        cp(T.lu[:, 0:56], wk(6), "w6", "lu")
+        for view, c_, key in ((T.kl[:, 14:418:31], NR, "kll"), (T.kl[:, 30:C:32], NR, "kll"),
+                              (T.kl[:, 449::33], R15, "klr"), (T.kl[:, 478::32], R15, "klr")):
+            act(view, T.i16[:, 0:14], F.Identity, "i16 nr_ r15", key, 0.0, col(c_))
+        act(tab(168, 84), tab(168, 84), F.Identity, "ck ck1 r", "ck ck1", 1.0, col(R_))
+        act(T.k01[:], T.klev[:], F.Relu, "klev", "k01", -2.0 / HUGE, 1.0)
+        act(T.kc[:], T.k01[:], F.Identity, "k01", "kc", 2.0, -1.0)
+
+    def weights(t, key, w):
+        act(t[:], T.dg[:, 0:512], F.Copy, "dg", key + "z", 0.0)
+        for j, (at, v) in enumerate(((0, 1.0), (1, w), (6, 1.0), (7, w))):
+            act(t[:, at::8], T.blk[:, j // 2::2], F.Copy, "blk %sz" % key, key + str(j), v)
+
+    def setup_a():
+        quant("c", VR, VR + 128, T.dv[:, 1:513], "dv", "cvr")
+        quant("c", VL, VL + 128, T.dv[:, 3:515], "dv", "cvl")
+        weights(T.cn, "cn", 32.0)
+        weights(T.cp, "cp", 1.0)
+
+    def setup_b():
+        act(col(RH), col(R_), F.Identity, "r", "rh", -1.0, 0.5)
+        act(T.k8a[:], T.i16[:, 0:C:2], F.Abs, "i16 rh", "k8a", 1.0, col(RH))
+        act(T.k8a[:], T.k8a[:], F.Relu, "k8a", "k8a", -1.0, 1.5)
+        act(T.kd8[:], T.k8a[:], F.Identity, "k8a", "kd8", -16384.0, 1024.0)
+        quant("c", CN, CN + 128, T.cn[:], "cn0 cn1 cn2 cn3", "cn")
+
+    def setup_c():
+        act(col(M15), col(R15), F.Sign, "r15", "m15")
+        act(col(NM15), col(R15), F.Sign, "r15", "nm15", -1.0)
+        act(col(NB), col(R15), F.Copy, "r15", "nb", -1024.0)
+        act(col(R16), col(R_), F.Copy, "r", "r16", 16.0)
+
+    def setup_d():
+        ts(T.pi[:, 2:3], T.pi[:, 0:1], 4, A.arith_shift_right, "pi0", "pi2")
+        quant("c", CP, CP + 128, T.cp[:], "cp0 cp1 cp2 cp3", "cp")
+        tt(T.pi[:, 3:4], T.pi[:, 2:3], T.pi[:, 0:1], A.add, "pi2 pi0", "pi3")
+
+    def setup_e():
+        act(T.kdb[:], T.msk[:, 16:464], F.Identity, "msk", "kdb", -32768.0, 1024.0)
+        ts(T.pi[:, 4:5], T.pi[:, 3:4], 1, A.bitwise_and, "pi3", "pi4")
+        quant("c", 384, 512, T.dg[:, 0:512], "dg", "e3")
+        ts(col(PAR), T.pi[:, 4:5], 464.0, A.mult, "pi4 r16", "par", col(R16), A.add)
+
+    def setup_f():
+        ts(T.lu[:, PK:PK + 2], tab(260, 2), col(PAR), A.add, "kp par", "pk", 927.0, A.min)
+        quant("v", 0, 128, T.vt[:], "vt", "qv")
+
+    def planes():
+        for b in range(4):
+            act(plane(T.x64, b), T.x0[:, b::4], F.Copy, "x0a x0b", "fa%d fb%d" % (b, b), 64.0)
+
+    sma = lambda a, n=56: T.sma[:, a:a + n]
+    ni = lambda a, n=56: T.ni[:, a:a + n]
+    DD, WW, OWN, AT = 0, 64, 128, 192
+    IX, B16, NI, CNT, TT, PI, SEL = 0, 56, 112, 140, 196, 252, 308
+    off = lambda a, n=28: T.off[:, a:a + n]
+    WIN = "mr ml bm wino winp winq winr wins"
+    RL, FL, RR = 0, 1, 2
+
+    def counted(const, key, between):
+        quant("b", 0, HALF, T.tb[:], "tb0 tb1", "qb")
+        mm(1, "c", const, "b", 0, HALF, key + " qb")
+        between()
+        scan(T.nd[:, 0:HALF], T.kd8[:], bank(1, HALF), 0.0, A.add, A.max, "kd8 ps1", "nd")
+
+    for rnd in range(ROUNDS):
+        first, last = rnd == 0, rnd == ROUNDS - 1
+        l_, n_ = "l%d" % rnd, str(rnd)
+        once = lambda fn: fn() if first else None
+        send(T["q" + l_][:].bitcast(dt.uint8), T.qx[:].bitcast(dt.uint8), "arr" + n_, "out" + n_, 2 * nout, "qxa qxb", "")
+        send(T["s" + l_ + "_"][:], T["sx_"][:], "arr" + n_, "out" + n_, 2 * nout, "qxa qxb", "sent" + n_)
+        op("x", None, "", l_, ("arr" + n_, 2 * nin))
+        mm(0, "p", 0, "x", 0, C, "qp sp qxa qxb")
+        mm(2, "p", 128, "x", 0, C, "qp sp qxa qxb")
+        mm(1, "p", 0, "x", 0, C, "qp sp qxa qxb")
+        once(setup_0)
+        if first:
+            tt(T.sm[:], bank(0), T.msk[:, 16:464], A.mult, "ps0 msk", "sm smb")
+        else:
+            tt(T.sm[:, K:], bank(3, C - K), T.msk[:, 16 + K:464], A.mult, "ps3 msk", "smb")
+            tt(T.sm[:, 0:K], bank(0, K), T.msk[:, 16:16 + K], A.mult, "ps0 msk", "sm")
+        scan(rev(T.win, MLB), rbank(0), rev(T.kml, 0), -HUGE, A.max, A.subtract, "ps0 kml", "ml")
+        scan(T.sw[:], T.k16[:, 0:C], T.sm[:], 0.0, A.mult, A.add, "k16 sm smb", "sw")
+        act(T.sg[:], bank(2), F.Sign, "ps2", "sg")
+        scan(T.win[:, MRB:MRB + C], bank(0), T.kmr[:], -HUGE, A.max, A.subtract, "ps0 kmr", "mr")
+        act(T.t1[:, FL::4], T.sg[:], F.Relu, "sg", "t1f")
+        act(T.thr[:, 0:C], T.sw[:].indirect(T.lu[:, TL:TL + 28]), F.Copy, "sw ltl", "thl")
+        act(T.thr[:, C:2 * C], T.sw[:].indirect(T.lu[:, TR:TR + 28]), F.Copy, "sw ltr", "thr")
+        scan(rev(T.smr, 0), rbank(0), rev(T.klev, 0), -HUGE, A.max, A.subtract, "ps0 klev", "smr")
+        tt(sma(224, 28), T.win[:, MLB:MLB + C:16], T.win[:, 31:464:16], A.max, "ml mr", "bm0")
+        scan(T.sml[:, 8:456], bank(0), T.klev[:, 1:449], -HUGE, A.max, A.subtract, "ps0 klev", "sml")
+        tt(T.win[:, BMB:BMB + 28], sma(224, 28), T.sw[:, 15::16], A.max, "bm0 sw winq", "bm")
+        tt(T.t1[:, RR::4], bank(0), T.smr[:, 1:449], A.is_ge, "ps0 smr smrp", "t1r")
+        once(setup_1)
+        act(T.ssb[:], bank(1), F.Copy, "ps1", "ssb")
+        tt(T.t1[:, RL::4], bank(0), T.sml[:, 7:455], A.is_gt, "ps0 sml smlp", "t1l")
+        tt(T.nf[:, 0:C], T.win[:, 0:968].indirect(T.lu[:, CL:CL + 28]), T.thr[:, 0:C], A.is_lt, WIN + " lu thl", "nfl")
+        quant("1", 0, C, T.t1[:], "t1l t1f t1r t13", "q1")
+        tt(T.nf[:, C:2 * C], T.win[:, 0:968].indirect(T.lu[:, CR:CR + 28]), T.thr[:, C:2 * C], A.is_le, WIN + " lu thr", "nfr")
+        once(setup_a)
+        scan(T.run[:], T.kl[:], T.nf[:], 0.0, A.add, A.mult, "kll klr nfl nfr", "run")
+        mm(3, "c", 128 * FL, "1", 0, C, "e1 q1", True, False)
+        mm(3, "c", 128 * RL, "1", 0, C, "e0 q1", False, True)
+        mm(4, "c", 128 * FL, "1", 0, C, "e1 q1", True, False)
+        mm(4, "c", 128 * RR, "1", 0, C, "e2 q1", False, True)
+        mm(5, "c", VR, "1", 0, C, "cvr q1")
+        mm(6, "c", VL, "1", 0, C, "cvl q1")
+        mm(7, "c", 128 * RR, "1", 0, C, "e2 q1")
+        act(T.v1r[:], bank(3), F.Sign, "ps3", "v1r", -1.0, 1.5)
+        tt(ni(IX + 14, 28), T.run[:, 30::32], tab(182, 28), A.add, "run ck", "ixb")
+        tt(ni(IX, 14), T.run[:, 417:13:-31], tab(168, 14), A.add, "run ck", "ixa")
+        tt(ni(IX + 42, 14), T.run[:, 878:448:-33], tab(210, 14), A.add, "run ck", "ixc")
+        once(setup_b)
+        cp(off(O_L2, 56), ni(IX), "ixa ixb ixc", "ol2")
+        act(T.ga[:], T.win[:, 0:464].indirect(off(O_L2)), F.Copy, WIN + " ol2", "ga")
+        act(T.v1l[:], bank(4), F.Sign, "ps4", "v1l", -1.0, 1.5)
+        tt(T.tb[:, 1::2], T.win[:, MLW:936].indirect(off(O_L2 + 28)), T.ssb[:], A.is_le, WIN + " ol2 ssb", "tb1")
+        ts(ni(B16), ni(IX), 0xFFF0, A.bitwise_and, "ixa ixb ixc", "b16")
+        tt(T.tb[:, 0::2], T.ga[:], bank(0), A.is_ge, "ga ps0", "tb0")
+        once(setup_c)
+        act(T.vr[:], bank(5), F.Copy, "ps5", "vr")
+        act(T.nrr[:], T.t1[:, RR::4], F.Identity, "t1r", "nrr", -1.0, 1.0)
+        act(T.nrl[:], T.t1[:, RL::4], F.Identity, "t1l m15 nm15", "nrl", col(NM15), col(M15))
+        counted(CN, "cn", lambda: scan(rev(T.c1r, 17), rev(T.kc, 1), rev(T.v1r, 0), -1.0, A.min, A.mult, "kc v1r", "c1r"))
+        cp(ni(NI, 28), T.nd[:, 7:HALF:8], "nd", "ni")
+        scan(T.c1l[:, 16:464], T.kc[:, 0:C], T.v1l[:], -1.0, A.min, A.mult, "kc v1l", "c1l")
+        ts(ni(CNT, 28), ni(NI, 28), 31, A.bitwise_and, "ni", "nl")
+        ts(ni(CNT + 28, 28), ni(NI, 28), 5, A.arith_shift_right, "ni", "nr", 31, A.bitwise_and)
+        once(setup_d)
+        tt(ni(TT), ni(CNT), ni(B16), A.add, "nl nr b16", "tt_")
+        cp(off(O_LR, 56), ni(TT), "tt_", "olr")
+        act(T.g1l[:], T.c1l[:].indirect(off(O_LR)), F.Identity, "c1l c1lp c1lq olr", "g1l", -0.5, 1.5)
+        tt(T.b1r[:], T.c1r[:].indirect(off(O_LR + 28)), T.vr[:], A.is_equal, "c1r c1rp c1rq olr vr", "b1r")
+        tt(T.b1l[:], T.g1l[:], bank(6), A.is_le, "g1l ps6", "b1l")
+        scan(T.tb[:, 2 * C - 2::-2], rev(T.nrr, 0), rev(T.b1r, 0), 0.0, A.mult, A.add, "nrr b1r", "tb0")
+        scan(T.tb[:, 1::2], T.nrl[:], T.b1l[:], 0.0, A.mult, A.add, "nrl b1l", "tb1")
+        once(planes)
+
+        def lengths():
+            tt(sma(DD, 28), tab(224, 28), ni(TT, 28), A.subtract, "tt_ ck1", "dl")
+            tt(sma(DD + 28, 28), ni(TT + 28, 28), tab(196, 28), A.subtract, "tt_ ck", "dr")
+            once(setup_e)
+        counted(CP, "cp", lengths)
+        DB = (3, 4, 0, 1)
+        for b in range(4):
+            mm(DB[b], "c", 128 * b, l_, 0, C, "e%d %s" % (b, l_))
+        ts(ni(PI, 28), T.nd[:, 7:HALF:8], 1.0, A.add, "nd", "pa")
+        cp(ni(PI + 28, 28), T.nd[:, 7:HALF:8], "nd", "pb")
+        once(setup_f)
+        ts(ni(SEL), ni(PI), 1, A.bitwise_and, "pa pb", "sel")
+        tt(sma(WW), ni(SEL), sma(DD), A.mult, "sel dl dr", "ww")
+        cp(off(O_W, 56), sma(WW), "ww", "ow")
+        act(T.gw[:], T.iw[:].indirect(off(O_W)), F.Copy, "iw ow", "gw")
+        tt(T.w2r[:], T.iw[:].indirect(off(O_W + 28)), T.t1[:, RL::4], A.mult, "iw ow t1l", "w2r")
+        tt(sma(OWN, 28), sma(WW, 28), sma(WW + 28, 28), A.add, "ww", "own")
+        scan(rev(T.c2r, 17), rev(T.k01, 1), rev(T.w2r, 0), 0.0, A.mult, A.add, "k01 w2r", "c2r")
+        tt(T.w2l[:], T.gw[:], bank(7), A.mult, "gw ps7", "w2l")
+        act(T.ga[:], T.c2r[:].indirect(off(O_LR + 28)), F.Copy, "c2r c2rp c2rq olr", "ga")
+        scan(T.c2l[:, 16:464], T.k01[:, 0:C], T.w2l[:], 0.0, A.mult, A.add, "k01 w2l", "c2l")
+        act(T.gb[:], T.c2l[:].indirect(off(O_LR)), F.Copy, "c2l c2lp c2lq olr m15", "gb", col(M15))
+        tt(T.g2r[:], T.ga[:], bank(5), A.mult, "ga ps5", "g2r")
+        scan(rev(T.h2r, 0), rev(T.nrr, 0), rev(T.g2r, 0), 0.0, A.mult, A.add, "nrr g2r", "h2r")
+        tt(T.g2l[:], T.gb[:], bank(6), A.mult, "gb ps6", "g2l")
+        for b in range(4):
+            act(plane(T.dec, b), bank(DB[b]), F.Copy, "ps%d" % DB[b], "dec%d" % b)
+        scan(T.h2l[:], T.nrl[:], T.g2l[:], 0.0, A.mult, A.add, "nrl g2l", "h2l")
+        tt(T.hh[:, 16:464], T.h2r[:], T.h2l[:], A.add, "h2r h2l", "hh")
+        op("v", lambda: V.transpose(T.tt[:, 0:448], T.hh[:, 16:464]), "hh", "tta")
+        op("v", lambda: V.transpose(T.tt[:, 448:928], T.hh[:, 0:480]), "hh hhp hhq", "ttb")
+        scan(T.ts[:, 0:448], T.k16[:, 0:448], T.tt[:, 0:448], 0.0, A.mult, A.add, "k16 tta", "tsa")
+        scan(T.ts[:, 448:928], T.k16[:], T.tt[:, 448:928], 0.0, A.mult, A.add, "k16 ttb", "tsb")
+        tt(sma(AT, 32), T.ts[:].indirect(T.lu[:, PK:PK + 2]), sma(OWN, 32), A.add, "tsa tsb pk own ownp", "at")
+        ts(off(O_AT), sma(AT, 28), -1.0, A.add, "at", "oat")
+        cp(T.ord[:].indirect(off(O_AT)), T.iw[:, 0:C], "oat iw", "ord")
+        scan(T.nd[:], T.kdb[:], T.ord[:], 0.0, A.add, A.max, "kdb ord", "nd")
+        oo = O_O + 32 * rnd
+        ts(off(oo), T.nd[:, 15::16], col(NB), A.add, "nd nb", "oo")
+        send(T["came" + n_][:], off(oo + 20, 8), "larr" + n_, "lout" + n_, nout, "oo", "lsent" + n_)
+        op("x", None, "", "came" + n_, ("larr" + n_, nin))
+        if last:
+            dma("s", T.ol[:], T.ord[0:128:16, :], "ord", "y_ol")
+
+        def scale(e, out, src, by, rd, wr):
+            if e == "v":
+                ts(out, src, by, A.mult, rd, wr)
+            else:
+                act(out, src, F.Copy, rd, wr, by)
+        own, came = (lambda t, b: t[:, 4 * K + b::4]), (lambda t, b: t[:, b:4 * K:4])
+        for b, e in ((2, "a"), (0, "v"), (3, "a"), (1, "v")):
+            scale(e, own(T.z, b), plane(T.x64, b).indirect(off(oo, 20)), 1.0 / 64, "oo fa%d fb%d" % (b, b), "zb%d" % b)
+        quant("z", K, C, T.z[:, 4 * K:], "zb0 zb1 zb2 zb3", "qzb")
+        for b in range(4):
+            mm(b, "w", 128 * b, "z", K, C, "qw sw_ qzb")
+
+        def step(name, b, e):
+            if name == "sb":
+                scale(e, plane(T.z64, b, K), own(T.z, b), 64.0, "zb%d" % b, "sb%d" % b)
+            elif name == "za":
+                scale(e, came(T.z, b), plane(T.dec, b).indirect(T["came" + n_][:]), 1.0, "dec%d came%s" % (b, n_), "za%d" % b)
+            elif name == "sa":
+                scale(e, plane(T.z64, b, 0, K), came(T.z, b), 64.0, "za%d" % b, "sa%d" % b)
+            elif name == "fb":
+                tt(plane(T.x64, b, K), bank(b, C - K), plane(T.z64, b, K), A.add, "ps%d sb%d" % (b, b), "fb%d" % b)
+            elif name == "fa":
+                tt(plane(T.x64, b, 0, K), bank(4 + b, K), plane(T.z64, b, 0, K), A.add, "ps%d sa%d" % (4 + b, b), "fa%d" % b)
+            elif name == "xb":
+                scale(e, own(T.xs, b), plane(T.x64, b, K), 1.0 / 64, "fb%d" % b, "xb%d" % b)
+            elif name == "xa":
+                scale(e, came(T.xs, b), plane(T.x64, b, 0, K), 1.0 / 64, "fa%d" % b, "xa%d" % b)
+            elif name == "qz":
+                quant("z", 0, K, T.z[:, 0:4 * K], "za0 za1 za2 za3", "qza")
+                for j in range(4):
+                    mm(4 + j, "w", 128 * j, "z", 0, K, "qw sw_ qza")
+            elif name == "qb":
+                quant("x", K, C, T.xs[:, 4 * K:], "xb0 xb1 xb2 xb3 sent" + n_, "qxb")
+                if last:
+                    mm(0, "v", 0, "x", K, C, "qv qxb")
+                    dma("s", T.oc[:, 4 * K:], T.qx[:, K:C].bitcast(dt.uint8), "qxb", "y_ocb")
+                else:
+                    mm(3, "p", 0, "x", K, C, "qp sp qxb")
+            elif name == "yb":
+                act(T.ysb[:, K:C], bank(0, C - K), F.Copy, "ps0", "yb")
+                dma("a", T.y[:, K:C], T.ysb[:, K:C], "yb", "y_b")
+            else:
+                quant("x", 0, K, T.xs[:, 0:4 * K], "xa0 xa1 xa2 xa3", "qxa")
+        order = "sb0a sb1a za0v za1v za2a za3a sb2a sb3a fb0v qz0v fb1v xb0a "
+        if last:
+            order += "xb1a fb2v fb3v xb2v xb3v sa0a sa1a sa2a sa3a qb0v fa0v fa1v fa2v fa3v yb0a xa0v xa1v xa2v xa3v qa0v"
+        else:
+            order += "sa0a sa1a xb1a fb2v sa2a sa3a fb3v xb2a xb3v fa0v fa1v fa2v fa3v qb0v xa0a xa1a xa2v xa3v qa0v"
+        for w in order.split():
+            step(w[:2], int(w[2]), w[3])
+    mm(1, "v", 0, "x", 0, K, "qv qxa")
+    dma("s", T.oc[:, 0:4 * K], T.qx[:, 0:K].bitcast(dt.uint8), "qxa", "y_oc")
+    cp(T.ysb[:, 0:K], bank(1, K), "ps1", "ya")
+    for k in range(4):
+        dma("s" if k % 2 else "a", T.osc[4 * k:4 * k + 4, :], T["sx_"][32 * k:32 * k + 4, :], "qxa qxb", "y_s%d" % k)
+    dma("s", T.y[:, 0:K], T.ysb[:, 0:K], "ya", "y_a")
+    op("g", None, "sent0 sent1 lsent0 lsent1 y_ol y_ocb y_oc y_s0 y_s1 y_s2 y_s3 y_a y_b", "")
+    emit(g, T, ops)

@@ -12,19 +12,19 @@ def _sb(n, d):
 SCRATCH = {"ps": ("psum", [128, 4096], "float32")}
 for _n, _w in (("x0", 1792), ("xs", 1792), ("x64", 1792), ("z", 1792), ("z64", 1792), ("dec", 1792), ("ut", 512), ("vt", 512),
                ("t1", 1792), ("tb", 896), ("kd8", 224), ("k8a", 224), ("i16", 464), ("tz", 464), ("msk", 464), ("kml", 448),
-               ("kmr", 448), ("klev", 464), ("k01", 464), ("kc", 464), ("k16", 480), ("kdb", 448), ("kl", 896), ("dgi", 528),
-               ("dga", 528), ("dg", 528), ("dv", 520), ("cn", 512), ("cp", 512), ("blk", 128), ("sg", 448),
+               ("kmr", 448), ("klev", 464), ("k01", 464), ("kc", 464), ("k16", 448), ("kdb", 448), ("kl", 896), ("dgi", 528),
+               ("dga", 528), ("dg", 528), ("dv", 520), ("cn", 520), ("ks", 480), ("b32", 480), ("blk", 128), ("sg", 448),
                ("nrr", 448), ("nrl", 448), ("v1r", 448), ("v1l", 448), ("vr", 448), ("c1r", 480), ("c1l", 480), ("b1r", 448),
                ("b1l", 448), ("g1l", 448), ("nf", 896)):
     SCRATCH[_n] = _sb(_w, "bfloat16")
 for _n, _w in (("w2r", 448), ("w2l", 448), ("g2r", 448), ("g2l", 448), ("h2r", 448), ("h2l", 448), ("hh", 480), ("tt", 928),
-               ("run", 896)):
+               ("run", 896), ("ts", 928)):
     SCRATCH[_n] = _sb(_w, "float16")
 for _n, _w in (("win", 968), ("sm", 448), ("sw", 448), ("smr", 456), ("sml", 456), ("thr", 896), ("ssb", 448), ("nd", 448),
-               ("c2r", 480), ("c2l", 480), ("ts", 928), ("ord", 448), ("iw", 464), ("ga", 448), ("gb", 448), ("gw", 448),
-               ("ysb", 448), ("col", 16), ("tab", 320), ("wk", 512), ("sma", 256)):
+               ("c2r", 480), ("c2l", 480), ("ord", 448), ("iw", 464), ("ga", 448), ("gb", 448), ("gw", 448),
+               ("ysb", 448), ("col", 16), ("tab", 336), ("wk", 512), ("sma", 320)):
     SCRATCH[_n] = _sb(_w, "float32")
-for _n, _w in (("pi", 8), ("ni", 384)):
+for _n, _w in (("pi", 8), ("ni", 256)):
     SCRATCH[_n] = _sb(_w, "int32")
 for _n, _w in (("lu", 128), ("upk", 16), ("off", 272), ("came0", 8), ("came1", 8)):
     SCRATCH[_n] = _sb(_w, "uint16")
@@ -169,9 +169,9 @@ def rank_program(g, core, T, topo):
         return rev(T.ps, 512 * k)
 
     col = lambda j: T.col[:, j:j + 1]
-    R_, NR, R15, H1, H2, NB, R16, PAR, RH, M15, NM15 = range(11)
+    R_, NR, R15, H1, H2, NB, N8, PAR, RH, M15, NM15, P8 = range(12)
     MRB, MLW, MLB, BMB = 16, 464, 480, 937
-    CL, CR, TL, TR, PK = 0, 28, 56, 84, 112
+    CL, CR, TL, TR = 0, 28, 56, 84
     O_L2, O_LR, O_W, O_AT, O_O = 0, 56, 112, 168, 200
     VR, VL, CN, CP = 512, 640, 768, 896
     HALF = C // 2
@@ -179,12 +179,19 @@ def rank_program(g, core, T, topo):
     wk = lambda j, a=0, n=56: T.wk[:, 64 * j + a:64 * j + n]
     plane = lambda t, b, a=0, n=C: t[:, C * b + a:C * b + n]
 
+    def blocks(k, a, b, tag):
+        n, src = b - a, "ps%d " % k
+        tt(T.sm[:, a:b], bank(k, n), T.msk[:, 16 + a:16 + b], A.mult, src + "msk", "sm" + tag)
+        scan(rev(T.win, MLB + a, n), rev(T.ps, 512 * k, n), rev(T.kml, a, n), -HUGE, A.max, A.subtract, src + "kml", "ml" + tag)
+        scan(T.sw[:, a:b], T.k16[:, a:b], T.sm[:, a:b], 0.0, A.mult, A.add, "k16 sm" + tag, "sw" + tag)
+        scan(T.win[:, MRB + a:MRB + b], bank(k, n), T.kmr[:, a:b], -HUGE, A.max, A.subtract, src + "kmr", "mr" + tag)
+
     dma("a", T.ut[:], T.u[:], "", "ut")
     dma("s", T.x0[:, 0:896], T.x[:, 0:896], "", "x0a")
     dma("s", T.x0[:, 896:], T.x[:, 896:], "", "x0b")
 
     op("g", lambda: g.iota(T.pi[:, 0:1], [[0, 1]], 0, 1), "", "pi0")
-    iota(T.tab[:, 296:312], [[1, 2], [16, 8]], 0, 0, "upl")
+    iota(T.tab[:, 320:336], [[1, 2], [16, 8]], 0, 0, "upl")
     iota(T.i16[:], [[0, 29], [1, 16]], 0, 0, "i16")
     iota(tab(0), [[0, 28], [16, 2]], 1, 0, "c0")
     iota(tab(56, 28), [[-1, 14], [0, 2]], 15, 0, "ta")
@@ -195,21 +202,21 @@ def rank_program(g, core, T, topo):
     iota(T.blk[:], [[0, 128]], 1, 0, "blk")
     pick(T.blk[:], T.blk[:], [[-16, 8], [0, 16]], A.is_ge, 0.0, 0, 1, "blk", "blk")
     pick(T.blk[:], T.blk[:], [[16, 8], [0, 16]], A.is_ge, 0.0, 15, -1, "blk", "blk")
+    iota(T.kl[:, 0:C], [[0, C]], -16, 0, "kll")
+    iota(T.kl[:, C:], [[0, C]], 16, 0, "klr")
     iota(T.t1[:, 3::4], [[0, C]], 0, 0, "t13")
 
     ms(T.tz[:], 0.0, "tz")
     ms(T.k16[:], 1.0, "k16")
     ts(T.pi[:, 1:2], T.pi[:, 0:1], 15, A.bitwise_and, "pi0", "pi1")
     fill = [lambda: cp(col(R_), T.pi[:, 1:2], "pi1", "r"), lambda: ms(T.k16[:, 0::16], 0.0, "k16"),
-            lambda: cp(T.upk[:], T.tab[:, 296:312], "upl", "upk"), lambda: ms(T.win[:, 0:15], HUGE, "wino"),
+            lambda: cp(T.upk[:], T.tab[:, 320:336], "upl", "upk"), lambda: ms(T.win[:, 0:15], HUGE, "wino"),
             lambda: ms(T.win[:, 464:480], HUGE, "winp"), lambda: ms(T.win[:, 929:968], HUGE, "winq"),
             lambda: ms(T.smr[:, 448:456], -HUGE, "smrp"), lambda: ms(T.sml[:, 0:8], -HUGE, "smlp")]
     for j in range(1, 9):
         ms(T.tz[:, 0::2 ** j], float(j), "tz")
         fill[j - 1]()
     ms(T.tz[:, 0:1], 15.0, "tz")
-    ms(T.kl[:, 0:C], -16.0, "kll")
-    ms(T.kl[:, C:], 16.0, "klr")
     ts(T.msk[:], T.i16[:], col(R_), A.is_equal, "i16 r", "msk")
     act(col(H1), col(R_), F.Identity, "r", "h1", -HUGE, HUGE)
     act(col(H2), col(R_), F.Identity, "r", "h2", HUGE, HUGE)
@@ -218,30 +225,32 @@ def rank_program(g, core, T, topo):
     act(wk(0), tab(0), F.Identity, "c0 r", "w0", 1.0, col(R_))
     act(tab(112), tab(56), F.Identity, "ta tb_", "tc", -2.0, 31.0)
     quant("u", 0, 128, T.ut[:], "ut", "qu")
+    tt(wk(1), wk(0), tab(56), A.is_gt, "w0 ta tb_", "w1")
     op("v", lambda: V.tensor_copy(T.qp[:, 0:256].bitcast(dt.uint32), T.qu[:, 0:128].bitcast(dt.uint32).indirect(T.upk[:, 0:16])),
        "qu upk", "qp")
     act(T["sp_"][:, 0:256], T["su_"][:, 0:128].indirect(T.upk[:, 0:16]), F.Copy, "qu upk", "sp")
     act(T.klev[:], T.tz[:], F.Relu, "tz h1", "klev", HUGE, col(H1))
-    tt(wk(1), wk(0), tab(56), A.is_gt, "w0 ta tb_", "w1")
-    quant("x", 0, HALF, T.x0[:, 0:896], "x0a", "qxa")
     tt(wk(2), wk(1), tab(112), A.mult, "w1 tc", "w2")
     tt(wk(3), wk(1), tab(56), A.mult, "w1", "w3")
-    quant("x", HALF, C, T.x0[:, 896:], "x0b", "qxb")
-    dma("s", T.qw[:].bitcast(dt.uint8), T.wc[:], "x0a x0b", "qw")
-    dma("s", T["sw_"][:], T.ws[:], "", "sw_")
-    dma("s", T.vt[:], T.v[:], "", "vt")
+    quant("x", 0, HALF, T.x0[:, 0:896], "x0a", "qxa")
+    mm(3, "p", 0, "x", 0, HALF, "qp sp qxa")
     tt(wk(4), wk(2), tab(56), A.add, "w2", "w4")
     tt(wk(5), wk(0), wk(3), A.subtract, "w0 w3", "w5")
-    act(T.dga[:], T.dgi[:], F.Abs, "dgi", "dga", 1.0, -3.0)
-    act(T.win[:, 15:16], T.msk[:, 16:17], F.Identity, "msk", "winr", -2 * HUGE, HUGE)
-    act(T.win[:, 928:929], T.msk[:, 16:17], F.Identity, "msk", "wins", -2 * HUGE, HUGE)
+    ts(T.lu[:, TL:TL + 28], wk(4, 0, 28), 16.0, A.mult, "w4", "ltl", -17.0, A.add)
+    blocks(3, 0, HALF, "a")
+    quant("x", HALF, C, T.x0[:, 896:], "x0b", "qxb")
+    ts(T.lu[:, TR:TR + 28], wk(4, 28), -16.0, A.mult, "w4", "ltr", 479.0, A.add)
+    tt(wk(6), wk(5), wk(4), A.is_equal, "w5 w4", "w6")
     act(wk(7, 0, 28), wk(4, 0, 28), F.Identity, "w4", "w7a", 15.0, float(MLB - BMB - 30))
     act(wk(7, 28), wk(4, 28), F.Identity, "w4", "w7b", -15.0, float(466 - BMB))
     act(wk(1, 0, 28), wk(5, 0, 28), F.Identity, "w5", "w1a w1", 1.0, float(BMB - 2))
     act(wk(1, 28), wk(5, 28), F.Identity, "w5 w1", "w1b", -1.0, float(BMB + 29))
-    ts(T.lu[:, TL:TL + 28], wk(4, 0, 28), 16.0, A.mult, "w4", "ltl", -17.0, A.add)
-    ts(T.lu[:, TR:TR + 28], wk(4, 28), -16.0, A.mult, "w4", "ltr", 479.0, A.add)
-    tt(wk(6), wk(5), wk(4), A.is_equal, "w5 w4", "w6")
+    dma("s", T.qw[:].bitcast(dt.uint8), T.wc[:], "x0a x0b", "qw")
+    dma("s", T["sw_"][:], T.ws[:], "", "sw_")
+    dma("s", T.vt[:], T.v[:], "", "vt")
+    act(T.win[:, 15:16], T.msk[:, 16:17], F.Identity, "msk", "winr", -2 * HUGE, HUGE)
+    act(T.win[:, 928:929], T.msk[:, 16:17], F.Identity, "msk", "wins", -2 * HUGE, HUGE)
+    act(T.dga[:], T.dgi[:], F.Abs, "dgi", "dga", 1.0, -3.0)
 
     def setup_0():
         act(T.dg[:], T.dga[:], F.Relu, "dga", "dg", -1.0, 1.0)
@@ -255,80 +264,80 @@ def rank_program(g, core, T, topo):
             iota(T[n][:, 0:16], [[0, 16]], v, 0, n + "p")
             iota(T[n][:, 464:480], [[0, 16]], v, 0, n + "q")
         iota(T.iw[:], [[1, 464]], 0, 0, "iw")
-        iota(tab(260, 2), [[256, 2]], 15, 0, "kp")
-        iota(T.sma[:, 156:160], [[0, 4]], 0, 0, "ownp")
+        iota(T.b32[:], [[0, 15], [1, 2], [0, 16]], 0, 0, "b32")
         act(col(NR), col(R_), F.Copy, "r", "nr_", -1.0)
         act(col(R15), col(R_), F.Identity, "r", "r15", -1.0, 15.0)
+        act(col(RH), col(R_), F.Identity, "r", "rh", -1.0, 0.5)
+        tt(wk(6), wk(6), wk(7), A.mult, "w6 w7a w7b", "w6")
+
+    def unit(b):
+        quant("c", 128 * b, 128 * b + 128, T.dg[:, 3 - b:515 - b], "dg", "e%d" % b)
 
     def setup_1():
-        tt(wk(6), wk(6), wk(7), A.mult, "w6 w7a w7b", "w6")
-        for b in range(3):
-            quant("c", 128 * b, 128 * b + 128, T.dg[:, 3 - b:515 - b], "dg", "e%d" % b)
+        unit(0)
         tt(wk(6), wk(6), wk(1), A.add, "w6 w1a w1b", "w6")
+        unit(1)
         cp(T.lu[:, 0:56], wk(6), "w6", "lu")
-        for view, c_, key in ((T.kl[:, 14:418:31], NR, "kll"), (T.kl[:, 30:C:32], NR, "kll"),
-                              (T.kl[:, 449::33], R15, "klr"), (T.kl[:, 478::32], R15, "klr")):
+        unit(2)
+        act(T.k01[:], T.klev[:], F.Relu, "klev", "k01", -2.0 / HUGE, 1.0)
+        for view, c_, key in ((T.kl[:, 14:418:31], NR, "kll"), (T.kl[:, 449::33], R15, "klr"),
+                              (T.kl[:, 30:C:32], NR, "kll"), (T.kl[:, 478::32], R15, "klr")):
             act(view, T.i16[:, 0:14], F.Identity, "i16 nr_ r15", key, 0.0, col(c_))
         act(tab(168, 84), tab(168, 84), F.Identity, "ck ck1 r", "ck ck1", 1.0, col(R_))
-        act(T.k01[:], T.klev[:], F.Relu, "klev", "k01", -2.0 / HUGE, 1.0)
         act(T.kc[:], T.k01[:], F.Identity, "k01", "kc", 2.0, -1.0)
 
-    def weights(t, key, w):
-        act(t[:], T.dg[:, 0:512], F.Copy, "dg", key + "z", 0.0)
-        for j, (at, v) in enumerate(((0, 1.0), (1, w), (6, 1.0), (7, w))):
-            act(t[:, at::8], T.blk[:, j // 2::2], F.Copy, "blk %sz" % key, key + str(j), v)
-
     def setup_a():
+        ts(T.pi[:, 3:4], T.pi[:, 1:2], 1, A.arith_shift_right, "pi1", "pi3")
         quant("c", VR, VR + 128, T.dv[:, 1:513], "dv", "cvr")
+        ts(col(N8), T.pi[:, 3:4], 1024.0, A.mult, "pi3", "n8", -7168.0, A.add)
         quant("c", VL, VL + 128, T.dv[:, 3:515], "dv", "cvl")
-        weights(T.cn, "cn", 32.0)
-        weights(T.cp, "cp", 1.0)
-
-    def setup_b():
-        act(col(RH), col(R_), F.Identity, "r", "rh", -1.0, 0.5)
+        act(T.cn[:], T.dg[:, 0:520], F.Copy, "dg", "cnz", 0.0)
         act(T.k8a[:], T.i16[:, 0:C:2], F.Abs, "i16 rh", "k8a", 1.0, col(RH))
+        act(T.cn[:, 1:513:8], T.blk[:, 0::2], F.Copy, "blk cnz", "cn0")
+        act(T.cn[:, 7:513:8], T.blk[:, 1::2], F.Copy, "blk cnz", "cn1")
         act(T.k8a[:], T.k8a[:], F.Relu, "k8a", "k8a", -1.0, 1.5)
-        act(T.kd8[:], T.k8a[:], F.Identity, "k8a", "kd8", -16384.0, 1024.0)
-        quant("c", CN, CN + 128, T.cn[:], "cn0 cn1 cn2 cn3", "cn")
-
-    def setup_c():
         act(col(M15), col(R15), F.Sign, "r15", "m15")
         act(col(NM15), col(R15), F.Sign, "r15", "nm15", -1.0)
-        act(col(NB), col(R15), F.Copy, "r15", "nb", -1024.0)
-        act(col(R16), col(R_), F.Copy, "r", "r16", 16.0)
+        act(T.kd8[:], T.k8a[:], F.Identity, "k8a", "kd8", -16384.0, 1024.0)
+
+    def setup_b():
+        quant("c", CN, CN + 128, T.cn[:, 1:513], "cn0 cn1", "cn")
+        quant("c", CP, CP + 128, T.cn[:, 0:512], "cn0 cn1", "cp")
 
     def setup_d():
-        ts(T.pi[:, 2:3], T.pi[:, 0:1], 4, A.arith_shift_right, "pi0", "pi2")
-        quant("c", CP, CP + 128, T.cp[:], "cp0 cp1 cp2 cp3", "cp")
-        tt(T.pi[:, 3:4], T.pi[:, 2:3], T.pi[:, 0:1], A.add, "pi2 pi0", "pi3")
+        ts(T.pi[:, 2:3], T.pi[:, 0:1], 4, A.arith_shift_right, "pi0", "pi2", 1, A.bitwise_and)
 
     def setup_e():
+        ts(col(PAR), T.pi[:, 2:3], -1.0, A.add, "pi2", "par")
+        act(T.ks[:], T.b32[:], F.Abs, "b32 par", "ks", 1.0, col(PAR))
         act(T.kdb[:], T.msk[:, 16:464], F.Identity, "msk", "kdb", -32768.0, 1024.0)
-        ts(T.pi[:, 4:5], T.pi[:, 3:4], 1, A.bitwise_and, "pi3", "pi4")
-        quant("c", 384, 512, T.dg[:, 0:512], "dg", "e3")
-        ts(col(PAR), T.pi[:, 4:5], 464.0, A.mult, "pi4 r16", "par", col(R16), A.add)
+        unit(3)
 
     def setup_f():
-        ts(T.lu[:, PK:PK + 2], tab(260, 2), col(PAR), A.add, "kp par", "pk", 927.0, A.min)
         quant("v", 0, 128, T.vt[:], "vt", "qv")
 
     def planes():
+        act(col(P8), col(N8), F.Copy, "n8", "p8", -1.0)
+        act(col(NB), col(R15), F.Copy, "r15", "nb", -1024.0)
+        act(tab(256, 28), tab(224, 28), F.Identity, "ck1 p8", "ckd0", 1.0, col(P8))
+        act(tab(284, 28), tab(196, 28), F.Identity, "ck p8", "ckd1", 1.0, col(P8))
         for b in range(4):
             act(plane(T.x64, b), T.x0[:, b::4], F.Copy, "x0a x0b", "fa%d fb%d" % (b, b), 64.0)
 
     sma = lambda a, n=56: T.sma[:, a:a + n]
     ni = lambda a, n=56: T.ni[:, a:a + n]
-    DD, WW, OWN, AT = 0, 64, 128, 192
-    IX, B16, NI, CNT, TT, PI, SEL = 0, 56, 112, 140, 196, 252, 308
+    DD, WW, OWN, AT, TT = 0, 64, 128, 160, 256
+    IX, B16, PI, SEL = 0, 56, 112, 168
     off = lambda a, n=28: T.off[:, a:a + n]
-    WIN = "mr ml bm wino winp winq winr wins"
+    WIN = "mra mrb mla mlb bm wino winp winq winr wins"
     RL, FL, RR = 0, 1, 2
 
-    def counted(const, key, between):
-        quant("b", 0, HALF, T.tb[:], "tb0 tb1", "qb")
-        mm(1, "c", const, "b", 0, HALF, key + " qb")
-        between()
-        scan(T.nd[:, 0:HALF], T.kd8[:], bank(1, HALF), 0.0, A.add, A.max, "kd8 ps1", "nd")
+    def others():
+        act(T.nrr[:], T.t1[:, RR::4], F.Identity, "t1r", "nrr", -1.0, 1.0)
+        act(T.nrl[:], T.t1[:, RL::4], F.Identity, "t1l m15 nm15", "nrl", col(NM15), col(M15))
+
+    def fold8(k, h, key):
+        scan(T.nd[:, HALF * h:HALF * h + HALF], T.kd8[:], bank(k, HALF), 0.0, A.add, A.max, "kd8 ps%d" % k, key)
 
     for rnd in range(ROUNDS):
         first, last = rnd == 0, rnd == ROUNDS - 1
@@ -337,34 +346,33 @@ def rank_program(g, core, T, topo):
         send(T["q" + l_][:].bitcast(dt.uint8), T.qx[:].bitcast(dt.uint8), "arr" + n_, "out" + n_, 2 * nout, "qxa qxb", "")
         send(T["s" + l_ + "_"][:], T["sx_"][:], "arr" + n_, "out" + n_, 2 * nout, "qxa qxb", "sent" + n_)
         op("x", None, "", l_, ("arr" + n_, 2 * nin))
+        a, b = (HALF, C) if first else (0, K)
+        mm(4, "p", 0, "x", a, b, "qp sp qxa qxb")
         mm(0, "p", 0, "x", 0, C, "qp sp qxa qxb")
         mm(2, "p", 128, "x", 0, C, "qp sp qxa qxb")
         mm(1, "p", 0, "x", 0, C, "qp sp qxa qxb")
         once(setup_0)
-        if first:
-            tt(T.sm[:], bank(0), T.msk[:, 16:464], A.mult, "ps0 msk", "sm smb")
-        else:
-            tt(T.sm[:, K:], bank(3, C - K), T.msk[:, 16 + K:464], A.mult, "ps3 msk", "smb")
-            tt(T.sm[:, 0:K], bank(0, K), T.msk[:, 16:16 + K], A.mult, "ps0 msk", "sm")
-        scan(rev(T.win, MLB), rbank(0), rev(T.kml, 0), -HUGE, A.max, A.subtract, "ps0 kml", "ml")
-        scan(T.sw[:], T.k16[:, 0:C], T.sm[:], 0.0, A.mult, A.add, "k16 sm smb", "sw")
+        if not first:
+            blocks(3, K, C, "a")
+        blocks(4, a, b, "b")
         act(T.sg[:], bank(2), F.Sign, "ps2", "sg")
-        scan(T.win[:, MRB:MRB + C], bank(0), T.kmr[:], -HUGE, A.max, A.subtract, "ps0 kmr", "mr")
+        act(T.thr[:, 0:C], T.sw[:].indirect(T.lu[:, TL:TL + 28]), F.Copy, "swa swb ltl", "thl")
+        act(T.thr[:, C:2 * C], T.sw[:].indirect(T.lu[:, TR:TR + 28]), F.Copy, "swa swb ltr", "thr")
         act(T.t1[:, FL::4], T.sg[:], F.Relu, "sg", "t1f")
-        act(T.thr[:, 0:C], T.sw[:].indirect(T.lu[:, TL:TL + 28]), F.Copy, "sw ltl", "thl")
-        act(T.thr[:, C:2 * C], T.sw[:].indirect(T.lu[:, TR:TR + 28]), F.Copy, "sw ltr", "thr")
         scan(rev(T.smr, 0), rbank(0), rev(T.klev, 0), -HUGE, A.max, A.subtract, "ps0 klev", "smr")
-        tt(sma(224, 28), T.win[:, MLB:MLB + C:16], T.win[:, 31:464:16], A.max, "ml mr", "bm0")
+        tt(sma(224, 28), T.win[:, MLB:MLB + C:16], T.win[:, 31:464:16], A.max, "mla mlb mra mrb", "bm0")
         scan(T.sml[:, 8:456], bank(0), T.klev[:, 1:449], -HUGE, A.max, A.subtract, "ps0 klev", "sml")
-        tt(T.win[:, BMB:BMB + 28], sma(224, 28), T.sw[:, 15::16], A.max, "bm0 sw winq", "bm")
-        tt(T.t1[:, RR::4], bank(0), T.smr[:, 1:449], A.is_ge, "ps0 smr smrp", "t1r")
+        tt(T.win[:, BMB:BMB + 28], sma(224, 28), T.sw[:, 15::16], A.max, "bm0 swa swb winq", "bm")
         once(setup_1)
         act(T.ssb[:], bank(1), F.Copy, "ps1", "ssb")
-        tt(T.t1[:, RL::4], bank(0), T.sml[:, 7:455], A.is_gt, "ps0 sml smlp", "t1l")
+        tt(T.t1[:, RR::4], bank(0), T.smr[:, 1:449], A.is_ge, "ps0 smr smrp", "t1r")
         tt(T.nf[:, 0:C], T.win[:, 0:968].indirect(T.lu[:, CL:CL + 28]), T.thr[:, 0:C], A.is_lt, WIN + " lu thl", "nfl")
-        quant("1", 0, C, T.t1[:], "t1l t1f t1r t13", "q1")
+        tt(T.t1[:, RL::4], bank(0), T.sml[:, 7:455], A.is_gt, "ps0 sml smlp", "t1l")
         tt(T.nf[:, C:2 * C], T.win[:, 0:968].indirect(T.lu[:, CR:CR + 28]), T.thr[:, C:2 * C], A.is_le, WIN + " lu thr", "nfr")
         once(setup_a)
+        quant("1", 0, C, T.t1[:], "t1l t1f t1r t13", "q1")
+        if not first:
+            others()
         scan(T.run[:], T.kl[:], T.nf[:], 0.0, A.add, A.mult, "kll klr nfl nfr", "run")
         mm(3, "c", 128 * FL, "1", 0, C, "e1 q1", True, False)
         mm(3, "c", 128 * RL, "1", 0, C, "e0 q1", False, True)
@@ -373,41 +381,43 @@ def rank_program(g, core, T, topo):
         mm(5, "c", VR, "1", 0, C, "cvr q1")
         mm(6, "c", VL, "1", 0, C, "cvl q1")
         mm(7, "c", 128 * RR, "1", 0, C, "e2 q1")
-        act(T.v1r[:], bank(3), F.Sign, "ps3", "v1r", -1.0, 1.5)
         tt(ni(IX + 14, 28), T.run[:, 30::32], tab(182, 28), A.add, "run ck", "ixb")
         tt(ni(IX, 14), T.run[:, 417:13:-31], tab(168, 14), A.add, "run ck", "ixa")
         tt(ni(IX + 42, 14), T.run[:, 878:448:-33], tab(210, 14), A.add, "run ck", "ixc")
         once(setup_b)
         cp(off(O_L2, 56), ni(IX), "ixa ixb ixc", "ol2")
         act(T.ga[:], T.win[:, 0:464].indirect(off(O_L2)), F.Copy, WIN + " ol2", "ga")
-        act(T.v1l[:], bank(4), F.Sign, "ps4", "v1l", -1.0, 1.5)
-        tt(T.tb[:, 1::2], T.win[:, MLW:936].indirect(off(O_L2 + 28)), T.ssb[:], A.is_le, WIN + " ol2 ssb", "tb1")
         ts(ni(B16), ni(IX), 0xFFF0, A.bitwise_and, "ixa ixb ixc", "b16")
-        tt(T.tb[:, 0::2], T.ga[:], bank(0), A.is_ge, "ga ps0", "tb0")
-        once(setup_c)
+        act(T.v1r[:], bank(3), F.Sign, "ps3", "v1r", -1.0, 1.5)
+        act(T.v1l[:], bank(4), F.Sign, "ps4", "v1l", -1.0, 1.5)
         act(T.vr[:], bank(5), F.Copy, "ps5", "vr")
-        act(T.nrr[:], T.t1[:, RR::4], F.Identity, "t1r", "nrr", -1.0, 1.0)
-        act(T.nrl[:], T.t1[:, RL::4], F.Identity, "t1l m15 nm15", "nrl", col(NM15), col(M15))
-        counted(CN, "cn", lambda: scan(rev(T.c1r, 17), rev(T.kc, 1), rev(T.v1r, 0), -1.0, A.min, A.mult, "kc v1r", "c1r"))
-        cp(ni(NI, 28), T.nd[:, 7:HALF:8], "nd", "ni")
+        once(others)
+        tt(T.tb[:, 1::2], T.win[:, MLW:936].indirect(off(O_L2 + 28)), T.ssb[:], A.is_le, WIN + " ol2 ssb", "tb1")
+        tt(T.tb[:, 0::2], T.ga[:], bank(0), A.is_ge, "ga ps0", "tb0")
+        quant("b", 0, HALF, T.tb[:], "tb0 tb1", "qb")
+        mm(1, "c", CN, "b", 0, HALF, "cn qb")
+        mm(2, "c", CP, "b", 0, HALF, "cp qb")
+        scan(rev(T.c1r, 17), rev(T.kc, 1), rev(T.v1r, 0), -1.0, A.min, A.mult, "kc v1r", "c1r")
         scan(T.c1l[:, 16:464], T.kc[:, 0:C], T.v1l[:], -1.0, A.min, A.mult, "kc v1l", "c1l")
-        ts(ni(CNT, 28), ni(NI, 28), 31, A.bitwise_and, "ni", "nl")
-        ts(ni(CNT + 28, 28), ni(NI, 28), 5, A.arith_shift_right, "ni", "nr", 31, A.bitwise_and)
+        fold8(1, 0, "nd")
+        fold8(2, 1, "nd1")
+        tt(sma(TT, 28), T.nd[:, 7:HALF:8], ni(B16, 28), A.add, "nd b16", "tl")
+        tt(sma(TT + 28, 28), T.nd[:, HALF + 7::8], ni(B16 + 28, 28), A.add, "nd1 b16", "tr")
         once(setup_d)
-        tt(ni(TT), ni(CNT), ni(B16), A.add, "nl nr b16", "tt_")
-        cp(off(O_LR, 56), ni(TT), "tt_", "olr")
+        ts(off(O_LR, 56), sma(TT), col(N8), A.add, "tl tr n8", "olr")
         act(T.g1l[:], T.c1l[:].indirect(off(O_LR)), F.Identity, "c1l c1lp c1lq olr", "g1l", -0.5, 1.5)
         tt(T.b1r[:], T.c1r[:].indirect(off(O_LR + 28)), T.vr[:], A.is_equal, "c1r c1rp c1rq olr vr", "b1r")
-        tt(T.b1l[:], T.g1l[:], bank(6), A.is_le, "g1l ps6", "b1l")
         scan(T.tb[:, 2 * C - 2::-2], rev(T.nrr, 0), rev(T.b1r, 0), 0.0, A.mult, A.add, "nrr b1r", "tb0")
-        scan(T.tb[:, 1::2], T.nrl[:], T.b1l[:], 0.0, A.mult, A.add, "nrl b1l", "tb1")
+        tt(T.b1l[:], T.g1l[:], bank(6), A.is_le, "g1l ps6", "b1l")
         once(planes)
-
-        def lengths():
-            tt(sma(DD, 28), tab(224, 28), ni(TT, 28), A.subtract, "tt_ ck1", "dl")
-            tt(sma(DD + 28, 28), ni(TT + 28, 28), tab(196, 28), A.subtract, "tt_ ck", "dr")
-            once(setup_e)
-        counted(CP, "cp", lengths)
+        tt(sma(DD, 28), tab(256, 28), sma(TT, 28), A.subtract, "tl ckd0", "dl")
+        scan(T.tb[:, 1::2], T.nrl[:], T.b1l[:], 0.0, A.mult, A.add, "nrl b1l", "tb1")
+        quant("b", 0, HALF, T.tb[:], "tb0 tb1", "qb")
+        mm(1, "c", CN, "b", 0, HALF, "cn qb", True, False)
+        mm(1, "c", CP, "b", 0, HALF, "cp qb", False, True)
+        tt(sma(DD + 28, 28), sma(TT + 28, 28), tab(284, 28), A.subtract, "tr ckd1", "dr")
+        once(setup_e)
+        fold8(1, 0, "nd")
         DB = (3, 4, 0, 1)
         for b in range(4):
             mm(DB[b], "c", 128 * b, l_, 0, C, "e%d %s" % (b, l_))
@@ -434,14 +444,15 @@ def rank_program(g, core, T, topo):
         tt(T.hh[:, 16:464], T.h2r[:], T.h2l[:], A.add, "h2r h2l", "hh")
         op("v", lambda: V.transpose(T.tt[:, 0:448], T.hh[:, 16:464]), "hh", "tta")
         op("v", lambda: V.transpose(T.tt[:, 448:928], T.hh[:, 0:480]), "hh hhp hhq", "ttb")
-        scan(T.ts[:, 0:448], T.k16[:, 0:448], T.tt[:, 0:448], 0.0, A.mult, A.add, "k16 tta", "tsa")
-        scan(T.ts[:, 448:928], T.k16[:], T.tt[:, 448:928], 0.0, A.mult, A.add, "k16 ttb", "tsb")
-        tt(sma(AT, 32), T.ts[:].indirect(T.lu[:, PK:PK + 2]), sma(OWN, 32), A.add, "tsa tsb pk own ownp", "at")
-        ts(off(O_AT), sma(AT, 28), -1.0, A.add, "at", "oat")
+        scan(T.ts[:, 0:448], T.tt[:, 0:448], T.ks[:, 0:448], 0.0, A.add, A.mult, "ks tta", "tsa")
+        scan(T.ts[:, 448:928], T.tt[:, 448:928], T.ks[:], 0.0, A.add, A.mult, "ks ttb", "tsb")
+        tt(sma(AT, 28), T.ts[:, 15:448:16], sma(OWN, 28), A.add, "tsa own", "at0")
+        tt(sma(AT + 32, 28), T.ts[:, 479:927:16], sma(AT, 28), A.add, "tsb at0", "at")
+        ts(off(O_AT), sma(AT + 32, 28), -1.0, A.add, "at", "oat")
         cp(T.ord[:].indirect(off(O_AT)), T.iw[:, 0:C], "oat iw", "ord")
-        scan(T.nd[:], T.kdb[:], T.ord[:], 0.0, A.add, A.max, "kdb ord", "nd")
+        scan(T.nd[:], T.kdb[:], T.ord[:], 0.0, A.add, A.max, "kdb ord", "nd nd1")
         oo = O_O + 32 * rnd
-        ts(off(oo), T.nd[:, 15::16], col(NB), A.add, "nd nb", "oo")
+        ts(off(oo), T.nd[:, 15::16], col(NB), A.add, "nd nd1 nb", "oo")
         send(T["came" + n_][:], off(oo + 20, 8), "larr" + n_, "lout" + n_, nout, "oo", "lsent" + n_)
         op("x", None, "", "came" + n_, ("larr" + n_, nin))
         if last:
@@ -455,6 +466,7 @@ def rank_program(g, core, T, topo):
         own, came = (lambda t, b: t[:, 4 * K + b::4]), (lambda t, b: t[:, b:4 * K:4])
         for b, e in ((2, "a"), (0, "v"), (3, "a"), (1, "v")):
             scale(e, own(T.z, b), plane(T.x64, b).indirect(off(oo, 20)), 1.0 / 64, "oo fa%d fb%d" % (b, b), "zb%d" % b)
+        scale("v", plane(T.z64, 0, K), own(T.z, 0), 64.0, "zb0", "sb0")
         quant("z", K, C, T.z[:, 4 * K:], "zb0 zb1 zb2 zb3", "qzb")
         for b in range(4):
             mm(b, "w", 128 * b, "z", K, C, "qw sw_ qzb")
@@ -490,7 +502,7 @@ def rank_program(g, core, T, topo):
                 dma("a", T.y[:, K:C], T.ysb[:, K:C], "yb", "y_b")
             else:
                 quant("x", 0, K, T.xs[:, 0:4 * K], "xa0 xa1 xa2 xa3", "qxa")
-        order = "sb0a sb1a za0v za1v za2a za3a sb2a sb3a fb0v qz0v fb1v xb0a "
+        order = "sb1a sb2a za0v za1v za2a za3a sb3a fb0v fb1v qz0v xb0a "
         if last:
             order += "xb1a fb2v fb3v xb2v xb3v sa0a sa1a sa2a sa3a qb0v fa0v fa1v fa2v fa3v yb0a xa0v xa1v xa2v xa3v qa0v"
         else:

@@ -2,7 +2,9 @@ from concourse.mybir import dt, AluOpType as A, ActivationFunctionType as F
 
 C, K, ROUNDS = 448, 128, 2
 HUGE = 2.0 ** 90
+MID = 224.0
 CODE, PLANE = "float8_e4m3fn_x4", "uint8"
+WIDTH = {"bfloat16": 2, "float16": 2, "uint16": 2, "float32": 4, "int32": 4, CODE: 4, PLANE: 1}
 
 
 def _sb(n, d):
@@ -11,67 +13,131 @@ def _sb(n, d):
 
 SCRATCH = {"ps": ("psum", [128, 4096], "float32")}
 for _n, _w in (("x0", 1792), ("xs", 1792), ("x64", 1792), ("z", 1792), ("z64", 1792), ("dec", 1792), ("ut", 512), ("vt", 512),
-               ("t1", 1792), ("tb", 896), ("kd8", 224), ("k8a", 224), ("i16", 464), ("tz", 464), ("msk", 464), ("kml", 448),
-               ("kmr", 448), ("klev", 464), ("k01", 464), ("kc", 464), ("k16", 448), ("kdb", 448), ("kl", 896), ("dgi", 528),
-               ("dga", 528), ("dg", 528), ("dv", 520), ("cn", 520), ("ks", 480), ("b32", 480), ("blk", 128), ("sg", 448),
-               ("nrr", 448), ("nrl", 448), ("v1r", 448), ("v1l", 448), ("vr", 448), ("c1r", 480), ("c1l", 480), ("b1r", 448),
-               ("b1l", 448), ("g1l", 448), ("nf", 896)):
+               ("t1", 1792), ("tb", 1024), ("kd4", 128), ("k4a", 128), ("i16", 464), ("tz", 464), ("msk", 464), ("kml", 448),
+               ("kmr", 448), ("klev", 464), ("k01", 464), ("kc", 464), ("kc2", 464), ("k16", 448), ("kdb", 448), ("ka", 464),
+               ("kb", 464), ("kl", 896), ("dgi", 528), ("dga", 528), ("dg", 528), ("dv", 520), ("c4", 512), ("c5", 512),
+               ("ks", 480), ("b32", 480), ("blk", 64), ("nrr", 448), ("nrl", 448), ("v1r", 448), ("v1l", 448), ("vr", 448),
+               ("c1r", 480), ("c1l", 480), ("c2r", 480), ("c2l", 480), ("b1r", 448), ("b1l", 448), ("g1l", 448), ("nf", 896),
+               ("run", 896), ("ord", 448), ("rb", 448)):
     SCRATCH[_n] = _sb(_w, "bfloat16")
 for _n, _w in (("w2r", 448), ("w2l", 448), ("g2r", 448), ("g2l", 448), ("h2r", 448), ("h2l", 448), ("hh", 480), ("tt", 928),
-               ("run", 896), ("ts", 928)):
+               ("ts", 928), ("no", 448)):
     SCRATCH[_n] = _sb(_w, "float16")
-for _n, _w in (("win", 968), ("sm", 448), ("sw", 448), ("smr", 456), ("sml", 456), ("thr", 896), ("ssb", 448), ("nd", 448),
-               ("c2r", 480), ("c2l", 480), ("ord", 448), ("iw", 464), ("ga", 448), ("gb", 448), ("gw", 448),
-               ("ysb", 448), ("col", 16), ("tab", 336), ("wk", 512), ("sma", 320)):
+for _n, _w in (("win", 968), ("sm", 448), ("sw", 448), ("smr", 456), ("sml", 456), ("thr", 896), ("nd", 336), ("kd", 224),
+               ("ordf", 448), ("iw", 976), ("ga", 448), ("gb", 448), ("gw", 448), ("ysb", 448), ("col", 24), ("tab", 336),
+               ("wk", 640), ("sma", 320)):
     SCRATCH[_n] = _sb(_w, "float32")
 for _n, _w in (("pi", 8), ("ni", 256)):
     SCRATCH[_n] = _sb(_w, "int32")
 for _n, _w in (("lu", 128), ("upk", 16), ("off", 272), ("came0", 8), ("came1", 8)):
     SCRATCH[_n] = _sb(_w, "uint16")
-for _n, _w in (("x", 448), ("z", 448), ("u", 128), ("p", 256), ("v", 128), ("w", 512), ("c", 1024), ("1", 448), ("b", 224),
+for _n, _w in (("x", 448), ("z", 448), ("u", 128), ("p", 256), ("v", 128), ("w", 512), ("c", 1024), ("1", 448), ("b", 256),
                ("l0", 448), ("l1", 448)):
     SCRATCH["q" + _n] = _sb(_w, CODE)
     SCRATCH["s" + _n + "_"] = _sb(_w, PLANE)
 
-NSEM, NDMA = 112, 20
+NSEM, NDMA = 112, 24
 SEMAPHORES = (["c%d" % i for i in range(NSEM)] + ["d%d" % i for i in range(NDMA)]
               + [n + str(t) for n in ("arr", "out", "larr", "lout") for t in range(ROUNDS)])
+CYCLE, WAKE, ISSUE, DMA, RATE, PASSES, PATIENCE = 0.83, 200.0, 60.0, 700.0, 180.0, 4, 10.0
+
+
+def depends(ops):
+    seen, deps, after = {}, [], []
+    for i, (e, fn, rd, wr, kind, cost) in enumerate(ops):
+        d, o = set(), set()
+        for writes, parts in ((False, rd), (True, wr)):
+            for name, m in parts:
+                for j, mj, wj in seen.get(name, []):
+                    if m & mj and j != i:
+                        if wj and writes and kind == "acc" or name == "turn":
+                            o.add(j)
+                        elif wj or writes or name == "ps" and ops[j][0] != e:
+                            d.add(j)
+        for writes, parts in ((False, rd), (True, wr)):
+            for name, m in parts:
+                old = seen.get(name, [])
+                if writes:
+                    old = [x for x in old if x[1] & ~m]
+                seen[name] = old + [(i, m, writes)]
+        deps.append(d)
+        after.append(o)
+    return deps, after
+
+
+def place(ops, edges, urgency):
+    n = len(ops)
+    users = [[] for _ in range(n)]
+    for i in range(n):
+        for j in edges[i]:
+            users[j].append(i)
+    hold = [0.0 if o[0] == "x" else ISSUE if o[4] == "dma" or isinstance(o[4], tuple) else o[5] for o in ops]
+    left, start, free, seq = [len(x) for x in edges], [0.0] * n, {}, []
+    ready = {i: 0.0 for i in range(n) if not left[i]}
+    while ready:
+        best = None
+        for e in "vapgsx":
+            mine = [i for i in ready if ops[i][0] == e]
+            if mine:
+                t = max(free.get(e, 0.0), min(ready[i] for i in mine))
+                i = max(mine, key=lambda i: (urgency[i] - PATIENCE * max(0.0, ready[i] - t), -i))
+                if best is None or (max(t, ready[i]), i) < best:
+                    best = (max(t, ready[i]), i)
+        t, i = best
+        del ready[i]
+        seq.append(i)
+        start[i] = t
+        free[ops[i][0]] = t + hold[i]
+        for u in users[i]:
+            left[u] -= 1
+            if not left[u]:
+                ready[u] = max(start[j] + d for j, d in edges[u].items())
+    return start, seq
+
+
+def schedule(ops, deps, after):
+    n = len(ops)
+    lag = [0.0 if o[0] == "x" or o[4] == "dma" or isinstance(o[4], tuple) else WAKE for o in ops]
+    fore, back = [{} for _ in ops], [{} for _ in ops]
+    for i in range(n):
+        for j in deps[i] | after[i]:
+            fore[i][j] = ops[j][5] + lag[j] if j in deps[i] else 0.0
+            back[j][i] = ops[i][5] + lag[j] if j in deps[i] else max(0.0, ops[i][5] - ops[j][5])
+    urgency, best = [0.0] * n, None
+    for i in reversed(range(n)):
+        urgency[i] = ops[i][5] + max([urgency[u] - ops[u][5] + d for u, d in back[i].items()] + [0.0])
+    for _ in range(PASSES):
+        start, seq = place(ops, fore, urgency)
+        end = max(start[i] + ops[i][5] for i in range(n))
+        if best is None or end < best[0]:
+            best = (end, [seq[k] for k in sorted(range(n), key=lambda k: (start[seq[k]], k))])
+        start, seq = place(ops, back, [start[i] + ops[i][5] for i in range(n)])
+        urgency = [start[i] + ops[i][5] for i in range(n)]
+    return best[1]
 
 
 def emit(g, T, ops):
     queue = {"v": g.vector, "a": g.scalar, "p": g.tensor, "g": g, "s": g.sync}
-    writer, readers, known, at_issue, waits, needed = {}, {}, {}, [], [], set()
-    for i, (e, fn, rd, wr, kind) in enumerate(ops):
-        deps = set()
-        for key in rd:
-            if key in writer:
-                deps.add(writer[key])
-            if key.startswith("ps"):
-                deps.update(j for j in readers.get(key, []) if ops[j][0] != e)
-        implied = 0
-        for key in wr:
-            if key in writer:
-                if kind == "acc":
-                    implied |= 1 << writer[key]
-                else:
-                    deps.add(writer[key])
-            deps.update(readers.get(key, []))
+    deps, after = depends(ops)
+    order = schedule(ops, deps, after)
+    place = {i: n for n, i in enumerate(order)}
+    known, at_issue, waits, needed = {}, {}, {}, set()
+    for i in order:
+        e = ops[i][0]
         kn, mine = known.get(e, 0), []
-        for j in sorted(deps, reverse=True):
-            if not kn >> j & 1:
+        for j in sorted(deps[i], key=lambda j: -place[j]):
+            if e != "x" and not kn >> j & 1:
                 mine.append(j)
                 needed.add(j)
                 kn |= 1 << j | at_issue[j]
         known[e] = kn
-        at_issue.append(kn | implied)
-        waits.append(mine)
-        for key in rd:
-            readers.setdefault(key, []).append(i)
-        for key in wr:
-            writer[key] = i
-            readers[key] = []
+        for j in after[i]:
+            kn |= 1 << j | at_issue[j]
+        at_issue[i] = kn
+        waits[i] = mine
     user, count, mark, ndma = {}, {}, {}, 0
-    for i, (e, fn, rd, wr, kind) in enumerate(ops):
+    for i in order:
+        e, fn, rd, wr, kind, cost = ops[i]
         for j in reversed(waits[i]):
             queue[e].wait_ge(T.sem[mark[j][0]], mark[j][1])
         if isinstance(kind, tuple):
@@ -109,411 +175,382 @@ def rank_program(g, core, T, topo):
     ops = []
     V, S, P = g.vector, g.scalar, g.tensor
 
-    def op(e, fn, rd, wr, kind=None):
-        ops.append((e, fn, rd.split(), wr.split(), kind))
+    def w(name, a=0, b=None, s=1):
+        cols = range(*slice(a, b, s).indices(SCRATCH[name][1][1]))
+        bits = sum(set(1 << (c // 512 if name == "ps" else c) for c in cols))
+        return (T[name][:, a:b:s], [(name, bits)], len(cols), WIDTH[SCRATCH[name][2]], None)
 
-    def tt(out, a, b, o, rd, wr):
-        op("v", lambda: V.tensor_tensor(out, a, b, o), rd, wr)
+    def rev(name, a, n=C):
+        return w(name, a + n - 1, a - 1 if a else None, -1)
 
-    def ts(out, a, s1, o1, rd, wr, s2=None, o2=None):
-        if o2 is None:
-            op("v", lambda: V.tensor_scalar(out, a, s1, None, o1), rd, wr)
-        else:
-            op("v", lambda: V.tensor_scalar(out, a, s1, s2, o1, o2), rd, wr)
+    def by(win, lst, words=False):
+        ap = win[0].bitcast(dt.uint32) if words else win[0]
+        return (ap.indirect(lst[0]), win[1], 16 * lst[2], win[3], lst)
 
-    def cp(out, a, rd, wr):
-        op("v", lambda: V.tensor_copy(out, a), rd, wr)
+    def op(e, fn, rd, wr, cost, kind=None):
+        parts = lambda vs: [p for v in vs if isinstance(v, tuple) for p in (v[1] if len(v) == 5 else [v])]
+        lists = [v[4] for v in rd + wr if isinstance(v, tuple) and len(v) == 5 and v[4]]
+        ops.append((e, fn, parts(rd + lists), parts(wr), kind, cost))
 
-    def scan(out, d0, d1, init, o0, o1, rd, wr):
-        op("v", lambda: V.tensor_tensor_scan(out, d0, d1, init, o0, o1), rd, wr)
+    def time(out, ins, slow=1):
+        if out[4] or ins[0][4]:
+            return 50 + out[2] * CYCLE * (3 if out[4] else 1.5)
+        return max(64, out[2] * slow * (0.5 if all(v[3] == 2 for v in [out] + ins) else 1)) * CYCLE
 
-    def ms(out, val, wr):
-        op("v", lambda: V.memset(out, val), "", wr)
+    ap = lambda x: x[0] if isinstance(x, tuple) else x
 
-    def act(out, a, f, rd, wr, scale=None, bias=None):
+    def tt(out, a, b, o):
+        both = 1 if "ps" in (a[1][0][0], b[1][0][0]) else 2
+        op("v", lambda: V.tensor_tensor(out[0], a[0], b[0], o), [a, b], [out], time(out, [a, b], both))
+
+    def ts(out, a, s1, o1, s2=None, o2=None):
+        more = () if o2 is None else (o2,)
+        op("v", lambda: V.tensor_scalar(out[0], a[0], ap(s1), ap(s2), o1, *more), [a, s1, s2], [out], time(out, [a]))
+
+    def cp(out, a):
+        op("v", lambda: V.tensor_copy(out[0], a[0]), [a], [out], time(out, [a]))
+
+    def scan(out, d0, d1, init, o0, o1):
+        op("v", lambda: V.tensor_tensor_scan(out[0], d0[0], d1[0], init, o0, o1), [d0, d1], [out], time(out, [d0, d1]))
+
+    def turn(out, a):
+        op("v", lambda: V.transpose(out[0], a[0]), [a], [out], time(out, [a]))
+
+    def ms(out, val):
+        op("v", lambda: V.memset(out[0], val), [], [out], time(out, [out]))
+
+    def act(out, a, f, scale=None, bias=None):
         kw = {}
         if scale is not None:
-            kw["scale"] = scale
+            kw["scale"] = ap(scale)
         if bias is not None:
-            kw["bias"] = bias
-        op("a", lambda: S.activation(out, a, f, **kw), rd, wr)
+            kw["bias"] = ap(bias)
+        op("a", lambda: S.activation(out[0], a[0], f, **kw), [a, scale, bias], [out],
+           65 + 1.5 * CYCLE * out[2] if a[4] else max(64, out[2]) * CYCLE)
 
-    def quant(name, a, b, src, rd, wr):
-        op("v", lambda: V.quantize_mx(T["q" + name][:, a:b], T["s" + name + "_"][:, a:b], src), rd, wr)
+    codes = lambda n, a=0, b=None: w("q" + n, a, b)
+    scales = lambda n, a=0, b=None: w("s" + n + "_", a, b)
 
-    def bank(k, n=C):
-        return T.ps[:, 512 * k:512 * k + n]
+    def quant(name, a, b, src):
+        q, s = codes(name, a, b), scales(name, a, b)
+        op("v", lambda: V.quantize_mx(q[0], s[0], src[0]), [src], [q, s], 12 + 0.22 * src[2])
 
-    def mm(k, ln, la, rn, a, b, rd, start=True, stop=True):
-        op("p", lambda: P.matmul_mx(bank(k, b - a), T["q" + ln][:, la:la + 128], T["s" + ln + "_"][:, la:la + 128],
-                                    T["q" + rn][:, a:b], T["s" + rn + "_"][:, a:b], start, stop),
-           rd, "ps%d" % k, None if start else "acc")
+    def bank(k, n=C, a=0):
+        return w("ps", 512 * k + a, 512 * k + a + n)
 
-    def iota(out, pat, base, cm, wr):
-        op("g", lambda: g.iota(out, pat, base, cm, allow_small_or_imprecise_dtypes=True), "", wr)
+    def mm(k, ln, la, rn, a, b, start=True, stop=True):
+        ins = [codes(ln, la, la + 128), scales(ln, la, la + 128), codes(rn, a, b), scales(rn, a, b)]
+        out = bank(k, b - a)
+        op("p", lambda: P.matmul_mx(out[0], ins[0][0], ins[1][0], ins[2][0], ins[3][0], start, stop), ins, [out],
+           (b - a + 16) * CYCLE, None if start else "acc")
 
-    def pick(out, src, pat, cmp, fill, base, cm, rd, wr):
-        op("g", lambda: g.affine_select(out, src, pat, cmp, fill, base, cm), rd, wr)
+    def iota(out, pat, base, cm=0):
+        op("g", lambda: g.iota(out[0], pat, base, cm, allow_small_or_imprecise_dtypes=True), [], [out], 130 + 2 * CYCLE * out[2])
 
-    def dma(e, out, src, rd, wr):
+    def pick(out, src, pat, cmp, fill, base, cm):
+        op("g", lambda: g.affine_select(out[0], src[0], pat, cmp, fill, base, cm), [src], [out], 170 + 2 * CYCLE * out[2])
+
+    stored = []
+
+    def dma(e, out, src, rd, wr, nbytes):
         q = g.sync if e == "s" else g.scalar
-        op(e, lambda: q.dma_start(out, src), rd, wr, "dma")
+        if not wr:
+            wr = [("store%d" % len(stored), 1)]
+            stored.extend(wr)
+        op(e, lambda: q.dma_start(out, src), rd, wr, DMA + nbytes / RATE, "dma")
 
-    def send(dst, src, there, here, total, rd, wr):
-        op("g", lambda: g.remote_dma(dst, src, T.sem[there], T.sem[here], pid, rid, mask), rd, wr, (here, total))
+    def send(parts, there, here):
+        for n, (dst, src, raw) in enumerate(parts):
+            a, b = (dst[0].bitcast(dt.uint8), src[0].bitcast(dt.uint8)) if raw else (dst[0], src[0])
+            op("g", lambda a=a, b=b: g.remote_dma(a, b, T.sem[there], T.sem[here], pid, rid, mask),
+               [p[1] for p in parts], [(here, 1 << n)], DMA + 128 * src[2] * src[3] / RATE, (here, len(parts) * nout))
+        stored.append((here, 1 << len(parts) - 1))
+        op("x", None, [(here, (1 << len(parts)) - 1)], [p[0] for p in parts], 0.0, (there, len(parts) * nin))
 
-    def rev(t, a, n=C):
-        return t[:, a + n - 1:(a - 1 if a else None):-1]
-
-    def rbank(k):
-        return rev(T.ps, 512 * k)
-
-    col = lambda j: T.col[:, j:j + 1]
-    R_, NR, R15, H1, H2, NB, N8, PAR, RH, M15, NM15, P8 = range(12)
+    col = lambda j: w("col", j, j + 1)
+    R_, NR, R15, H1, H2, NB, N4, PAR, RH, M15, NM15, MM15, RN4, N4A = range(14)
     MRB, MLW, MLB, BMB = 16, 464, 480, 937
     CL, CR, TL, TR = 0, 28, 56, 84
     O_L2, O_LR, O_W, O_AT, O_O = 0, 56, 112, 168, 200
-    VR, VL, CN, CP = 512, 640, 768, 896
-    HALF = C // 2
-    tab = lambda a, n=56: T.tab[:, a:a + n]
-    wk = lambda j, a=0, n=56: T.wk[:, 64 * j + a:64 * j + n]
-    plane = lambda t, b, a=0, n=C: t[:, C * b + a:C * b + n]
+    VR, VL, C4, C5 = 512, 640, 768, 896
+    HALF, WORDS, SPLIT, STEP, ODD = C // 2, C // 4, 256, 8192.0, 512
+    tab = lambda a, n=56: w("tab", a, a + n)
+    wk = lambda j, a=0, n=56: w("wk", 64 * j + a, 64 * j + n)
+    plane = lambda t, b, a=0, n=C: w(t, C * b + a, C * b + n)
+    lu = lambda a: w("lu", a, a + 28)
+    TK, TE = 168, 200
 
-    def blocks(k, a, b, tag):
-        n, src = b - a, "ps%d " % k
-        tt(T.sm[:, a:b], bank(k, n), T.msk[:, 16 + a:16 + b], A.mult, src + "msk", "sm" + tag)
-        scan(rev(T.win, MLB + a, n), rev(T.ps, 512 * k, n), rev(T.kml, a, n), -HUGE, A.max, A.subtract, src + "kml", "ml" + tag)
-        scan(T.sw[:, a:b], T.k16[:, a:b], T.sm[:, a:b], 0.0, A.mult, A.add, "k16 sm" + tag, "sw" + tag)
-        scan(T.win[:, MRB + a:MRB + b], bank(k, n), T.kmr[:, a:b], -HUGE, A.max, A.subtract, src + "kmr", "mr" + tag)
+    def blocks(k, a, b):
+        n = b - a
+        tt(w("sm", a, b), bank(k, n), w("msk", 16 + a, 16 + b), A.mult)
+        scan(rev("win", MLB + a, n), rev("ps", 512 * k, n), rev("kml", a, n), -HUGE, A.max, A.subtract)
+        scan(w("sw", a, b), w("k16", a, b), w("sm", a, b), 0.0, A.mult, A.add)
+        scan(w("win", MRB + a, MRB + b), bank(k, n), w("kmr", a, b), -HUGE, A.max, A.subtract)
 
-    dma("a", T.ut[:], T.u[:], "", "ut")
-    dma("s", T.x0[:, 0:896], T.x[:, 0:896], "", "x0a")
-    dma("s", T.x0[:, 896:], T.x[:, 896:], "", "x0b")
+    dma("a", T.ut[:], T.u[:], [], [w("ut")], 128 * 1024)
+    dma("s", T.x0[:, 0:896], T.x[:, 0:896], [], [w("x0", 0, 896), ("turn", 1)], 128 * 2816)
+    dma("s", T.x0[:, 896:], T.x[:, 896:], [], [w("x0", 896), ("turn", 1)], 128 * 4608)
+    dma("s", T.qw[:].bitcast(dt.uint8), T.wc[:], [w("x0")], [codes("w")], 128 * 2048)
+    dma("s", T["sw_"][:], T.ws[:], [w("x0")], [scales("w")], 128 * 2560)
+    dma("s", T.vt[:], T.v[:], [w("x0")], [w("vt")], 128 * 3584)
 
-    op("g", lambda: g.iota(T.pi[:, 0:1], [[0, 1]], 0, 1), "", "pi0")
-    iota(T.tab[:, 320:336], [[1, 2], [16, 8]], 0, 0, "upl")
-    iota(T.i16[:], [[0, 29], [1, 16]], 0, 0, "i16")
-    iota(tab(0), [[0, 28], [16, 2]], 1, 0, "c0")
-    iota(tab(56, 28), [[-1, 14], [0, 2]], 15, 0, "ta")
-    iota(tab(84, 28), [[1, 14], [0, 2]], 2, 0, "tb_")
-    iota(T.dgi[:], [[1, 528]], 0, -4, "dgi")
-    iota(tab(168), [[2, 2], [16, 28]], 15, 0, "ck")
-    iota(tab(224, 28), [[16, 28]], 16, 0, "ck1")
-    iota(T.blk[:], [[0, 128]], 1, 0, "blk")
-    pick(T.blk[:], T.blk[:], [[-16, 8], [0, 16]], A.is_ge, 0.0, 0, 1, "blk", "blk")
-    pick(T.blk[:], T.blk[:], [[16, 8], [0, 16]], A.is_ge, 0.0, 15, -1, "blk", "blk")
-    iota(T.kl[:, 0:C], [[0, C]], -16, 0, "kll")
-    iota(T.kl[:, C:], [[0, C]], 16, 0, "klr")
-    iota(T.t1[:, 3::4], [[0, C]], 0, 0, "t13")
+    op("g", lambda: g.iota(T.pi[:, 0:1], [[0, 1]], 0, 1), [], [w("pi", 0, 1)], 130)
+    ts(w("pi", 1, 2), w("pi", 0, 1), 15, A.bitwise_and)
+    cp(col(R_), w("pi", 1, 2))
+    for c_, sc, bi in ((H1, -HUGE, HUGE), (H2, HUGE, HUGE), (NR, -1.0, 0.0), (R15, -1.0, 15.0), (RH, -1.0, 1.5)):
+        act(col(c_), col(R_), F.Identity, sc, bi)
+    for c_, sc in ((M15, 1.0), (NM15, -1.0)):
+        act(col(c_), col(R15), F.Sign, sc)
+    act(col(MM15), col(M15), F.Copy, MID)
+    act(col(NB), col(M15), F.Identity, -512.0, MID)
+    iota(tab(320, 16), [[1, 2], [16, 8]], 0)
+    cp(w("upk"), tab(320, 16))
+    quant("u", 0, 128, w("ut"))
+    words = by(codes("u"), w("upk"), True)
+    op("v", lambda: V.tensor_copy(T.qp[:, 0:256].bitcast(dt.uint32), words[0]), [words], [codes("p")], time(codes("p"), [words]))
+    act(scales("p"), by(scales("u"), w("upk")), F.Copy)
+    quant("v", 0, 128, w("vt"))
+    iota(w("i16"), [[0, 29], [1, 16]], 0)
+    ts(w("msk"), w("i16"), col(R_), A.is_equal)
+    act(w("k16"), w("i16", 0, C), F.Sign)
+    act(w("kml"), w("i16", 0, C), F.Relu, HUGE, col(H1))
+    act(w("kmr"), w("i16", 0, C), F.Relu, -HUGE, col(H2))
+    for j in range(9):
+        ms(w("tz", 2 ** j, None, 2 ** (j + 1)), float(j))
+    ms(w("tz", 0, 1), 15.0)
+    act(w("klev"), w("tz"), F.Relu, HUGE, col(H1))
+    act(w("k01"), w("klev"), F.Relu, -2.0 / HUGE, 1.0)
+    act(w("kc"), w("k01"), F.Identity, 2.0, -1.0)
+    act(w("kc2"), w("k01"), F.Identity, 512.0 + MID, -MID)
+    for a, b, val in ((0, 15, HUGE), (464, 480, HUGE), (929, 968, HUGE)):
+        ms(w("win", a, b), val)
+    for a in (15, 928):
+        act(w("win", a, a + 1), w("msk", 16, 17), F.Identity, -2 * HUGE, HUGE)
+    ms(w("smr", 448), -HUGE)
+    ms(w("sml", 0, 8), -HUGE)
+    iota(tab(0), [[0, 28], [16, 2]], 1)
+    iota(tab(56, 28), [[-1, 14], [0, 2]], 15)
+    iota(tab(84, 28), [[1, 14], [0, 2]], 2)
+    act(wk(0), tab(0), F.Identity, 1.0, col(R_))
+    act(tab(112), tab(56), F.Identity, -2.0, 31.0)
+    tt(wk(1), wk(0), tab(56), A.is_gt)
+    tt(wk(2), wk(1), tab(112), A.mult)
+    tt(wk(3), wk(1), tab(56), A.mult)
+    tt(wk(4), wk(2), tab(56), A.add)
+    tt(wk(5), wk(0), wk(3), A.subtract)
+    ts(lu(TL), wk(4, 0, 28), 16.0, A.mult, -17.0, A.add)
+    ts(lu(TR), wk(4, 28), -16.0, A.mult, 479.0, A.add)
+    tt(wk(6), wk(5), wk(4), A.is_equal)
+    act(wk(7, 0, 28), wk(4, 0, 28), F.Identity, 15.0, float(MLB - BMB - 30))
+    act(wk(7, 28), wk(4, 28), F.Identity, -15.0, float(466 - BMB))
+    act(wk(8, 0, 28), wk(5, 0, 28), F.Identity, 1.0, float(BMB - 2))
+    act(wk(8, 28), wk(5, 28), F.Identity, -1.0, float(BMB + 29))
+    tt(wk(9), wk(6), wk(7), A.mult)
+    tt(wk(2), wk(9), wk(8), A.add)
+    cp(w("lu", 0, 56), wk(2))
+    iota(tab(TK, 28), [[16, 28]], 0)
+    act(tab(TK, 28), tab(TK, 28), F.Identity, 1.0, col(R_))
+    iota(w("kl", 0, C), [[0, C]], -16)
+    iota(w("kl", C), [[0, C]], 16)
+    for a, s, c_, down, bi in ((14, 31, NR, True, -225.0), (30, 32, NR, False, -1.0), (449, 33, R15, True, 1.0), (478, 32, R15, False, -223.0)):
+        act(w("kl", a - 1, a + 13 * s, s), tab(TK, 14), F.Identity, 0.0, col(c_))
+        act(w("kl", a, a + 13 * s + 1, s), rev("tab", TK, 14) if down else tab(TK, 14), F.Identity, 1.0, bi)
+    iota(w("dgi"), [[1, 528]], 0, -4)
+    act(w("dga"), w("dgi"), F.Abs, 1.0, -3.0)
+    act(w("dg"), w("dga"), F.Relu, -1.0, 1.0)
+    for b in range(4):
+        quant("c", 128 * b, 128 * b + 128, w("dg", 3 - b, 515 - b))
+    pick(w("dv"), w("dg", 0, 520), [[1, 520]], A.not_equal, -1.0, 1, -4)
+    iota(w("dv", 63, None, 64), [[0, 8]], 0)
+    pick(w("dv", 64, None, 64), w("dv", 64, None, 64), [[-16, 8]], A.not_equal, 2.0, -15, 1)
+    quant("c", VR, VR + 128, w("dv", 1, 513))
+    quant("c", VL, VL + 128, w("dv", 3, 515))
+    iota(w("blk", 0, 32), [[16, 8], [0, 4]], 0, -1)
+    act(w("blk", 0, 32), w("blk", 0, 32), F.Abs, 1.0, 7.5)
+    ts(w("blk", 32), w("blk", 0, 32), 8.0, A.is_lt)
+    iota(w("c4"), [[0, 512]], 0)
+    for b in range(4):
+        act(w("c4", 5 * b, None, 16), w("blk", 32), F.Copy)
+    act(w("c5"), w("c4"), F.Copy, float(ODD))
+    quant("c", C4, C4 + 128, w("c4"))
+    quant("c", C5, C5 + 128, w("c5"))
+    act(w("k4a", 0, 116), w("i16", 0, 464, 4), F.Abs, 1.0, col(RH))
+    act(w("k4a", 0, 116), w("k4a", 0, 116), F.Relu, -1.0, 2.5)
+    act(w("kd4", 0, 116), w("k4a", 0, 116), F.Identity, -8 * STEP, STEP)
+    for h in range(2):
+        act(w("kd", WORDS * h, WORDS * h + WORDS), w("kd4", 1, WORDS + 1), F.Copy)
+    ts(w("pi", 3, 4), w("pi", 1, 2), 2, A.arith_shift_right)
+    ts(col(N4A), w("pi", 3, 4), STEP, A.mult, -3 * STEP, A.add)
+    tt(col(N4), col(N4A), w("kd4", 0, 1), A.subtract)
+    tt(col(RN4), col(R_), col(N4), A.subtract)
+    iota(tab(TE), [[1, 2], [16, 28]], 16)
+    act(tab(TE), tab(TE), F.Identity, 1.0, col(RN4))
+    act(w("ka"), w("msk"), F.Copy, 512.0)
+    act(w("kb"), w("msk"), F.Copy, 1024.0)
+    tt(w("kdb"), w("ka", 15, 463), w("kb", 16, 464), A.subtract)
+    ts(w("pi", 2, 3), w("pi", 0, 1), 4, A.arith_shift_right, 1, A.bitwise_and)
+    ts(col(PAR), w("pi", 2, 3), -1.0, A.add)
+    iota(w("b32"), [[0, 15], [1, 2], [0, 16]], 0)
+    act(w("ks"), w("b32"), F.Abs, 1.0, col(PAR))
+    iota(w("t1", 3, None, 4), [[0, C]], 0)
+    iota(w("tb", C, 512), [[0, 64]], 0)
+    iota(w("tb", 512 + C), [[0, 64]], 0)
+    for n, a, v in (("c1r", 17, 2), ("c2r", 17, -224), ("c1l", 16, -1), ("c2l", 16, -224), ("hh", 16, 0)):
+        iota(w(n, 0, a), [[0, a]], v)
+        iota(w(n, a + C), [[0, 32 - a]], v)
+    iota(w("iw", 0, ODD), [[0, ODD]], 0)
+    iota(w("iw", ODD), [[1, 464]], 0)
+    iota(w("rb"), [[1, C]], -224)
+    for b in range(4):
+        act(plane("x64", b), w("x0", b, None, 4), F.Copy, 64.0)
+    quant("x", 0, HALF, w("x0", 0, 896))
+    mm(3, "p", 0, "x", 0, HALF)
+    quant("x", HALF, C, w("x0", 896))
 
-    ms(T.tz[:], 0.0, "tz")
-    ms(T.k16[:], 1.0, "k16")
-    ts(T.pi[:, 1:2], T.pi[:, 0:1], 15, A.bitwise_and, "pi0", "pi1")
-    fill = [lambda: cp(col(R_), T.pi[:, 1:2], "pi1", "r"), lambda: ms(T.k16[:, 0::16], 0.0, "k16"),
-            lambda: cp(T.upk[:], T.tab[:, 320:336], "upl", "upk"), lambda: ms(T.win[:, 0:15], HUGE, "wino"),
-            lambda: ms(T.win[:, 464:480], HUGE, "winp"), lambda: ms(T.win[:, 929:968], HUGE, "winq"),
-            lambda: ms(T.smr[:, 448:456], -HUGE, "smrp"), lambda: ms(T.sml[:, 0:8], -HUGE, "smlp")]
-    for j in range(1, 9):
-        ms(T.tz[:, 0::2 ** j], float(j), "tz")
-        fill[j - 1]()
-    ms(T.tz[:, 0:1], 15.0, "tz")
-    ts(T.msk[:], T.i16[:], col(R_), A.is_equal, "i16 r", "msk")
-    act(col(H1), col(R_), F.Identity, "r", "h1", -HUGE, HUGE)
-    act(col(H2), col(R_), F.Identity, "r", "h2", HUGE, HUGE)
-    act(T.kml[:], T.i16[:, 0:C], F.Relu, "i16 h1", "kml", HUGE, col(H1))
-    act(T.kmr[:], T.i16[:, 0:C], F.Relu, "i16 h2", "kmr", -HUGE, col(H2))
-    act(wk(0), tab(0), F.Identity, "c0 r", "w0", 1.0, col(R_))
-    act(tab(112), tab(56), F.Identity, "ta tb_", "tc", -2.0, 31.0)
-    quant("u", 0, 128, T.ut[:], "ut", "qu")
-    tt(wk(1), wk(0), tab(56), A.is_gt, "w0 ta tb_", "w1")
-    op("v", lambda: V.tensor_copy(T.qp[:, 0:256].bitcast(dt.uint32), T.qu[:, 0:128].bitcast(dt.uint32).indirect(T.upk[:, 0:16])),
-       "qu upk", "qp")
-    act(T["sp_"][:, 0:256], T["su_"][:, 0:128].indirect(T.upk[:, 0:16]), F.Copy, "qu upk", "sp")
-    act(T.klev[:], T.tz[:], F.Relu, "tz h1", "klev", HUGE, col(H1))
-    tt(wk(2), wk(1), tab(112), A.mult, "w1 tc", "w2")
-    tt(wk(3), wk(1), tab(56), A.mult, "w1", "w3")
-    quant("x", 0, HALF, T.x0[:, 0:896], "x0a", "qxa")
-    mm(3, "p", 0, "x", 0, HALF, "qp sp qxa")
-    tt(wk(4), wk(2), tab(56), A.add, "w2", "w4")
-    tt(wk(5), wk(0), wk(3), A.subtract, "w0 w3", "w5")
-    ts(T.lu[:, TL:TL + 28], wk(4, 0, 28), 16.0, A.mult, "w4", "ltl", -17.0, A.add)
-    blocks(3, 0, HALF, "a")
-    quant("x", HALF, C, T.x0[:, 896:], "x0b", "qxb")
-    ts(T.lu[:, TR:TR + 28], wk(4, 28), -16.0, A.mult, "w4", "ltr", 479.0, A.add)
-    tt(wk(6), wk(5), wk(4), A.is_equal, "w5 w4", "w6")
-    act(wk(7, 0, 28), wk(4, 0, 28), F.Identity, "w4", "w7a", 15.0, float(MLB - BMB - 30))
-    act(wk(7, 28), wk(4, 28), F.Identity, "w4", "w7b", -15.0, float(466 - BMB))
-    act(wk(1, 0, 28), wk(5, 0, 28), F.Identity, "w5", "w1a w1", 1.0, float(BMB - 2))
-    act(wk(1, 28), wk(5, 28), F.Identity, "w5 w1", "w1b", -1.0, float(BMB + 29))
-    dma("s", T.qw[:].bitcast(dt.uint8), T.wc[:], "x0a x0b", "qw")
-    dma("s", T["sw_"][:], T.ws[:], "", "sw_")
-    dma("s", T.vt[:], T.v[:], "", "vt")
-    act(T.win[:, 15:16], T.msk[:, 16:17], F.Identity, "msk", "winr", -2 * HUGE, HUGE)
-    act(T.win[:, 928:929], T.msk[:, 16:17], F.Identity, "msk", "wins", -2 * HUGE, HUGE)
-    act(T.dga[:], T.dgi[:], F.Abs, "dgi", "dga", 1.0, -3.0)
-
-    def setup_0():
-        act(T.dg[:], T.dga[:], F.Relu, "dga", "dg", -1.0, 1.0)
-        pick(T.dv[:], T.dg[:, 0:520], [[1, 520]], A.not_equal, -1.0, 1, -4, "dg", "dv")
-        iota(T.dv[:, 63::64], [[0, 8]], 0, 0, "dv")
-        pick(T.dv[:, 64::64], T.dv[:, 64::64], [[-16, 8]], A.not_equal, 2.0, -15, 1, "dv", "dv")
-        for n, v in (("c1r", 2), ("c2r", 0)):
-            iota(T[n][:, 0:17], [[0, 17]], v, 0, n + "p")
-            iota(T[n][:, 465:480], [[0, 15]], v, 0, n + "q")
-        for n, v in (("c1l", -1), ("c2l", 0), ("hh", 0)):
-            iota(T[n][:, 0:16], [[0, 16]], v, 0, n + "p")
-            iota(T[n][:, 464:480], [[0, 16]], v, 0, n + "q")
-        iota(T.iw[:], [[1, 464]], 0, 0, "iw")
-        iota(T.b32[:], [[0, 15], [1, 2], [0, 16]], 0, 0, "b32")
-        act(col(NR), col(R_), F.Copy, "r", "nr_", -1.0)
-        act(col(R15), col(R_), F.Identity, "r", "r15", -1.0, 15.0)
-        act(col(RH), col(R_), F.Identity, "r", "rh", -1.0, 0.5)
-        tt(wk(6), wk(6), wk(7), A.mult, "w6 w7a w7b", "w6")
-
-    def unit(b):
-        quant("c", 128 * b, 128 * b + 128, T.dg[:, 3 - b:515 - b], "dg", "e%d" % b)
-
-    def setup_1():
-        unit(0)
-        tt(wk(6), wk(6), wk(1), A.add, "w6 w1a w1b", "w6")
-        unit(1)
-        cp(T.lu[:, 0:56], wk(6), "w6", "lu")
-        unit(2)
-        act(T.k01[:], T.klev[:], F.Relu, "klev", "k01", -2.0 / HUGE, 1.0)
-        for view, c_, key in ((T.kl[:, 14:418:31], NR, "kll"), (T.kl[:, 449::33], R15, "klr"),
-                              (T.kl[:, 30:C:32], NR, "kll"), (T.kl[:, 478::32], R15, "klr")):
-            act(view, T.i16[:, 0:14], F.Identity, "i16 nr_ r15", key, 0.0, col(c_))
-        act(tab(168, 84), tab(168, 84), F.Identity, "ck ck1 r", "ck ck1", 1.0, col(R_))
-        act(T.kc[:], T.k01[:], F.Identity, "k01", "kc", 2.0, -1.0)
-
-    def setup_a():
-        ts(T.pi[:, 3:4], T.pi[:, 1:2], 1, A.arith_shift_right, "pi1", "pi3")
-        quant("c", VR, VR + 128, T.dv[:, 1:513], "dv", "cvr")
-        ts(col(N8), T.pi[:, 3:4], 1024.0, A.mult, "pi3", "n8", -7168.0, A.add)
-        quant("c", VL, VL + 128, T.dv[:, 3:515], "dv", "cvl")
-        act(T.cn[:], T.dg[:, 0:520], F.Copy, "dg", "cnz", 0.0)
-        act(T.k8a[:], T.i16[:, 0:C:2], F.Abs, "i16 rh", "k8a", 1.0, col(RH))
-        act(T.cn[:, 1:513:8], T.blk[:, 0::2], F.Copy, "blk cnz", "cn0")
-        act(T.cn[:, 7:513:8], T.blk[:, 1::2], F.Copy, "blk cnz", "cn1")
-        act(T.k8a[:], T.k8a[:], F.Relu, "k8a", "k8a", -1.0, 1.5)
-        act(col(M15), col(R15), F.Sign, "r15", "m15")
-        act(col(NM15), col(R15), F.Sign, "r15", "nm15", -1.0)
-        act(T.kd8[:], T.k8a[:], F.Identity, "k8a", "kd8", -16384.0, 1024.0)
-
-    def setup_b():
-        quant("c", CN, CN + 128, T.cn[:, 1:513], "cn0 cn1", "cn")
-        quant("c", CP, CP + 128, T.cn[:, 0:512], "cn0 cn1", "cp")
-
-    def setup_d():
-        ts(T.pi[:, 2:3], T.pi[:, 0:1], 4, A.arith_shift_right, "pi0", "pi2", 1, A.bitwise_and)
-
-    def setup_e():
-        ts(col(PAR), T.pi[:, 2:3], -1.0, A.add, "pi2", "par")
-        act(T.ks[:], T.b32[:], F.Abs, "b32 par", "ks", 1.0, col(PAR))
-        act(T.kdb[:], T.msk[:, 16:464], F.Identity, "msk", "kdb", -32768.0, 1024.0)
-        unit(3)
-
-    def setup_f():
-        quant("v", 0, 128, T.vt[:], "vt", "qv")
-
-    def planes():
-        act(col(P8), col(N8), F.Copy, "n8", "p8", -1.0)
-        act(col(NB), col(R15), F.Copy, "r15", "nb", -1024.0)
-        act(tab(256, 28), tab(224, 28), F.Identity, "ck1 p8", "ckd0", 1.0, col(P8))
-        act(tab(284, 28), tab(196, 28), F.Identity, "ck p8", "ckd1", 1.0, col(P8))
-        for b in range(4):
-            act(plane(T.x64, b), T.x0[:, b::4], F.Copy, "x0a x0b", "fa%d fb%d" % (b, b), 64.0)
-
-    sma = lambda a, n=56: T.sma[:, a:a + n]
-    ni = lambda a, n=56: T.ni[:, a:a + n]
-    DD, WW, OWN, AT, TT = 0, 64, 128, 160, 256
-    IX, B16, PI, SEL = 0, 56, 112, 168
-    off = lambda a, n=28: T.off[:, a:a + n]
-    WIN = "mra mrb mla mlb bm wino winp winq winr wins"
+    sma = lambda a, n=56: w("sma", a, a + n)
+    ni = lambda a, n=56: w("ni", a, a + n)
+    EE, OW, OWN, BASE, AT, BM = 0, 64, 128, 160, 192, 256
+    QQ, IX, SEL = 0, 56, 112
+    off = lambda a, n=28: w("off", a, a + n)
     RL, FL, RR = 0, 1, 2
-
-    def others():
-        act(T.nrr[:], T.t1[:, RR::4], F.Identity, "t1r", "nrr", -1.0, 1.0)
-        act(T.nrl[:], T.t1[:, RL::4], F.Identity, "t1l m15 nm15", "nrl", col(NM15), col(M15))
-
-    def fold8(k, h, key):
-        scan(T.nd[:, HALF * h:HALF * h + HALF], T.kd8[:], bank(k, HALF), 0.0, A.add, A.max, "kd8 ps%d" % k, key)
+    t1 = lambda b: w("t1", b, None, 4)
+    flags = lambda h: w("tb", 512 * h, 512 * h + C)
+    parts = ((0, SPLIT), (SPLIT, C))
 
     for rnd in range(ROUNDS):
         first, last = rnd == 0, rnd == ROUNDS - 1
         l_, n_ = "l%d" % rnd, str(rnd)
-        once = lambda fn: fn() if first else None
-        send(T["q" + l_][:].bitcast(dt.uint8), T.qx[:].bitcast(dt.uint8), "arr" + n_, "out" + n_, 2 * nout, "qxa qxb", "")
-        send(T["s" + l_ + "_"][:], T["sx_"][:], "arr" + n_, "out" + n_, 2 * nout, "qxa qxb", "sent" + n_)
-        op("x", None, "", l_, ("arr" + n_, 2 * nin))
+        send([(codes(l_), codes("x"), True), (scales(l_), scales("x"), False)], "arr" + n_, "out" + n_)
         a, b = (HALF, C) if first else (0, K)
-        mm(4, "p", 0, "x", a, b, "qp sp qxa qxb")
-        mm(0, "p", 0, "x", 0, C, "qp sp qxa qxb")
-        mm(2, "p", 128, "x", 0, C, "qp sp qxa qxb")
-        mm(1, "p", 0, "x", 0, C, "qp sp qxa qxb")
-        once(setup_0)
-        if not first:
-            blocks(3, K, C, "a")
-        blocks(4, a, b, "b")
-        act(T.sg[:], bank(2), F.Sign, "ps2", "sg")
-        act(T.thr[:, 0:C], T.sw[:].indirect(T.lu[:, TL:TL + 28]), F.Copy, "swa swb ltl", "thl")
-        act(T.thr[:, C:2 * C], T.sw[:].indirect(T.lu[:, TR:TR + 28]), F.Copy, "swa swb ltr", "thr")
-        act(T.t1[:, FL::4], T.sg[:], F.Relu, "sg", "t1f")
-        scan(rev(T.smr, 0), rbank(0), rev(T.klev, 0), -HUGE, A.max, A.subtract, "ps0 klev", "smr")
-        tt(sma(224, 28), T.win[:, MLB:MLB + C:16], T.win[:, 31:464:16], A.max, "mla mlb mra mrb", "bm0")
-        scan(T.sml[:, 8:456], bank(0), T.klev[:, 1:449], -HUGE, A.max, A.subtract, "ps0 klev", "sml")
-        tt(T.win[:, BMB:BMB + 28], sma(224, 28), T.sw[:, 15::16], A.max, "bm0 swa swb winq", "bm")
-        once(setup_1)
-        act(T.ssb[:], bank(1), F.Copy, "ps1", "ssb")
-        tt(T.t1[:, RR::4], bank(0), T.smr[:, 1:449], A.is_ge, "ps0 smr smrp", "t1r")
-        tt(T.nf[:, 0:C], T.win[:, 0:968].indirect(T.lu[:, CL:CL + 28]), T.thr[:, 0:C], A.is_lt, WIN + " lu thl", "nfl")
-        tt(T.t1[:, RL::4], bank(0), T.sml[:, 7:455], A.is_gt, "ps0 sml smlp", "t1l")
-        tt(T.nf[:, C:2 * C], T.win[:, 0:968].indirect(T.lu[:, CR:CR + 28]), T.thr[:, C:2 * C], A.is_le, WIN + " lu thr", "nfr")
-        once(setup_a)
-        quant("1", 0, C, T.t1[:], "t1l t1f t1r t13", "q1")
-        if not first:
-            others()
-        scan(T.run[:], T.kl[:], T.nf[:], 0.0, A.add, A.mult, "kll klr nfl nfr", "run")
-        mm(3, "c", 128 * FL, "1", 0, C, "e1 q1", True, False)
-        mm(3, "c", 128 * RL, "1", 0, C, "e0 q1", False, True)
-        mm(4, "c", 128 * FL, "1", 0, C, "e1 q1", True, False)
-        mm(4, "c", 128 * RR, "1", 0, C, "e2 q1", False, True)
-        mm(5, "c", VR, "1", 0, C, "cvr q1")
-        mm(6, "c", VL, "1", 0, C, "cvl q1")
-        mm(7, "c", 128 * RR, "1", 0, C, "e2 q1")
-        tt(ni(IX + 14, 28), T.run[:, 30::32], tab(182, 28), A.add, "run ck", "ixb")
-        tt(ni(IX, 14), T.run[:, 417:13:-31], tab(168, 14), A.add, "run ck", "ixa")
-        tt(ni(IX + 42, 14), T.run[:, 878:448:-33], tab(210, 14), A.add, "run ck", "ixc")
-        once(setup_b)
-        cp(off(O_L2, 56), ni(IX), "ixa ixb ixc", "ol2")
-        act(T.ga[:], T.win[:, 0:464].indirect(off(O_L2)), F.Copy, WIN + " ol2", "ga")
-        ts(ni(B16), ni(IX), 0xFFF0, A.bitwise_and, "ixa ixb ixc", "b16")
-        act(T.v1r[:], bank(3), F.Sign, "ps3", "v1r", -1.0, 1.5)
-        act(T.v1l[:], bank(4), F.Sign, "ps4", "v1l", -1.0, 1.5)
-        act(T.vr[:], bank(5), F.Copy, "ps5", "vr")
-        once(others)
-        tt(T.tb[:, 1::2], T.win[:, MLW:936].indirect(off(O_L2 + 28)), T.ssb[:], A.is_le, WIN + " ol2 ssb", "tb1")
-        tt(T.tb[:, 0::2], T.ga[:], bank(0), A.is_ge, "ga ps0", "tb0")
-        quant("b", 0, HALF, T.tb[:], "tb0 tb1", "qb")
-        mm(1, "c", CN, "b", 0, HALF, "cn qb")
-        mm(2, "c", CP, "b", 0, HALF, "cp qb")
-        scan(rev(T.c1r, 17), rev(T.kc, 1), rev(T.v1r, 0), -1.0, A.min, A.mult, "kc v1r", "c1r")
-        scan(T.c1l[:, 16:464], T.kc[:, 0:C], T.v1l[:], -1.0, A.min, A.mult, "kc v1l", "c1l")
-        fold8(1, 0, "nd")
-        fold8(2, 1, "nd1")
-        tt(sma(TT, 28), T.nd[:, 7:HALF:8], ni(B16, 28), A.add, "nd b16", "tl")
-        tt(sma(TT + 28, 28), T.nd[:, HALF + 7::8], ni(B16 + 28, 28), A.add, "nd1 b16", "tr")
-        once(setup_d)
-        ts(off(O_LR, 56), sma(TT), col(N8), A.add, "tl tr n8", "olr")
-        act(T.g1l[:], T.c1l[:].indirect(off(O_LR)), F.Identity, "c1l c1lp c1lq olr", "g1l", -0.5, 1.5)
-        tt(T.b1r[:], T.c1r[:].indirect(off(O_LR + 28)), T.vr[:], A.is_equal, "c1r c1rp c1rq olr vr", "b1r")
-        scan(T.tb[:, 2 * C - 2::-2], rev(T.nrr, 0), rev(T.b1r, 0), 0.0, A.mult, A.add, "nrr b1r", "tb0")
-        tt(T.b1l[:], T.g1l[:], bank(6), A.is_le, "g1l ps6", "b1l")
-        once(planes)
-        tt(sma(DD, 28), tab(256, 28), sma(TT, 28), A.subtract, "tl ckd0", "dl")
-        scan(T.tb[:, 1::2], T.nrl[:], T.b1l[:], 0.0, A.mult, A.add, "nrl b1l", "tb1")
-        quant("b", 0, HALF, T.tb[:], "tb0 tb1", "qb")
-        mm(1, "c", CN, "b", 0, HALF, "cn qb", True, False)
-        mm(1, "c", CP, "b", 0, HALF, "cp qb", False, True)
-        tt(sma(DD + 28, 28), sma(TT + 28, 28), tab(284, 28), A.subtract, "tr ckd1", "dr")
-        once(setup_e)
-        fold8(1, 0, "nd")
-        DB = (3, 4, 0, 1)
+        mm(4, "p", 0, "x", a, b)
+        mm(0, "p", 0, "x", 0, C)
+        mm(2, "p", 128, "x", 0, C)
+        blocks(3, *((0, HALF) if first else (K, C)))
+        blocks(4, a, b)
+        act(t1(FL), bank(2), F.Sign)
+        act(w("thr", 0, C), by(w("sw"), lu(TL)), F.Copy)
+        act(w("thr", C), by(w("sw"), lu(TR)), F.Copy)
+        scan(rev("smr", 0), rev("ps", 0), rev("klev", 0), -HUGE, A.max, A.subtract)
+        scan(w("sml", 8), bank(0), w("klev", 1, 449), -HUGE, A.max, A.subtract)
+        tt(sma(BM, 28), w("win", MLB, MLB + C, 16), w("win", 31, 464, 16), A.max)
+        tt(w("win", BMB, BMB + 28), sma(BM, 28), w("sw", 15, None, 16), A.max)
+        tt(t1(RR), bank(0), w("smr", 1, 449), A.is_ge)
+        tt(t1(RL), bank(0), w("sml", 7, 455), A.is_gt)
+        quant("1", 0, C, w("t1"))
+        act(w("nrr"), t1(RR), F.Identity, -1.0, 1.0)
+        act(w("nrl"), t1(RL), F.Identity, col(NM15), col(M15))
+        for k, e in ((3, RL), (4, RR)):
+            mm(k, "c", 128 * FL, "1", 0, C, True, False)
+            mm(k, "c", 128 * e, "1", 0, C, False, True)
+        mm(5, "c", VR, "1", 0, C)
+        mm(6, "c", VL, "1", 0, C)
+        mm(7, "c", 128 * RR, "1", 0, C)
+        act(w("v1r"), bank(3), F.Sign, -1.0, 1.5)
+        act(w("v1l"), bank(4), F.Sign, -1.0, 1.5)
+        act(w("vr"), bank(5), F.Copy)
+        scan(rev("c1r", 17), rev("kc", 1), rev("v1r", 0), -1.0, A.min, A.mult)
+        scan(w("c1l", 16, 464), w("kc", 0, C), w("v1l"), -1.0, A.min, A.mult)
+        for h, lst, cmp, ends in ((0, CL, A.is_lt, ((417, 13, -31), (30, C, 32))), (1, CR, A.is_le, ((478, None, 32), (878, C, -33)))):
+            tt(w("nf", C * h, C * h + C), by(w("win"), lu(lst)), w("thr", C * h, C * h + C), cmp)
+            scan(w("run", C * h, C * h + C), w("nf", C * h, C * h + C), w("kl", C * h, C * h + C), 0.0, A.mult, A.add)
+            for j in range(2):
+                ts(off(O_L2 + 28 * h + 14 * j, 14), w("run", *ends[j]), 240.0, A.add)
+        ts(ni(QQ), off(O_L2, 56), 1.0 / 16, A.mult, -0.46875, A.add)
+        ts(w("kd", 3, None, 4), ni(QQ), 16.0, A.mult, w("kd4", 0, 1), A.add)
+        for h, got, win, cmp in ((0, "ga", w("win", 0, 464), A.is_ge), (1, "gb", w("win", MLW, 936), A.is_le)):
+            act(w(got), by(win, off(O_L2 + 28 * h)), F.Copy)
+            tt(flags(h), w(got), bank(0), cmp)
+            quant("b", 128 * h, 128 * h + 128, w("tb", 512 * h, 512 * h + 512))
+            mm(1 + h, "c", C4, "b", 128 * h, 128 * h + 128)
+            nd = w("nd", WORDS * h, WORDS * h + WORDS)
+            scan(nd, bank(1 + h, WORDS), w("kd", WORDS * h, WORDS * h + WORDS), 0.0, A.max, A.add)
+            ts(off(O_LR + 28 * h), w("nd", WORDS * h + 3, WORDS * h + WORDS, 4), col(N4), A.add)
+        tt(sma(EE), w("nd", 3, HALF, 4), tab(TE), A.subtract)
+        left, right = off(O_LR), off(O_LR + 28)
+        act(w("g1l"), by(w("c1l"), left), F.Identity, -0.5, 1.5)
+        tt(w("b1r"), by(w("c1r"), right), w("vr"), A.is_equal)
+        scan(rev("tb", 512), rev("nrr", 0), rev("b1r", 0), 0.0, A.mult, A.add)
+        tt(w("b1l"), w("g1l"), bank(6), A.is_le)
+        scan(flags(0), w("nrl"), w("b1l"), 0.0, A.mult, A.add)
+        for h in (1, 0):
+            quant("b", 128 * h, 128 * h + 128, w("tb", 512 * h, 512 * h + 512))
+            mm(1, "c", C5, "b", 128 * h, 128 * h + 128, h == 1, h == 0)
+        scan(w("nd", HALF), w("kd4", 0, WORDS), bank(1, WORDS), 0.0, A.add, A.max)
+        DB = (3, 4, 0, 2)
         for b in range(4):
-            mm(DB[b], "c", 128 * b, l_, 0, C, "e%d %s" % (b, l_))
-        ts(ni(PI, 28), T.nd[:, 7:HALF:8], 1.0, A.add, "nd", "pa")
-        cp(ni(PI + 28, 28), T.nd[:, 7:HALF:8], "nd", "pb")
-        once(setup_f)
-        ts(ni(SEL), ni(PI), 1, A.bitwise_and, "pa pb", "sel")
-        tt(sma(WW), ni(SEL), sma(DD), A.mult, "sel dl dr", "ww")
-        cp(off(O_W, 56), sma(WW), "ww", "ow")
-        act(T.gw[:], T.iw[:].indirect(off(O_W)), F.Copy, "iw ow", "gw")
-        tt(T.w2r[:], T.iw[:].indirect(off(O_W + 28)), T.t1[:, RL::4], A.mult, "iw ow t1l", "w2r")
-        tt(sma(OWN, 28), sma(WW, 28), sma(WW + 28, 28), A.add, "ww", "own")
-        scan(rev(T.c2r, 17), rev(T.k01, 1), rev(T.w2r, 0), 0.0, A.mult, A.add, "k01 w2r", "c2r")
-        tt(T.w2l[:], T.gw[:], bank(7), A.mult, "gw ps7", "w2l")
-        act(T.ga[:], T.c2r[:].indirect(off(O_LR + 28)), F.Copy, "c2r c2rp c2rq olr", "ga")
-        scan(T.c2l[:, 16:464], T.k01[:, 0:C], T.w2l[:], 0.0, A.mult, A.add, "k01 w2l", "c2l")
-        act(T.gb[:], T.c2l[:].indirect(off(O_LR)), F.Copy, "c2l c2lp c2lq olr m15", "gb", col(M15))
-        tt(T.g2r[:], T.ga[:], bank(5), A.mult, "ga ps5", "g2r")
-        scan(rev(T.h2r, 0), rev(T.nrr, 0), rev(T.g2r, 0), 0.0, A.mult, A.add, "nrr g2r", "h2r")
-        tt(T.g2l[:], T.gb[:], bank(6), A.mult, "gb ps6", "g2l")
-        for b in range(4):
-            act(plane(T.dec, b), bank(DB[b]), F.Copy, "ps%d" % DB[b], "dec%d" % b)
-        scan(T.h2l[:], T.nrl[:], T.g2l[:], 0.0, A.mult, A.add, "nrl g2l", "h2l")
-        tt(T.hh[:, 16:464], T.h2r[:], T.h2l[:], A.add, "h2r h2l", "hh")
-        op("v", lambda: V.transpose(T.tt[:, 0:448], T.hh[:, 16:464]), "hh", "tta")
-        op("v", lambda: V.transpose(T.tt[:, 448:928], T.hh[:, 0:480]), "hh hhp hhq", "ttb")
-        scan(T.ts[:, 0:448], T.tt[:, 0:448], T.ks[:, 0:448], 0.0, A.add, A.mult, "ks tta", "tsa")
-        scan(T.ts[:, 448:928], T.tt[:, 448:928], T.ks[:], 0.0, A.add, A.mult, "ks ttb", "tsb")
-        tt(sma(AT, 28), T.ts[:, 15:448:16], sma(OWN, 28), A.add, "tsa own", "at0")
-        tt(sma(AT + 32, 28), T.ts[:, 479:927:16], sma(AT, 28), A.add, "tsb at0", "at")
-        ts(off(O_AT), sma(AT + 32, 28), -1.0, A.add, "at", "oat")
-        cp(T.ord[:].indirect(off(O_AT)), T.iw[:, 0:C], "oat iw", "ord")
-        scan(T.nd[:], T.kdb[:], T.ord[:], 0.0, A.add, A.max, "kdb ord", "nd nd1")
+            mm(DB[b], "c", 128 * b, l_, 0, C)
+            act(plane("dec", b), bank(DB[b]), F.Copy)
+        tt(ni(IX, 28), w("nd", HALF + 3, None, 4), sma(EE, 28), A.subtract)
+        tt(ni(IX + 28, 28), w("nd", HALF + 3, None, 4), sma(EE + 28, 28), A.add)
+        ts(ni(SEL), ni(IX), 2 * ODD - 1, A.bitwise_and)
+        cp(off(O_W, 56), ni(SEL))
+        ts(sma(OW), ni(SEL), -float(ODD), A.add, 0.0, A.max)
+        tt(sma(OWN, 28), sma(OW + 28, 28), sma(OW, 28), A.subtract)
+        tt(sma(BASE, 28), sma(OWN, 28), tab(TK, 28), A.add)
+        act(w("gw"), by(w("iw"), off(O_W)), F.Copy)
+        tt(w("w2r"), by(w("iw"), off(O_W + 28)), t1(RL), A.mult)
+        scan(rev("c2r", 17), rev("kc2", 1), rev("w2r", 0), -MID, A.min, A.add)
+        tt(w("w2l"), w("gw"), bank(7), A.mult)
+        scan(w("c2l", 16, 464), w("kc2", 0, C), w("w2l"), -MID, A.min, A.add)
+        act(w("ga"), by(w("c2r"), right), F.Identity, 1.0, MID)
+        act(w("gb"), by(w("c2l"), left), F.Identity, col(M15), col(MM15))
+        tt(w("g2r"), w("ga"), bank(5), A.mult)
+        scan(rev("h2r", 0), rev("nrr", 0), rev("g2r", 0), 0.0, A.mult, A.add)
+        for a, b in parts:
+            tt(w("g2l", a, b), w("gb", a, b), bank(6, b - a, a), A.mult)
+            scan(w("h2l", a, b), w("nrl", a, b), w("g2l", a, b), 0.0, A.mult, A.add)
+            tt(w("hh", 16 + a, 16 + b), w("h2r", a, b), w("h2l", a, b), A.subtract)
+        for src, dst, n in ((16, 0, SPLIT), (0, C, SPLIT), (16 + SPLIT, SPLIT, C - SPLIT), (SPLIT, C + SPLIT, 480 - SPLIT)):
+            turn(w("tt", dst, dst + n), w("hh", src, src + n))
+            scan(w("ts", dst, dst + n), w("tt", dst, dst + n), w("ks", 0, n), 0.0, A.add, A.mult)
+        tt(sma(AT, 28), w("ts", 15, C, 16), sma(BASE, 28), A.add)
+        tt(sma(AT + 32, 28), w("ts", 479, 927, 16), sma(AT, 28), A.add)
+        cp(off(O_AT), sma(AT + 32, 28))
+        cp(by(w("ord"), off(O_AT)), w("rb"))
         oo = O_O + 32 * rnd
-        ts(off(oo), T.nd[:, 15::16], col(NB), A.add, "nd nd1 nb", "oo")
-        send(T["came" + n_][:], off(oo + 20, 8), "larr" + n_, "lout" + n_, nout, "oo", "lsent" + n_)
-        op("x", None, "", "came" + n_, ("larr" + n_, nin))
+        scan(w("no"), w("kdb"), w("ord"), 0.0, A.add, A.max)
+        ts(off(oo), w("no", 15, None, 16), col(NB), A.add)
+        came = w("came" + n_)
+        send([(came, off(oo + 20, 8), False)], "larr" + n_, "lout" + n_)
         if last:
-            dma("s", T.ol[:], T.ord[0:128:16, :], "ord", "y_ol")
+            act(w("ordf"), w("ord"), F.Identity, 1.0, MID)
+            dma("s", T.ol[:], T.ordf[0:128:16, :], [w("ordf")], [], 8 * 1792)
 
-        def scale(e, out, src, by, rd, wr):
+        def scale(e, out, src, f):
             if e == "v":
-                ts(out, src, by, A.mult, rd, wr)
+                ts(out, src, f, A.mult)
             else:
-                act(out, src, F.Copy, rd, wr, by)
-        own, came = (lambda t, b: t[:, 4 * K + b::4]), (lambda t, b: t[:, b:4 * K:4])
-        for b, e in ((2, "a"), (0, "v"), (3, "a"), (1, "v")):
-            scale(e, own(T.z, b), plane(T.x64, b).indirect(off(oo, 20)), 1.0 / 64, "oo fa%d fb%d" % (b, b), "zb%d" % b)
-        scale("v", plane(T.z64, 0, K), own(T.z, 0), 64.0, "zb0", "sb0")
-        quant("z", K, C, T.z[:, 4 * K:], "zb0 zb1 zb2 zb3", "qzb")
-        for b in range(4):
-            mm(b, "w", 128 * b, "z", K, C, "qw sw_ qzb")
-
-        def step(name, b, e):
-            if name == "sb":
-                scale(e, plane(T.z64, b, K), own(T.z, b), 64.0, "zb%d" % b, "sb%d" % b)
-            elif name == "za":
-                scale(e, came(T.z, b), plane(T.dec, b).indirect(T["came" + n_][:]), 1.0, "dec%d came%s" % (b, n_), "za%d" % b)
-            elif name == "sa":
-                scale(e, plane(T.z64, b, 0, K), came(T.z, b), 64.0, "za%d" % b, "sa%d" % b)
-            elif name == "fb":
-                tt(plane(T.x64, b, K), bank(b, C - K), plane(T.z64, b, K), A.add, "ps%d sb%d" % (b, b), "fb%d" % b)
-            elif name == "fa":
-                tt(plane(T.x64, b, 0, K), bank(4 + b, K), plane(T.z64, b, 0, K), A.add, "ps%d sa%d" % (4 + b, b), "fa%d" % b)
-            elif name == "xb":
-                scale(e, own(T.xs, b), plane(T.x64, b, K), 1.0 / 64, "fb%d" % b, "xb%d" % b)
-            elif name == "xa":
-                scale(e, came(T.xs, b), plane(T.x64, b, 0, K), 1.0 / 64, "fa%d" % b, "xa%d" % b)
-            elif name == "qz":
-                quant("z", 0, K, T.z[:, 0:4 * K], "za0 za1 za2 za3", "qza")
-                for j in range(4):
-                    mm(4 + j, "w", 128 * j, "z", 0, K, "qw sw_ qza")
-            elif name == "qb":
-                quant("x", K, C, T.xs[:, 4 * K:], "xb0 xb1 xb2 xb3 sent" + n_, "qxb")
-                if last:
-                    mm(0, "v", 0, "x", K, C, "qv qxb")
-                    dma("s", T.oc[:, 4 * K:], T.qx[:, K:C].bitcast(dt.uint8), "qxb", "y_ocb")
+                act(out, src, F.Copy, f)
+        for a, n, eng in ((K, C, "vvaa vaaa aaav"), (0, K, "vvaa aaaa aavv")):
+            step = lambda t, b: w(t, 4 * a + b, 4 * n, 4)
+            pb = 0 if a else 4
+            for b in range(4):
+                if a:
+                    scale(eng[b], step("z", b), by(plane("x64", b), off(oo, 20)), 1.0 / 64)
                 else:
-                    mm(3, "p", 0, "x", K, C, "qp sp qxb")
-            elif name == "yb":
-                act(T.ysb[:, K:C], bank(0, C - K), F.Copy, "ps0", "yb")
-                dma("a", T.y[:, K:C], T.ysb[:, K:C], "yb", "y_b")
-            else:
-                quant("x", 0, K, T.xs[:, 0:4 * K], "xa0 xa1 xa2 xa3", "qxa")
-        order = "sb1a sb2a za0v za1v za2a za3a sb3a fb0v fb1v qz0v xb0a "
-        if last:
-            order += "xb1a fb2v fb3v xb2v xb3v sa0a sa1a sa2a sa3a qb0v fa0v fa1v fa2v fa3v yb0a xa0v xa1v xa2v xa3v qa0v"
-        else:
-            order += "sa0a sa1a xb1a fb2v sa2a sa3a fb3v xb2a xb3v fa0v fa1v fa2v fa3v qb0v xa0a xa1a xa2v xa3v qa0v"
-        for w in order.split():
-            step(w[:2], int(w[2]), w[3])
-    mm(1, "v", 0, "x", 0, K, "qv qxa")
-    dma("s", T.oc[:, 0:4 * K], T.qx[:, 0:K].bitcast(dt.uint8), "qxa", "y_oc")
-    cp(T.ysb[:, 0:K], bank(1, K), "ps1", "ya")
+                    scale(eng[b], step("z", b), by(plane("dec", b), came), 1.0)
+            quant("z", a, n, w("z", 4 * a, 4 * n))
+            for b in range(4):
+                scale(eng[5 + b], plane("z64", b, a, n), step("z", b), 64.0)
+                mm(pb + b, "w", 128 * b, "z", a, n)
+        for a, n, eng in ((K, C, "vvaa vaaa aaav"), (0, K, "vvaa aaaa aavv")):
+            step = lambda t, b: w(t, 4 * a + b, 4 * n, 4)
+            pb = 0 if a else 4
+            for b in range(4):
+                tt(plane("x64", b, a, n), bank(pb + b, n - a), plane("z64", b, a, n), A.add)
+                scale(eng[10 + b], step("xs", b), plane("x64", b, a, n), 1.0 / 64)
+            quant("x", a, n, w("xs", 4 * a, 4 * n))
+            if last:
+                mm(pb, "v", 0, "x", a, n)
+                dma("s", T.oc[:, 4 * a:4 * n], T.qx[:, a:n].bitcast(dt.uint8), [codes("x", a, n)], [], 512 * (n - a))
+                if a:
+                    act(w("ysb", a, n), bank(pb, n - a), F.Copy)
+                else:
+                    cp(w("ysb", a, n), bank(pb, n - a))
+                dma("a" if a else "s", T.y[:, a:n], T.ysb[:, a:n], [w("ysb", a, n)], [], 512 * (n - a))
+            elif a:
+                mm(3, "p", 0, "x", a, n)
     for k in range(4):
-        dma("s" if k % 2 else "a", T.osc[4 * k:4 * k + 4, :], T["sx_"][32 * k:32 * k + 4, :], "qxa qxb", "y_s%d" % k)
-    dma("s", T.y[:, 0:K], T.ysb[:, 0:K], "ya", "y_a")
-    op("g", None, "sent0 sent1 lsent0 lsent1 y_ol y_ocb y_oc y_s0 y_s1 y_s2 y_s3 y_a y_b", "")
+        dma("s" if k % 2 else "a", T.osc[4 * k:4 * k + 4, :], T["sx_"][32 * k:32 * k + 4, :], [scales("x")], [], 4 * C)
+    op("g", None, stored, [], 0.0)
     emit(g, T, ops)

@@ -3,6 +3,11 @@ from concourse.mybir import dt, AluOpType as A, ActivationFunctionType as F
 C, K, ROUNDS = 448, 128, 2
 HUGE = 2.0 ** 90
 MID = 224.0
+LOADS = ((0, 192), (192, 320), (320, 448))
+LAYER = ((128, 288, "vvaa vvaa aaav a"), (288, 448, "vaaa vvva aaav a"), (0, 128, "vvaa vvaa aavv v"))
+SEARCH = (("a", 0, 7), ("v", 7, 14), ("a", 14, 21), ("v", 21, 28))
+STORES = ((128, 288), (288, 448), (0, 128))
+ROWS = 18000
 CODE, PLANE = "float8_e4m3fn_x4", "uint8"
 WIDTH = {"bfloat16": 2, "float16": 2, "uint16": 2, "float32": 4, "int32": 4, CODE: 4, PLANE: 1}
 
@@ -12,26 +17,26 @@ def _sb(n, d):
 
 
 SCRATCH = {"ps": ("psum", [128, 4096], "float32")}
-for _n, _w in (("x0", 1792), ("xs", 1792), ("x64", 1792), ("z", 1792), ("z64", 1792), ("dec", 1792), ("ut", 512), ("vt", 512),
+for _n, _w in (("x0", 1792), ("xs", 1792), ("x64a", 1792), ("x64b", 1792), ("z", 1792), ("z64", 1792), ("dec", 1792), ("ut", 512), ("vt", 512),
                ("t1", 1792), ("tb", 1024), ("kd4", 128), ("k4a", 128), ("i16", 464), ("tz", 464), ("msk", 464), ("kml", 448),
                ("kmr", 448), ("klev", 464), ("k01", 464), ("kc", 464), ("kc2", 464), ("k16", 448), ("kdb", 448), ("ka", 464),
-               ("kb", 464), ("kl", 896), ("dgi", 528), ("dga", 528), ("dg", 528), ("dv", 520), ("c4", 512), ("c5", 512),
+               ("kb", 464), ("kl", 896), ("dgi", 528), ("dga", 528), ("dg", 528), ("dg2", 528), ("dv", 520), ("c4", 512), ("c5", 512),
                ("ks", 480), ("b32", 480), ("blk", 64), ("nrr", 448), ("nrl", 448), ("v1r", 448), ("v1l", 448), ("vr", 448),
                ("c1r", 480), ("c1l", 480), ("c2r", 480), ("c2l", 480), ("b1r", 448), ("b1l", 448), ("g1l", 448), ("nf", 896),
-               ("run", 896), ("ord", 448), ("rb", 448)):
+               ("ord", 448), ("rb", 448)):
     SCRATCH[_n] = _sb(_w, "bfloat16")
 for _n, _w in (("w2r", 448), ("w2l", 448), ("g2r", 448), ("g2l", 448), ("h2r", 448), ("h2l", 448), ("hh", 480), ("tt", 928),
-               ("ts", 928), ("no", 448)):
+               ("ts", 928), ("run", 896), ("no", 448)):
     SCRATCH[_n] = _sb(_w, "float16")
-for _n, _w in (("win", 968), ("sm", 448), ("sw", 448), ("smr", 456), ("sml", 456), ("thr", 896), ("nd", 336), ("kd", 224),
-               ("ordf", 448), ("iw", 976), ("ga", 448), ("gb", 448), ("gw", 448), ("ysb", 448), ("col", 24), ("tab", 336),
-               ("wk", 640), ("sma", 320)):
+for _n, _w in (("win", 936), ("sm", 448), ("sw", 448), ("smr", 456), ("sml", 456), ("wb", 64), ("nd", 336), ("kd", 224),
+               ("ordf", 448), ("iw", 976), ("ga", 448), ("gb", 448), ("gw", 448), ("ysb", 448), ("col", 24), ("tab", 112),
+               ("sma", 320)):
     SCRATCH[_n] = _sb(_w, "float32")
 for _n, _w in (("pi", 8), ("ni", 256)):
     SCRATCH[_n] = _sb(_w, "int32")
-for _n, _w in (("lu", 128), ("upk", 16), ("off", 272), ("came0", 8), ("came1", 8)):
+for _n, _w in (("upk", 16), ("off", 272), ("came0", 8), ("came1", 8)):
     SCRATCH[_n] = _sb(_w, "uint16")
-for _n, _w in (("x", 448), ("z", 448), ("u", 128), ("p", 256), ("v", 128), ("w", 512), ("c", 1024), ("1", 448), ("b", 256),
+for _n, _w in (("x", 448), ("z", 448), ("u", 128), ("p", 256), ("v", 128), ("w", 512), ("c", 1280), ("1", 448), ("b", 256),
                ("l0", 448), ("l1", 448)):
     SCRATCH["q" + _n] = _sb(_w, CODE)
     SCRATCH["s" + _n + "_"] = _sb(_w, PLANE)
@@ -39,7 +44,9 @@ for _n, _w in (("x", 448), ("z", 448), ("u", 128), ("p", 256), ("v", 128), ("w",
 NSEM, NDMA = 112, 24
 SEMAPHORES = (["c%d" % i for i in range(NSEM)] + ["d%d" % i for i in range(NDMA)]
               + [n + str(t) for n in ("arr", "out", "larr", "lout") for t in range(ROUNDS)])
-CYCLE, WAKE, ISSUE, DMA, RATE, PASSES, PATIENCE = 0.83, 200.0, 60.0, 700.0, 180.0, 4, 10.0
+CYCLE, WAKE, ISSUE, DMA, RATE, FAR, PATIENCE, MOVES = 0.83, 200.0, 60.0, 700.0, 180.0, 90.0, 10.0, 30000
+MACHINES = ((1.0, 1.0, 0.0, 1.0), (1.5, 1.5, 0.0, 1.3), (1.0, 0.6, 20.0, 0.75))
+ORDER = []
 
 
 def depends(ops):
@@ -50,7 +57,7 @@ def depends(ops):
             for name, m in parts:
                 for j, mj, wj in seen.get(name, []):
                     if m & mj and j != i:
-                        if wj and writes and kind == "acc" or name == "turn":
+                        if name == "turn":
                             o.add(j)
                         elif wj or writes or name == "ps" and ops[j][0] != e:
                             d.add(j)
@@ -97,29 +104,70 @@ def place(ops, edges, urgency):
 
 def schedule(ops, deps, after):
     n = len(ops)
-    lag = [0.0 if o[0] == "x" or o[4] == "dma" or isinstance(o[4], tuple) else WAKE for o in ops]
+    eng, cost = [o[0] for o in ops], [o[5] for o in ops]
+    moves = [o[0] == "x" or o[4] == "dma" or isinstance(o[4], tuple) for o in ops]
+    lag = [0.0 if moves[i] else WAKE * (1.3 if eng[i] == "p" else 1.0) for i in range(n)]
     fore, back = [{} for _ in ops], [{} for _ in ops]
     for i in range(n):
         for j in deps[i] | after[i]:
-            fore[i][j] = ops[j][5] + lag[j] if j in deps[i] else 0.0
-            back[j][i] = ops[i][5] + lag[j] if j in deps[i] else max(0.0, ops[i][5] - ops[j][5])
+            fore[i][j] = cost[j] + lag[j] if j in deps[i] else 0.0
+            back[j][i] = cost[i] + lag[j] if j in deps[i] else max(0.0, cost[i] - cost[j])
+
+    def length(seq):
+        total = 0.0
+        for slow, move, each, wake in MACHINES:
+            done, free = [0.0] * n, dict.fromkeys("vapgsxd", 0.0)
+            for i in seq:
+                e = eng[i]
+                t = free[e]
+                for j in deps[i]:
+                    if done[j] > t:
+                        t = done[j]
+                if not moves[i]:
+                    free[e] = t + slow * cost[i] + each
+                    done[i] = free[e] + wake * lag[i]
+                elif e == "x" or not cost[i]:
+                    done[i] = t
+                else:
+                    free[e] = t + ISSUE
+                    done[i] = free["d"] = max(t + move * DMA, free["d"]) + move * (cost[i] - DMA)
+            total += max(done) / slow
+        return total
+
     urgency, best = [0.0] * n, None
     for i in reversed(range(n)):
-        urgency[i] = ops[i][5] + max([urgency[u] - ops[u][5] + d for u, d in back[i].items()] + [0.0])
-    for _ in range(PASSES):
+        urgency[i] = cost[i] + max([urgency[u] - cost[u] + d for u, d in back[i].items()] + [0.0])
+    for _ in range(4):
         start, seq = place(ops, fore, urgency)
-        end = max(start[i] + ops[i][5] for i in range(n))
-        if best is None or end < best[0]:
-            best = (end, [seq[k] for k in sorted(range(n), key=lambda k: (start[seq[k]], k))])
-        start, seq = place(ops, back, [start[i] + ops[i][5] for i in range(n)])
-        urgency = [start[i] + ops[i][5] for i in range(n)]
+        if best is None or length(seq) < best[0]:
+            best = (length(seq), seq)
+        start, seq = place(ops, back, [start[i] + cost[i] for i in range(n)])
+        urgency = [start[i] + cost[i] for i in range(n)]
+    (now, seq), seed = best, 1
+    for turn in range(MOVES):
+        seed = seed * 1103515245 + 12345 & 0x7FFFFFFF
+        a, way, far = (seed >> 8) % n, (seed >> 20 & 1) * 2 - 1, 1 + (seed >> 22) % 5 // 3 + (seed >> 22) % 5 // 4
+        i, b = seq[a], a + way
+        while 0 <= b < n and seq[b] not in (fore if way < 0 else back)[i]:
+            far -= eng[seq[b]] == eng[i]
+            if not far:
+                new = seq[:b] + [i] + seq[b:a] + seq[a + 1:] if way < 0 else seq[:a] + seq[a + 1:b + 1] + [i] + seq[b + 1:]
+                end = length(new)
+                if end <= now + WAKE / 4 * (1 - turn / MOVES) * (seed >> 12 & 255) / 255:
+                    now, seq = end, new
+                    if end < best[0]:
+                        best = (end, new)
+                break
+            b += way
     return best[1]
 
 
 def emit(g, T, ops):
     queue = {"v": g.vector, "a": g.scalar, "p": g.tensor, "g": g, "s": g.sync}
     deps, after = depends(ops)
-    order = schedule(ops, deps, after)
+    if not ORDER:
+        ORDER.extend(schedule(ops, deps, after))
+    order = ORDER
     place = {i: n for n, i in enumerate(order)}
     known, at_issue, waits, needed = {}, {}, {}, set()
     for i in order:
@@ -130,10 +178,7 @@ def emit(g, T, ops):
                 mine.append(j)
                 needed.add(j)
                 kn |= 1 << j | at_issue[j]
-        known[e] = kn
-        for j in after[i]:
-            kn |= 1 << j | at_issue[j]
-        at_issue[i] = kn
+        known[e] = at_issue[i] = kn
         waits[i] = mine
     user, count, mark, ndma = {}, {}, {}, 0
     for i in order:
@@ -148,18 +193,20 @@ def emit(g, T, ops):
         if fn is None:
             continue
         ins = fn()
+        ins = ins if isinstance(ins, list) else [ins]
         if i not in needed:
             continue
         if kind == "dma":
             name = "d%d" % ndma
             ndma += 1
-            ins.then_inc(T.sem[name], 16)
+            ins[0].then_inc(T.sem[name], 16)
             mark[i] = (name, 16)
             continue
         n = [n for n in range(NSEM) if n not in user or at_issue[i] >> user[n] & 1][0]
         user[n] = i
-        count[n] = count.get(n, 0) + 1
-        ins.then_inc(T.sem["c%d" % n], 1)
+        count[n] = count.get(n, 0) + len(ins)
+        for one in ins:
+            one.then_inc(T.sem["c%d" % n], 1)
         mark[i] = ("c%d" % n, count[n])
 
 
@@ -194,7 +241,7 @@ def rank_program(g, core, T, topo):
 
     def time(out, ins, slow=1):
         if out[4] or ins[0][4]:
-            return 50 + out[2] * CYCLE * (3 if out[4] else 1.5)
+            return 50 + out[2] * CYCLE * (3.8 if out[4] else 1.56)
         return max(64, out[2] * slow * (0.5 if all(v[3] == 2 for v in [out] + ins) else 1)) * CYCLE
 
     ap = lambda x: x[0] if isinstance(x, tuple) else x
@@ -226,7 +273,7 @@ def rank_program(g, core, T, topo):
         if bias is not None:
             kw["bias"] = ap(bias)
         op("a", lambda: S.activation(out[0], a[0], f, **kw), [a, scale, bias], [out],
-           65 + 1.5 * CYCLE * out[2] if a[4] else max(64, out[2]) * CYCLE)
+           65 + 1.56 * CYCLE * out[2] if a[4] else max(64, out[2]) * CYCLE)
 
     codes = lambda n, a=0, b=None: w("q" + n, a, b)
     scales = lambda n, a=0, b=None: w("s" + n + "_", a, b)
@@ -238,11 +285,12 @@ def rank_program(g, core, T, topo):
     def bank(k, n=C, a=0):
         return w("ps", 512 * k + a, 512 * k + a + n)
 
-    def mm(k, ln, la, rn, a, b, start=True, stop=True):
-        ins = [codes(ln, la, la + 128), scales(ln, la, la + 128), codes(rn, a, b), scales(rn, a, b)]
-        out = bank(k, b - a)
-        op("p", lambda: P.matmul_mx(out[0], ins[0][0], ins[1][0], ins[2][0], ins[3][0], start, stop), ins, [out],
-           (b - a + 16) * CYCLE, None if start else "acc")
+    def mm(k, *terms):
+        terms = [terms[j:j + 5] for j in range(0, len(terms), 5)]
+        ins = [[codes(ln, la, la + 128), scales(ln, la, la + 128), codes(rn, a, b), scales(rn, a, b)] for ln, la, rn, a, b in terms]
+        out = bank(k, ins[0][2][2])
+        calls = lambda: [P.matmul_mx(out[0], *[v[0] for v in x], j == 0, j == len(ins) - 1) for j, x in enumerate(ins)][-1]
+        op("p", calls, sum(ins, []), [out], len(ins) * (out[2] + 16) * CYCLE)
 
     def iota(out, pat, base, cm=0):
         op("g", lambda: g.iota(out[0], pat, base, cm, allow_small_or_imprecise_dtypes=True), [], [out], 130 + 2 * CYCLE * out[2])
@@ -263,22 +311,19 @@ def rank_program(g, core, T, topo):
         for n, (dst, src, raw) in enumerate(parts):
             a, b = (dst[0].bitcast(dt.uint8), src[0].bitcast(dt.uint8)) if raw else (dst[0], src[0])
             op("g", lambda a=a, b=b: g.remote_dma(a, b, T.sem[there], T.sem[here], pid, rid, mask),
-               [p[1] for p in parts], [(here, 1 << n)], DMA + 128 * src[2] * src[3] / RATE, (here, len(parts) * nout))
+               [p[1] for p in parts], [(here, 1 << n)], DMA + 300 + 128 * src[2] * src[3] / FAR, (here, len(parts) * nout))
         stored.append((here, 1 << len(parts) - 1))
         op("x", None, [(here, (1 << len(parts)) - 1)], [p[0] for p in parts], 0.0, (there, len(parts) * nin))
 
     col = lambda j: w("col", j, j + 1)
-    R_, NR, R15, H1, H2, NB, N4, PAR, RH, M15, NM15, MM15, RN4, N4A = range(14)
-    MRB, MLW, MLB, BMB = 16, 464, 480, 937
-    CL, CR, TL, TR = 0, 28, 56, 84
+    R_, NR, R15, H1, H2, NB, N4, PAR, RH, M15, NM15, MM15, RN4, N4A, RK = range(15)
+    MRB, MLW, MLB = 16, 464, 480
     O_L2, O_LR, O_W, O_AT, O_O = 0, 56, 112, 168, 200
-    VR, VL, C4, C5 = 512, 640, 768, 896
+    VR, VL, C4, C5, EF = 512, 640, 768, 896, 1024
     HALF, WORDS, SPLIT, STEP, ODD = C // 2, C // 4, 256, 8192.0, 512
     tab = lambda a, n=56: w("tab", a, a + n)
-    wk = lambda j, a=0, n=56: w("wk", 64 * j + a, 64 * j + n)
     plane = lambda t, b, a=0, n=C: w(t, C * b + a, C * b + n)
-    lu = lambda a: w("lu", a, a + 28)
-    TK, TE = 168, 200
+    TK, TE, TU = 0, 32, 96
 
     def blocks(k, a, b):
         n = b - a
@@ -287,24 +332,24 @@ def rank_program(g, core, T, topo):
         scan(w("sw", a, b), w("k16", a, b), w("sm", a, b), 0.0, A.mult, A.add)
         scan(w("win", MRB + a, MRB + b), bank(k, n), w("kmr", a, b), -HUGE, A.max, A.subtract)
 
-    dma("a", T.ut[:], T.u[:], [], [w("ut")], 128 * 1024)
-    dma("s", T.x0[:, 0:896], T.x[:, 0:896], [], [w("x0", 0, 896), ("turn", 1)], 128 * 2816)
-    dma("s", T.x0[:, 896:], T.x[:, 896:], [], [w("x0", 896), ("turn", 1)], 128 * 4608)
-    dma("s", T.qw[:].bitcast(dt.uint8), T.wc[:], [w("x0")], [codes("w")], 128 * 2048)
-    dma("s", T["sw_"][:], T.ws[:], [w("x0")], [scales("w")], 128 * 2560)
-    dma("s", T.vt[:], T.v[:], [w("x0")], [w("vt")], 128 * 3584)
+    dma("a", T.ut[:], T.u[:], [], [w("ut"), ("turn", 1)], 128 * 1024)
+    for a, b in LOADS:
+        dma("s", T.x0[:, 4 * a:4 * b], T.x[:, 4 * a:4 * b], [], [w("x0", 4 * a, 4 * b), ("turn", 1)], 1024 * (b - a))
+    dma("s", T.qw[:].bitcast(dt.uint8), T.wc[:], [w("x0")], [codes("w"), ("turn", 1)], 128 * 2048)
+    dma("s", T["sw_"][:], T.ws[:], [w("x0")], [scales("w"), ("turn", 1)], 128 * 512)
+    dma("s", T.vt[:], T.v[:], [w("x0")], [w("vt"), ("turn", 1)], 128 * 1024)
 
     op("g", lambda: g.iota(T.pi[:, 0:1], [[0, 1]], 0, 1), [], [w("pi", 0, 1)], 130)
     ts(w("pi", 1, 2), w("pi", 0, 1), 15, A.bitwise_and)
     cp(col(R_), w("pi", 1, 2))
-    for c_, sc, bi in ((H1, -HUGE, HUGE), (H2, HUGE, HUGE), (NR, -1.0, 0.0), (R15, -1.0, 15.0), (RH, -1.0, 1.5)):
+    for c_, sc, bi in ((H1, -HUGE, HUGE), (H2, HUGE, HUGE), (R15, -1.0, 15.0), (RH, -1.0, 1.5)):
         act(col(c_), col(R_), F.Identity, sc, bi)
     for c_, sc in ((M15, 1.0), (NM15, -1.0)):
         act(col(c_), col(R15), F.Sign, sc)
     act(col(MM15), col(M15), F.Copy, MID)
     act(col(NB), col(M15), F.Identity, -512.0, MID)
-    iota(tab(320, 16), [[1, 2], [16, 8]], 0)
-    cp(w("upk"), tab(320, 16))
+    iota(tab(TU, 16), [[1, 2], [16, 8]], 0)
+    cp(w("upk"), tab(TU, 16))
     quant("u", 0, 128, w("ut"))
     words = by(codes("u"), w("upk"), True)
     op("v", lambda: V.tensor_copy(T.qp[:, 0:256].bitcast(dt.uint32), words[0]), [words], [codes("p")], time(codes("p"), [words]))
@@ -322,44 +367,33 @@ def rank_program(g, core, T, topo):
     act(w("k01"), w("klev"), F.Relu, -2.0 / HUGE, 1.0)
     act(w("kc"), w("k01"), F.Identity, 2.0, -1.0)
     act(w("kc2"), w("k01"), F.Identity, 512.0 + MID, -MID)
-    for a, b, val in ((0, 15, HUGE), (464, 480, HUGE), (929, 968, HUGE)):
+    for a, b, val in ((0, 15, HUGE), (464, 480, HUGE), (929, 936, HUGE)):
         ms(w("win", a, b), val)
     for a in (15, 928):
         act(w("win", a, a + 1), w("msk", 16, 17), F.Identity, -2 * HUGE, HUGE)
     ms(w("smr", 448), -HUGE)
     ms(w("sml", 0, 8), -HUGE)
-    iota(tab(0), [[0, 28], [16, 2]], 1)
-    iota(tab(56, 28), [[-1, 14], [0, 2]], 15)
-    iota(tab(84, 28), [[1, 14], [0, 2]], 2)
-    act(wk(0), tab(0), F.Identity, 1.0, col(R_))
-    act(tab(112), tab(56), F.Identity, -2.0, 31.0)
-    tt(wk(1), wk(0), tab(56), A.is_gt)
-    tt(wk(2), wk(1), tab(112), A.mult)
-    tt(wk(3), wk(1), tab(56), A.mult)
-    tt(wk(4), wk(2), tab(56), A.add)
-    tt(wk(5), wk(0), wk(3), A.subtract)
-    ts(lu(TL), wk(4, 0, 28), 16.0, A.mult, -17.0, A.add)
-    ts(lu(TR), wk(4, 28), -16.0, A.mult, 479.0, A.add)
-    tt(wk(6), wk(5), wk(4), A.is_equal)
-    act(wk(7, 0, 28), wk(4, 0, 28), F.Identity, 15.0, float(MLB - BMB - 30))
-    act(wk(7, 28), wk(4, 28), F.Identity, -15.0, float(466 - BMB))
-    act(wk(8, 0, 28), wk(5, 0, 28), F.Identity, 1.0, float(BMB - 2))
-    act(wk(8, 28), wk(5, 28), F.Identity, -1.0, float(BMB + 29))
-    tt(wk(9), wk(6), wk(7), A.mult)
-    tt(wk(2), wk(9), wk(8), A.add)
-    cp(w("lu", 0, 56), wk(2))
     iota(tab(TK, 28), [[16, 28]], 0)
     act(tab(TK, 28), tab(TK, 28), F.Identity, 1.0, col(R_))
-    iota(w("kl", 0, C), [[0, C]], -16)
-    iota(w("kl", C), [[0, C]], 16)
-    for a, s, c_, down, bi in ((14, 31, NR, True, -225.0), (30, 32, NR, False, -1.0), (449, 33, R15, True, 1.0), (478, 32, R15, False, -223.0)):
-        act(w("kl", a - 1, a + 13 * s, s), tab(TK, 14), F.Identity, 0.0, col(c_))
-        act(w("kl", a, a + 13 * s + 1, s), rev("tab", TK, 14) if down else tab(TK, 14), F.Identity, 1.0, bi)
+    for h in range(2):
+        act(w("kl", C * h, C * h + C), w("i16", 0, C), F.Identity, 0.0, -1.0 / 64)
+    pick(w("kl"), w("kl"), [[1, 28], [1, 32]], A.is_gt, 1.0 / 64, -29, 0)
+    act(col(NR), col(R_), F.Copy, -1.0 / 1024)
+    act(col(RK), col(R15), F.Copy, 1.0 / 1024)
+    for a, s, bi in ((0, 32, -4.0), (1, 32, col(RK)), (29, 31, -4.0), (30, 32, col(NR))):
+        act(w("kl", a, a + 27 * s + 1, s), tab(TK, 28), F.Identity, 0.0, bi)
+    act(w("kl", 31, None, 32), tab(TK, 28), F.Identity, 1.0 / 1024, -MID / 1024)
+    ms(w("nf", 31, None, 32), 0.0)
+    ms(w("wb", 28, 30), HUGE)
     iota(w("dgi"), [[1, 528]], 0, -4)
     act(w("dga"), w("dgi"), F.Abs, 1.0, -3.0)
     act(w("dg"), w("dga"), F.Relu, -1.0, 1.0)
     for b in range(4):
         quant("c", 128 * b, 128 * b + 128, w("dg", 3 - b, 515 - b))
+    act(w("dga"), w("dgi"), F.Abs, 1.0, -3.5)
+    act(w("dg2"), w("dga"), F.Relu, -1.0, 1.5)
+    quant("c", EF, EF + 128, w("dg2", 3, 515))
+    quant("c", EF + 128, EF + 256, w("dg2", 2, 514))
     pick(w("dv"), w("dg", 0, 520), [[1, 520]], A.not_equal, -1.0, 1, -4)
     iota(w("dv", 63, None, 64), [[0, 8]], 0)
     pick(w("dv", 64, None, 64), w("dv", 64, None, 64), [[-16, 8]], A.not_equal, 2.0, -15, 1)
@@ -402,16 +436,17 @@ def rank_program(g, core, T, topo):
     iota(w("iw", ODD), [[1, 464]], 0)
     iota(w("rb"), [[1, C]], -224)
     for b in range(4):
-        act(plane("x64", b), w("x0", b, None, 4), F.Copy, 64.0)
-    quant("x", 0, HALF, w("x0", 0, 896))
-    mm(3, "p", 0, "x", 0, HALF)
-    quant("x", HALF, C, w("x0", 896))
+        act(plane("x64a", b), w("x0", b, None, 4), F.Copy, 64.0)
+    for j, (a, b) in enumerate(LOADS):
+        quant("x", a, b, w("x0", 4 * a, 4 * b))
+        mm(4 + j, "p", 0, "x", a, b)
 
     sma = lambda a, n=56: w("sma", a, a + n)
     ni = lambda a, n=56: w("ni", a, a + n)
-    EE, OW, OWN, BASE, AT, BM = 0, 64, 128, 160, 192, 256
+    EE, OW, OWN, BASE, AT, BM, NS = 0, 64, 128, 160, 192, 256, 288
     QQ, IX, SEL = 0, 56, 112
     off = lambda a, n=28: w("off", a, a + n)
+    part = lambda lst, a, b: off(lst + a // 16, (b - a) // 16)
     RL, FL, RR = 0, 1, 2
     t1 = lambda b: w("t1", b, None, 4)
     flags = lambda h: w("tb", 512 * h, 512 * h + C)
@@ -421,27 +456,20 @@ def rank_program(g, core, T, topo):
         first, last = rnd == 0, rnd == ROUNDS - 1
         l_, n_ = "l%d" % rnd, str(rnd)
         send([(codes(l_), codes("x"), True), (scales(l_), scales("x"), False)], "arr" + n_, "out" + n_)
-        a, b = (HALF, C) if first else (0, K)
-        mm(4, "p", 0, "x", a, b)
         mm(0, "p", 0, "x", 0, C)
         mm(2, "p", 128, "x", 0, C)
-        blocks(3, *((0, HALF) if first else (K, C)))
-        blocks(4, a, b)
+        for j, piece in enumerate(LOADS if first else LAYER):
+            blocks(4 + j, *piece[:2])
         act(t1(FL), bank(2), F.Sign)
-        act(w("thr", 0, C), by(w("sw"), lu(TL)), F.Copy)
-        act(w("thr", C), by(w("sw"), lu(TR)), F.Copy)
         scan(rev("smr", 0), rev("ps", 0), rev("klev", 0), -HUGE, A.max, A.subtract)
         scan(w("sml", 8), bank(0), w("klev", 1, 449), -HUGE, A.max, A.subtract)
-        tt(sma(BM, 28), w("win", MLB, MLB + C, 16), w("win", 31, 464, 16), A.max)
-        tt(w("win", BMB, BMB + 28), sma(BM, 28), w("sw", 15, None, 16), A.max)
         tt(t1(RR), bank(0), w("smr", 1, 449), A.is_ge)
         tt(t1(RL), bank(0), w("sml", 7, 455), A.is_gt)
         quant("1", 0, C, w("t1"))
         act(w("nrr"), t1(RR), F.Identity, -1.0, 1.0)
         act(w("nrl"), t1(RL), F.Identity, col(NM15), col(M15))
         for k, e in ((3, RL), (4, RR)):
-            mm(k, "c", 128 * FL, "1", 0, C, True, False)
-            mm(k, "c", 128 * e, "1", 0, C, False, True)
+            mm(k, "c", EF + 64 * e, "1", 0, C)
         mm(5, "c", VR, "1", 0, C)
         mm(6, "c", VL, "1", 0, C)
         mm(7, "c", 128 * RR, "1", 0, C)
@@ -450,16 +478,30 @@ def rank_program(g, core, T, topo):
         act(w("vr"), bank(5), F.Copy)
         scan(rev("c1r", 17), rev("kc", 1), rev("v1r", 0), -1.0, A.min, A.mult)
         scan(w("c1l", 16, 464), w("kc", 0, C), w("v1l"), -1.0, A.min, A.mult)
-        for h, lst, cmp, ends in ((0, CL, A.is_lt, ((417, 13, -31), (30, C, 32))), (1, CR, A.is_le, ((478, None, 32), (878, C, -33)))):
-            tt(w("nf", C * h, C * h + C), by(w("win"), lu(lst)), w("thr", C * h, C * h + C), cmp)
-            scan(w("run", C * h, C * h + C), w("nf", C * h, C * h + C), w("kl", C * h, C * h + C), 0.0, A.mult, A.add)
-            for j in range(2):
-                ts(off(O_L2 + 28 * h + 14 * j, 14), w("run", *ends[j]), 240.0, A.add)
+        folded, before, behind = w("sw", 15, None, 16), w("win", MLB, MLB + C, 16), w("win", 31, 464, 16)
+        act(sma(NS, 28), folded, F.Copy, -1.0)
+        tt(sma(BM, 28), before, behind, A.max)
+        tt(w("wb", 0, 28), sma(BM, 28), folded, A.max)
+        act(sma(BM, 28), w("wb", 0, 28), F.Abs, 1.25 * 2.0 ** -24, 2.0 ** -124)
+        tt(w("wb", 30, 58), w("wb", 0, 28), sma(BM, 28), A.add)
+        tt(w("nf", 0, None, 32), behind, folded, A.is_gt)
+        tt(w("nf", 30, None, 32), before, folded, A.is_ge)
+        for e, a, b in SEARCH:
+            row = lambda m: (T.nf[:, 32 * m + 1:32 * m + 30], T.wb[:, m + 1:m + 30], T.sma[:, NS + m:NS + m + 1])
+            call = ((lambda o, x, c: S.activation(o, x, F.Sign, bias=c)) if e == "a" else
+                    (lambda o, x, c: V.tensor_scalar(o, x, c, 0.0, A.add, A.is_gt)))
+            op(e, lambda call=call, a=a, b=b: [call(*row(m)) for m in range(a, b)], [w("wb", 0, 58), sma(NS + a, b - a)],
+               [w("nf", 32 * m + 1, 32 * m + 30) for m in range(a, b)], (b - a) * 64 * CYCLE)
+        for h in range(2):
+            scan(w("run", C * h, C * h + C), w("kl", C * h, C * h + C), w("nf", C * h, C * h + C), 0.0, A.add, A.max)
+        ts(off(O_L2), w("run", 31, None, 32), 1024.0, A.mult, 15 + MID - 1024, A.add)
+        ts(off(O_L2 + 28), w("run", 28, 866, 31), -1024.0, A.mult, 464.0 + 1024, A.add)
         ts(ni(QQ), off(O_L2, 56), 1.0 / 16, A.mult, -0.46875, A.add)
         ts(w("kd", 3, None, 4), ni(QQ), 16.0, A.mult, w("kd4", 0, 1), A.add)
         for h, got, win, cmp in ((0, "ga", w("win", 0, 464), A.is_ge), (1, "gb", w("win", MLW, 936), A.is_le)):
-            act(w(got), by(win, off(O_L2 + 28 * h)), F.Copy)
-            tt(flags(h), w(got), bank(0), cmp)
+            for a, b in parts:
+                act(w(got, a, b), by(win, part(O_L2 + 28 * h, a, b)), F.Copy)
+                tt(w("tb", 512 * h + a, 512 * h + b), w(got, a, b), bank(0, b - a, a), cmp)
             quant("b", 128 * h, 128 * h + 128, w("tb", 512 * h, 512 * h + 512))
             mm(1 + h, "c", C4, "b", 128 * h, 128 * h + 128)
             nd = w("nd", WORDS * h, WORDS * h + WORDS)
@@ -474,7 +516,7 @@ def rank_program(g, core, T, topo):
         scan(flags(0), w("nrl"), w("b1l"), 0.0, A.mult, A.add)
         for h in (1, 0):
             quant("b", 128 * h, 128 * h + 128, w("tb", 512 * h, 512 * h + 512))
-            mm(1, "c", C5, "b", 128 * h, 128 * h + 128, h == 1, h == 0)
+        mm(1, "c", C5, "b", 128, 256, "c", C5, "b", 0, 128)
         scan(w("nd", HALF), w("kd4", 0, WORDS), bank(1, WORDS), 0.0, A.add, A.max)
         DB = (3, 4, 0, 2)
         for b in range(4):
@@ -487,13 +529,16 @@ def rank_program(g, core, T, topo):
         ts(sma(OW), ni(SEL), -float(ODD), A.add, 0.0, A.max)
         tt(sma(OWN, 28), sma(OW + 28, 28), sma(OW, 28), A.subtract)
         tt(sma(BASE, 28), sma(OWN, 28), tab(TK, 28), A.add)
-        act(w("gw"), by(w("iw"), off(O_W)), F.Copy)
+        for a, b in parts:
+            act(w("gw", a, b), by(w("iw"), part(O_W, a, b)), F.Copy)
         tt(w("w2r"), by(w("iw"), off(O_W + 28)), t1(RL), A.mult)
         scan(rev("c2r", 17), rev("kc2", 1), rev("w2r", 0), -MID, A.min, A.add)
-        tt(w("w2l"), w("gw"), bank(7), A.mult)
-        scan(w("c2l", 16, 464), w("kc2", 0, C), w("w2l"), -MID, A.min, A.add)
+        for a, b in parts:
+            tt(w("w2l", a, b), w("gw", a, b), bank(7, b - a, a), A.mult)
+            scan(w("c2l", 16 + a, 16 + b), w("kc2", a, b), w("w2l", a, b), -MID, A.min, A.add)
         act(w("ga"), by(w("c2r"), right), F.Identity, 1.0, MID)
-        act(w("gb"), by(w("c2l"), left), F.Identity, col(M15), col(MM15))
+        for a, b in parts:
+            act(w("gb", a, b), by(w("c2l"), part(O_LR, a, b)), F.Identity, col(M15), col(MM15))
         tt(w("g2r"), w("ga"), bank(5), A.mult)
         scan(rev("h2r", 0), rev("nrr", 0), rev("g2r", 0), 0.0, A.mult, A.add)
         for a, b in parts:
@@ -521,35 +566,30 @@ def rank_program(g, core, T, topo):
                 ts(out, src, f, A.mult)
             else:
                 act(out, src, F.Copy, f)
-        for a, n, eng in ((K, C, "vvaa vaaa aaav"), (0, K, "vvaa aaaa aavv")):
+        old, new = "x64" + "ab"[rnd % 2], "x64" + "ba"[rnd % 2]
+        for j, (a, n, eng) in enumerate(LAYER):
             step = lambda t, b: w(t, 4 * a + b, 4 * n, 4)
-            pb = 0 if a else 4
+            pb = 4 * (j % 2)
             for b in range(4):
                 if a:
-                    scale(eng[b], step("z", b), by(plane("x64", b), off(oo, 20)), 1.0 / 64)
+                    scale(eng[b], step("z", b), by(plane(old, b), off(oo + (a - K) // 16, (n - a) // 16)), 1.0 / 64)
                 else:
                     scale(eng[b], step("z", b), by(plane("dec", b), came), 1.0)
             quant("z", a, n, w("z", 4 * a, 4 * n))
             for b in range(4):
                 scale(eng[5 + b], plane("z64", b, a, n), step("z", b), 64.0)
                 mm(pb + b, "w", 128 * b, "z", a, n)
-        for a, n, eng in ((K, C, "vvaa vaaa aaav"), (0, K, "vvaa aaaa aavv")):
-            step = lambda t, b: w(t, 4 * a + b, 4 * n, 4)
-            pb = 0 if a else 4
             for b in range(4):
-                tt(plane("x64", b, a, n), bank(pb + b, n - a), plane("z64", b, a, n), A.add)
-                scale(eng[10 + b], step("xs", b), plane("x64", b, a, n), 1.0 / 64)
+                tt(plane(new, b, a, n), bank(pb + b, n - a), plane("z64", b, a, n), A.add)
+                scale(eng[10 + b], step("xs", b), plane(new, b, a, n), 1.0 / 64)
             quant("x", a, n, w("xs", 4 * a, 4 * n))
+        for j, (a, n, eng) in enumerate(LAYER):
+            mm(4 + j, "v" if last else "p", 0, "x", a, n)
             if last:
-                mm(pb, "v", 0, "x", a, n)
-                dma("s", T.oc[:, 4 * a:4 * n], T.qx[:, a:n].bitcast(dt.uint8), [codes("x", a, n)], [], 512 * (n - a))
-                if a:
-                    act(w("ysb", a, n), bank(pb, n - a), F.Copy)
-                else:
-                    cp(w("ysb", a, n), bank(pb, n - a))
-                dma("a" if a else "s", T.y[:, a:n], T.ysb[:, a:n], [w("ysb", a, n)], [], 512 * (n - a))
-            elif a:
-                mm(3, "p", 0, "x", a, n)
+                scale(eng[15], w("ysb", a, n), bank(4 + j, n - a), 1.0)
+    for a, n in STORES:
+        dma("s", T.oc[:, 4 * a:4 * n], T.qx[:, a:n].bitcast(dt.uint8), [codes("x", a, n)], [], 512 * (n - a) + ROWS)
+        dma("a", T.y[:, a:n], T.ysb[:, a:n], [w("ysb", a, n)], [], 512 * (n - a) + ROWS)
     for k in range(4):
         dma("s" if k % 2 else "a", T.osc[4 * k:4 * k + 4, :], T["sx_"][32 * k:32 * k + 4, :], [scales("x")], [], 4 * C)
     op("g", None, stored, [], 0.0)

from concourse.mybir import dt, AluOpType as A, ActivationFunctionType as F

C, K, ROUNDS = 448, 128, 2
HUGE = 2.0 ** 90
MID = 224.0
LOADS = ((0, 192), (192, 320), (320, 448))
LAYER = ((128, 288, "vvaa vvaa aaav a"), (288, 448, "vaaa vvva aaav a"), (0, 128, "vvaa vvaa aavv v"))
SEARCH = (("a", 0, 7), ("v", 7, 14), ("a", 14, 21), ("v", 21, 28))
STORES = ((128, 288), (288, 448), (0, 128))
ROWS = 18000
CODE, PLANE = "float8_e4m3fn_x4", "uint8"
WIDTH = {"bfloat16": 2, "float16": 2, "uint16": 2, "float32": 4, "int32": 4, CODE: 4, PLANE: 1}


def _sb(n, d):
    return ("sbuf", [128, n], d)


SCRATCH = {"ps": ("psum", [128, 4096], "float32")}
for _n, _w in (("x0", 1792), ("xs", 1792), ("x64a", 1792), ("x64b", 1792), ("z", 1792), ("z64", 1792), ("dec", 1792), ("ut", 512), ("vt", 512),
               ("t1", 1792), ("tb", 1024), ("kd4", 128), ("k4a", 128), ("i16", 464), ("tz", 464), ("msk", 464), ("kml", 448),
               ("kmr", 448), ("klev", 464), ("k01", 464), ("kc", 464), ("kc2", 464), ("k16", 448), ("kdb", 448), ("ka", 464),
               ("kb", 464), ("kl", 896), ("dgi", 528), ("dga", 528), ("dg", 528), ("dg2", 528), ("dv", 520), ("c4", 512), ("c5", 512),
               ("ks", 480), ("b32", 480), ("blk", 64), ("nrr", 448), ("nrl", 448), ("v1r", 448), ("v1l", 448), ("vr", 448),
               ("c1r", 480), ("c1l", 480), ("c2r", 480), ("c2l", 480), ("b1r", 448), ("b1l", 448), ("g1l", 448), ("nf", 896),
               ("ord", 448), ("rb", 448)):
    SCRATCH[_n] = _sb(_w, "bfloat16")
for _n, _w in (("w2r", 448), ("w2l", 448), ("g2r", 448), ("g2l", 448), ("h2r", 448), ("h2l", 448), ("hh", 480), ("tt", 928),
               ("ts", 928), ("run", 896), ("no", 448)):
    SCRATCH[_n] = _sb(_w, "float16")
for _n, _w in (("win", 936), ("sm", 448), ("sw", 448), ("smr", 456), ("sml", 456), ("wb", 64), ("nd", 336), ("kd", 224),
               ("ordf", 448), ("iw", 976), ("ga", 448), ("gb", 448), ("gw", 448), ("ysb", 448), ("col", 24), ("tab", 112),
               ("sma", 320)):
    SCRATCH[_n] = _sb(_w, "float32")
for _n, _w in (("pi", 8), ("ni", 256)):
    SCRATCH[_n] = _sb(_w, "int32")
for _n, _w in (("upk", 16), ("off", 272), ("came0", 8), ("came1", 8)):
    SCRATCH[_n] = _sb(_w, "uint16")
for _n, _w in (("x", 448), ("z", 448), ("u", 128), ("p", 256), ("v", 128), ("w", 512), ("c", 1280), ("1", 448), ("b", 256),
               ("l0", 448), ("l1", 448)):
    SCRATCH["q" + _n] = _sb(_w, CODE)
    SCRATCH["s" + _n + "_"] = _sb(_w, PLANE)

NSEM, NDMA = 112, 24
SEMAPHORES = (["c%d" % i for i in range(NSEM)] + ["d%d" % i for i in range(NDMA)]
              + [n + str(t) for n in ("arr", "out", "larr", "lout") for t in range(ROUNDS)])
CYCLE, WAKE, ISSUE, DMA, RATE, FAR, PATIENCE, MOVES = 0.83, 200.0, 60.0, 700.0, 180.0, 90.0, 10.0, 30000
MACHINES = ((1.0, 1.0, 0.0, 1.0), (1.5, 1.5, 0.0, 1.3), (1.0, 0.6, 20.0, 0.75))
ORDER = []


def depends(ops):
    seen, deps, after = {}, [], []
    for i, (e, fn, rd, wr, kind, cost) in enumerate(ops):
        d, o = set(), set()
        for writes, parts in ((False, rd), (True, wr)):
            for name, m in parts:
                for j, mj, wj in seen.get(name, []):
                    if m & mj and j != i:
                        if name == "turn":
                            o.add(j)
                        elif wj or writes or name == "ps" and ops[j][0] != e:
                            d.add(j)
        for writes, parts in ((False, rd), (True, wr)):
            for name, m in parts:
                old = seen.get(name, [])
                if writes:
                    old = [x for x in old if x[1] & ~m]
                seen[name] = old + [(i, m, writes)]
        deps.append(d)
        after.append(o)
    return deps, after


def place(ops, edges, urgency):
    n = len(ops)
    users = [[] for _ in range(n)]
    for i in range(n):
        for j in edges[i]:
            users[j].append(i)
    hold = [0.0 if o[0] == "x" else ISSUE if o[4] == "dma" or isinstance(o[4], tuple) else o[5] for o in ops]
    left, start, free, seq = [len(x) for x in edges], [0.0] * n, {}, []
    ready = {i: 0.0 for i in range(n) if not left[i]}
    while ready:
        best = None
        for e in "vapgsx":
            mine = [i for i in ready if ops[i][0] == e]
            if mine:
                t = max(free.get(e, 0.0), min(ready[i] for i in mine))
                i = max(mine, key=lambda i: (urgency[i] - PATIENCE * max(0.0, ready[i] - t), -i))
                if best is None or (max(t, ready[i]), i) < best:
                    best = (max(t, ready[i]), i)
        t, i = best
        del ready[i]
        seq.append(i)
        start[i] = t
        free[ops[i][0]] = t + hold[i]
        for u in users[i]:
            left[u] -= 1
            if not left[u]:
                ready[u] = max(start[j] + d for j, d in edges[u].items())
    return start, seq


def schedule(ops, deps, after):
    n = len(ops)
    eng, cost = [o[0] for o in ops], [o[5] for o in ops]
    moves = [o[0] == "x" or o[4] == "dma" or isinstance(o[4], tuple) for o in ops]
    lag = [0.0 if moves[i] else WAKE * (1.3 if eng[i] == "p" else 1.0) for i in range(n)]
    fore, back = [{} for _ in ops], [{} for _ in ops]
    for i in range(n):
        for j in deps[i] | after[i]:
            fore[i][j] = cost[j] + lag[j] if j in deps[i] else 0.0
            back[j][i] = cost[i] + lag[j] if j in deps[i] else max(0.0, cost[i] - cost[j])

    def length(seq):
        total = 0.0
        for slow, move, each, wake in MACHINES:
            done, free = [0.0] * n, dict.fromkeys("vapgsxd", 0.0)
            for i in seq:
                e = eng[i]
                t = free[e]
                for j in deps[i]:
                    if done[j] > t:
                        t = done[j]
                if not moves[i]:
                    free[e] = t + slow * cost[i] + each
                    done[i] = free[e] + wake * lag[i]
                elif e == "x" or not cost[i]:
                    done[i] = t
                else:
                    free[e] = t + ISSUE
                    done[i] = free["d"] = max(t + move * DMA, free["d"]) + move * (cost[i] - DMA)
            total += max(done) / slow
        return total

    urgency, best = [0.0] * n, None
    for i in reversed(range(n)):
        urgency[i] = cost[i] + max([urgency[u] - cost[u] + d for u, d in back[i].items()] + [0.0])
    for _ in range(4):
        start, seq = place(ops, fore, urgency)
        if best is None or length(seq) < best[0]:
            best = (length(seq), seq)
        start, seq = place(ops, back, [start[i] + cost[i] for i in range(n)])
        urgency = [start[i] + cost[i] for i in range(n)]
    (now, seq), seed = best, 1
    for turn in range(MOVES):
        seed = seed * 1103515245 + 12345 & 0x7FFFFFFF
        a, way, far = (seed >> 8) % n, (seed >> 20 & 1) * 2 - 1, 1 + (seed >> 22) % 5 // 3 + (seed >> 22) % 5 // 4
        i, b = seq[a], a + way
        while 0 <= b < n and seq[b] not in (fore if way < 0 else back)[i]:
            far -= eng[seq[b]] == eng[i]
            if not far:
                new = seq[:b] + [i] + seq[b:a] + seq[a + 1:] if way < 0 else seq[:a] + seq[a + 1:b + 1] + [i] + seq[b + 1:]
                end = length(new)
                if end <= now + WAKE / 4 * (1 - turn / MOVES) * (seed >> 12 & 255) / 255:
                    now, seq = end, new
                    if end < best[0]:
                        best = (end, new)
                break
            b += way
    return best[1]


def emit(g, T, ops):
    queue = {"v": g.vector, "a": g.scalar, "p": g.tensor, "g": g, "s": g.sync}
    deps, after = depends(ops)
    if not ORDER:
        ORDER.extend(schedule(ops, deps, after))
    order = ORDER
    place = {i: n for n, i in enumerate(order)}
    known, at_issue, waits, needed = {}, {}, {}, set()
    for i in order:
        e = ops[i][0]
        kn, mine = known.get(e, 0), []
        for j in sorted(deps[i], key=lambda j: -place[j]):
            if e != "x" and not kn >> j & 1:
                mine.append(j)
                needed.add(j)
                kn |= 1 << j | at_issue[j]
        known[e] = at_issue[i] = kn
        waits[i] = mine
    user, count, mark, ndma = {}, {}, {}, 0
    for i in order:
        e, fn, rd, wr, kind, cost = ops[i]
        for j in reversed(waits[i]):
            queue[e].wait_ge(T.sem[mark[j][0]], mark[j][1])
        if isinstance(kind, tuple):
            if fn is not None:
                fn()
            mark[i] = kind
            continue
        if fn is None:
            continue
        ins = fn()
        ins = ins if isinstance(ins, list) else [ins]
        if i not in needed:
            continue
        if kind == "dma":
            name = "d%d" % ndma
            ndma += 1
            ins[0].then_inc(T.sem[name], 16)
            mark[i] = (name, 16)
            continue
        n = [n for n in range(NSEM) if n not in user or at_issue[i] >> user[n] & 1][0]
        user[n] = i
        count[n] = count.get(n, 0) + len(ins)
        for one in ins:
            one.then_inc(T.sem["c%d" % n], 1)
        mark[i] = ("c%d" % n, count[n])


def rank_program(g, core, T, topo):
    rank = T.rank_of(core)
    if rank is None:
        return
    nxt = T.cores[(rank + 1) % len(T.cores)]
    prv = T.cores[(rank - 1) % len(T.cores)]
    rid, pid = topo.addr(nxt)[:2]
    mask = topo.mask(core, nxt)
    nout, nin = len(topo.engines(core, nxt)), len(topo.engines(prv, core))
    ops = []
    V, S, P = g.vector, g.scalar, g.tensor

    def w(name, a=0, b=None, s=1):
        cols = range(*slice(a, b, s).indices(SCRATCH[name][1][1]))
        bits = sum(set(1 << (c // 512 if name == "ps" else c) for c in cols))
        return (T[name][:, a:b:s], [(name, bits)], len(cols), WIDTH[SCRATCH[name][2]], None)

    def rev(name, a, n=C):
        return w(name, a + n - 1, a - 1 if a else None, -1)

    def by(win, lst, words=False):
        ap = win[0].bitcast(dt.uint32) if words else win[0]
        return (ap.indirect(lst[0]), win[1], 16 * lst[2], win[3], lst)

    def op(e, fn, rd, wr, cost, kind=None):
        parts = lambda vs: [p for v in vs if isinstance(v, tuple) for p in (v[1] if len(v) == 5 else [v])]
        lists = [v[4] for v in rd + wr if isinstance(v, tuple) and len(v) == 5 and v[4]]
        ops.append((e, fn, parts(rd + lists), parts(wr), kind, cost))

    def time(out, ins, slow=1):
        if out[4] or ins[0][4]:
            return 50 + out[2] * CYCLE * (3.8 if out[4] else 1.56)
        return max(64, out[2] * slow * (0.5 if all(v[3] == 2 for v in [out] + ins) else 1)) * CYCLE

    ap = lambda x: x[0] if isinstance(x, tuple) else x

    def tt(out, a, b, o):
        both = 1 if "ps" in (a[1][0][0], b[1][0][0]) else 2
        op("v", lambda: V.tensor_tensor(out[0], a[0], b[0], o), [a, b], [out], time(out, [a, b], both))

    def ts(out, a, s1, o1, s2=None, o2=None):
        more = () if o2 is None else (o2,)
        op("v", lambda: V.tensor_scalar(out[0], a[0], ap(s1), ap(s2), o1, *more), [a, s1, s2], [out], time(out, [a]))

    def cp(out, a):
        op("v", lambda: V.tensor_copy(out[0], a[0]), [a], [out], time(out, [a]))

    def scan(out, d0, d1, init, o0, o1):
        op("v", lambda: V.tensor_tensor_scan(out[0], d0[0], d1[0], init, o0, o1), [d0, d1], [out], time(out, [d0, d1]))

    def turn(out, a):
        op("v", lambda: V.transpose(out[0], a[0]), [a], [out], time(out, [a]))

    def ms(out, val):
        op("v", lambda: V.memset(out[0], val), [], [out], time(out, [out]))

    def act(out, a, f, scale=None, bias=None):
        kw = {}
        if scale is not None:
            kw["scale"] = ap(scale)
        if bias is not None:
            kw["bias"] = ap(bias)
        op("a", lambda: S.activation(out[0], a[0], f, **kw), [a, scale, bias], [out],
           65 + 1.56 * CYCLE * out[2] if a[4] else max(64, out[2]) * CYCLE)

    codes = lambda n, a=0, b=None: w("q" + n, a, b)
    scales = lambda n, a=0, b=None: w("s" + n + "_", a, b)

    def quant(name, a, b, src):
        q, s = codes(name, a, b), scales(name, a, b)
        op("v", lambda: V.quantize_mx(q[0], s[0], src[0]), [src], [q, s], 12 + 0.22 * src[2])

    def bank(k, n=C, a=0):
        return w("ps", 512 * k + a, 512 * k + a + n)

    def mm(k, *terms):
        terms = [terms[j:j + 5] for j in range(0, len(terms), 5)]
        ins = [[codes(ln, la, la + 128), scales(ln, la, la + 128), codes(rn, a, b), scales(rn, a, b)] for ln, la, rn, a, b in terms]
        out = bank(k, ins[0][2][2])
        calls = lambda: [P.matmul_mx(out[0], *[v[0] for v in x], j == 0, j == len(ins) - 1) for j, x in enumerate(ins)][-1]
        op("p", calls, sum(ins, []), [out], len(ins) * (out[2] + 16) * CYCLE)

    def iota(out, pat, base, cm=0):
        op("g", lambda: g.iota(out[0], pat, base, cm, allow_small_or_imprecise_dtypes=True), [], [out], 130 + 2 * CYCLE * out[2])

    def pick(out, src, pat, cmp, fill, base, cm):
        op("g", lambda: g.affine_select(out[0], src[0], pat, cmp, fill, base, cm), [src], [out], 170 + 2 * CYCLE * out[2])

    stored = []

    def dma(e, out, src, rd, wr, nbytes):
        q = g.sync if e == "s" else g.scalar
        if not wr:
            wr = [("store%d" % len(stored), 1)]
            stored.extend(wr)
        op(e, lambda: q.dma_start(out, src), rd, wr, DMA + nbytes / RATE, "dma")

    def send(parts, there, here):
        for n, (dst, src, raw) in enumerate(parts):
            a, b = (dst[0].bitcast(dt.uint8), src[0].bitcast(dt.uint8)) if raw else (dst[0], src[0])
            op("g", lambda a=a, b=b: g.remote_dma(a, b, T.sem[there], T.sem[here], pid, rid, mask),
               [p[1] for p in parts], [(here, 1 << n)], DMA + 300 + 128 * src[2] * src[3] / FAR, (here, len(parts) * nout))
        stored.append((here, 1 << len(parts) - 1))
        op("x", None, [(here, (1 << len(parts)) - 1)], [p[0] for p in parts], 0.0, (there, len(parts) * nin))

    col = lambda j: w("col", j, j + 1)
    R_, NR, R15, H1, H2, NB, N4, PAR, RH, M15, NM15, MM15, RN4, N4A, RK = range(15)
    MRB, MLW, MLB = 16, 464, 480
    O_L2, O_LR, O_W, O_AT, O_O = 0, 56, 112, 168, 200
    VR, VL, C4, C5, EF = 512, 640, 768, 896, 1024
    HALF, WORDS, SPLIT, STEP, ODD = C // 2, C // 4, 256, 8192.0, 512
    tab = lambda a, n=56: w("tab", a, a + n)
    plane = lambda t, b, a=0, n=C: w(t, C * b + a, C * b + n)
    TK, TE, TU = 0, 32, 96

    def blocks(k, a, b):
        n = b - a
        tt(w("sm", a, b), bank(k, n), w("msk", 16 + a, 16 + b), A.mult)
        scan(rev("win", MLB + a, n), rev("ps", 512 * k, n), rev("kml", a, n), -HUGE, A.max, A.subtract)
        scan(w("sw", a, b), w("k16", a, b), w("sm", a, b), 0.0, A.mult, A.add)
        scan(w("win", MRB + a, MRB + b), bank(k, n), w("kmr", a, b), -HUGE, A.max, A.subtract)

    dma("a", T.ut[:], T.u[:], [], [w("ut"), ("turn", 1)], 128 * 1024)
    for a, b in LOADS:
        dma("s", T.x0[:, 4 * a:4 * b], T.x[:, 4 * a:4 * b], [], [w("x0", 4 * a, 4 * b), ("turn", 1)], 1024 * (b - a))
    dma("s", T.qw[:].bitcast(dt.uint8), T.wc[:], [w("x0")], [codes("w"), ("turn", 1)], 128 * 2048)
    dma("s", T["sw_"][:], T.ws[:], [w("x0")], [scales("w"), ("turn", 1)], 128 * 512)
    dma("s", T.vt[:], T.v[:], [w("x0")], [w("vt"), ("turn", 1)], 128 * 1024)

    op("g", lambda: g.iota(T.pi[:, 0:1], [[0, 1]], 0, 1), [], [w("pi", 0, 1)], 130)
    ts(w("pi", 1, 2), w("pi", 0, 1), 15, A.bitwise_and)
    cp(col(R_), w("pi", 1, 2))
    for c_, sc, bi in ((H1, -HUGE, HUGE), (H2, HUGE, HUGE), (R15, -1.0, 15.0), (RH, -1.0, 1.5)):
        act(col(c_), col(R_), F.Identity, sc, bi)
    for c_, sc in ((M15, 1.0), (NM15, -1.0)):
        act(col(c_), col(R15), F.Sign, sc)
    act(col(MM15), col(M15), F.Copy, MID)
    act(col(NB), col(M15), F.Identity, -512.0, MID)
    iota(tab(TU, 16), [[1, 2], [16, 8]], 0)
    cp(w("upk"), tab(TU, 16))
    quant("u", 0, 128, w("ut"))
    words = by(codes("u"), w("upk"), True)
    op("v", lambda: V.tensor_copy(T.qp[:, 0:256].bitcast(dt.uint32), words[0]), [words], [codes("p")], time(codes("p"), [words]))
    act(scales("p"), by(scales("u"), w("upk")), F.Copy)
    quant("v", 0, 128, w("vt"))
    iota(w("i16"), [[0, 29], [1, 16]], 0)
    ts(w("msk"), w("i16"), col(R_), A.is_equal)
    act(w("k16"), w("i16", 0, C), F.Sign)
    act(w("kml"), w("i16", 0, C), F.Relu, HUGE, col(H1))
    act(w("kmr"), w("i16", 0, C), F.Relu, -HUGE, col(H2))
    for j in range(9):
        ms(w("tz", 2 ** j, None, 2 ** (j + 1)), float(j))
    ms(w("tz", 0, 1), 15.0)
    act(w("klev"), w("tz"), F.Relu, HUGE, col(H1))
    act(w("k01"), w("klev"), F.Relu, -2.0 / HUGE, 1.0)
    act(w("kc"), w("k01"), F.Identity, 2.0, -1.0)
    act(w("kc2"), w("k01"), F.Identity, 512.0 + MID, -MID)
    for a, b, val in ((0, 15, HUGE), (464, 480, HUGE), (929, 936, HUGE)):
        ms(w("win", a, b), val)
    for a in (15, 928):
        act(w("win", a, a + 1), w("msk", 16, 17), F.Identity, -2 * HUGE, HUGE)
    ms(w("smr", 448), -HUGE)
    ms(w("sml", 0, 8), -HUGE)
    iota(tab(TK, 28), [[16, 28]], 0)
    act(tab(TK, 28), tab(TK, 28), F.Identity, 1.0, col(R_))
    for h in range(2):
        act(w("kl", C * h, C * h + C), w("i16", 0, C), F.Identity, 0.0, -1.0 / 64)
    pick(w("kl"), w("kl"), [[1, 28], [1, 32]], A.is_gt, 1.0 / 64, -29, 0)
    act(col(NR), col(R_), F.Copy, -1.0 / 1024)
    act(col(RK), col(R15), F.Copy, 1.0 / 1024)
    for a, s, bi in ((0, 32, -4.0), (1, 32, col(RK)), (29, 31, -4.0), (30, 32, col(NR))):
        act(w("kl", a, a + 27 * s + 1, s), tab(TK, 28), F.Identity, 0.0, bi)
    act(w("kl", 31, None, 32), tab(TK, 28), F.Identity, 1.0 / 1024, -MID / 1024)
    ms(w("nf", 31, None, 32), 0.0)
    ms(w("wb", 28, 30), HUGE)
    iota(w("dgi"), [[1, 528]], 0, -4)
    act(w("dga"), w("dgi"), F.Abs, 1.0, -3.0)
    act(w("dg"), w("dga"), F.Relu, -1.0, 1.0)
    for b in range(4):
        quant("c", 128 * b, 128 * b + 128, w("dg", 3 - b, 515 - b))
    act(w("dga"), w("dgi"), F.Abs, 1.0, -3.5)
    act(w("dg2"), w("dga"), F.Relu, -1.0, 1.5)
    quant("c", EF, EF + 128, w("dg2", 3, 515))
    quant("c", EF + 128, EF + 256, w("dg2", 2, 514))
    pick(w("dv"), w("dg", 0, 520), [[1, 520]], A.not_equal, -1.0, 1, -4)
    iota(w("dv", 63, None, 64), [[0, 8]], 0)
    pick(w("dv", 64, None, 64), w("dv", 64, None, 64), [[-16, 8]], A.not_equal, 2.0, -15, 1)
    quant("c", VR, VR + 128, w("dv", 1, 513))
    quant("c", VL, VL + 128, w("dv", 3, 515))
    iota(w("blk", 0, 32), [[16, 8], [0, 4]], 0, -1)
    act(w("blk", 0, 32), w("blk", 0, 32), F.Abs, 1.0, 7.5)
    ts(w("blk", 32), w("blk", 0, 32), 8.0, A.is_lt)
    iota(w("c4"), [[0, 512]], 0)
    for b in range(4):
        act(w("c4", 5 * b, None, 16), w("blk", 32), F.Copy)
    act(w("c5"), w("c4"), F.Copy, float(ODD))
    quant("c", C4, C4 + 128, w("c4"))
    quant("c", C5, C5 + 128, w("c5"))
    act(w("k4a", 0, 116), w("i16", 0, 464, 4), F.Abs, 1.0, col(RH))
    act(w("k4a", 0, 116), w("k4a", 0, 116), F.Relu, -1.0, 2.5)
    act(w("kd4", 0, 116), w("k4a", 0, 116), F.Identity, -8 * STEP, STEP)
    for h in range(2):
        act(w("kd", WORDS * h, WORDS * h + WORDS), w("kd4", 1, WORDS + 1), F.Copy)
    ts(w("pi", 3, 4), w("pi", 1, 2), 2, A.arith_shift_right)
    ts(col(N4A), w("pi", 3, 4), STEP, A.mult, -3 * STEP, A.add)
    tt(col(N4), col(N4A), w("kd4", 0, 1), A.subtract)
    tt(col(RN4), col(R_), col(N4), A.subtract)
    iota(tab(TE), [[1, 2], [16, 28]], 16)
    act(tab(TE), tab(TE), F.Identity, 1.0, col(RN4))
    act(w("ka"), w("msk"), F.Copy, 512.0)
    act(w("kb"), w("msk"), F.Copy, 1024.0)
    tt(w("kdb"), w("ka", 15, 463), w("kb", 16, 464), A.subtract)
    ts(w("pi", 2, 3), w("pi", 0, 1), 4, A.arith_shift_right, 1, A.bitwise_and)
    ts(col(PAR), w("pi", 2, 3), -1.0, A.add)
    iota(w("b32"), [[0, 15], [1, 2], [0, 16]], 0)
    act(w("ks"), w("b32"), F.Abs, 1.0, col(PAR))
    iota(w("t1", 3, None, 4), [[0, C]], 0)
    iota(w("tb", C, 512), [[0, 64]], 0)
    iota(w("tb", 512 + C), [[0, 64]], 0)
    for n, a, v in (("c1r", 17, 2), ("c2r", 17, -224), ("c1l", 16, -1), ("c2l", 16, -224), ("hh", 16, 0)):
        iota(w(n, 0, a), [[0, a]], v)
        iota(w(n, a + C), [[0, 32 - a]], v)
    iota(w("iw", 0, ODD), [[0, ODD]], 0)
    iota(w("iw", ODD), [[1, 464]], 0)
    iota(w("rb"), [[1, C]], -224)
    for b in range(4):
        act(plane("x64a", b), w("x0", b, None, 4), F.Copy, 64.0)
    for j, (a, b) in enumerate(LOADS):
        quant("x", a, b, w("x0", 4 * a, 4 * b))
        mm(4 + j, "p", 0, "x", a, b)

    sma = lambda a, n=56: w("sma", a, a + n)
    ni = lambda a, n=56: w("ni", a, a + n)
    EE, OW, OWN, BASE, AT, BM, NS = 0, 64, 128, 160, 192, 256, 288
    QQ, IX, SEL = 0, 56, 112
    off = lambda a, n=28: w("off", a, a + n)
    part = lambda lst, a, b: off(lst + a // 16, (b - a) // 16)
    RL, FL, RR = 0, 1, 2
    t1 = lambda b: w("t1", b, None, 4)
    flags = lambda h: w("tb", 512 * h, 512 * h + C)
    parts = ((0, SPLIT), (SPLIT, C))

    for rnd in range(ROUNDS):
        first, last = rnd == 0, rnd == ROUNDS - 1
        l_, n_ = "l%d" % rnd, str(rnd)
        send([(codes(l_), codes("x"), True), (scales(l_), scales("x"), False)], "arr" + n_, "out" + n_)
        mm(0, "p", 0, "x", 0, C)
        mm(2, "p", 128, "x", 0, C)
        for j, piece in enumerate(LOADS if first else LAYER):
            blocks(4 + j, *piece[:2])
        act(t1(FL), bank(2), F.Sign)
        scan(rev("smr", 0), rev("ps", 0), rev("klev", 0), -HUGE, A.max, A.subtract)
        scan(w("sml", 8), bank(0), w("klev", 1, 449), -HUGE, A.max, A.subtract)
        tt(t1(RR), bank(0), w("smr", 1, 449), A.is_ge)
        tt(t1(RL), bank(0), w("sml", 7, 455), A.is_gt)
        quant("1", 0, C, w("t1"))
        act(w("nrr"), t1(RR), F.Identity, -1.0, 1.0)
        act(w("nrl"), t1(RL), F.Identity, col(NM15), col(M15))
        for k, e in ((3, RL), (4, RR)):
            mm(k, "c", EF + 64 * e, "1", 0, C)
        mm(5, "c", VR, "1", 0, C)
        mm(6, "c", VL, "1", 0, C)
        mm(7, "c", 128 * RR, "1", 0, C)
        act(w("v1r"), bank(3), F.Sign, -1.0, 1.5)
        act(w("v1l"), bank(4), F.Sign, -1.0, 1.5)
        act(w("vr"), bank(5), F.Copy)
        scan(rev("c1r", 17), rev("kc", 1), rev("v1r", 0), -1.0, A.min, A.mult)
        scan(w("c1l", 16, 464), w("kc", 0, C), w("v1l"), -1.0, A.min, A.mult)
        folded, before, behind = w("sw", 15, None, 16), w("win", MLB, MLB + C, 16), w("win", 31, 464, 16)
        act(sma(NS, 28), folded, F.Copy, -1.0)
        tt(sma(BM, 28), before, behind, A.max)
        tt(w("wb", 0, 28), sma(BM, 28), folded, A.max)
        act(sma(BM, 28), w("wb", 0, 28), F.Abs, 1.25 * 2.0 ** -24, 2.0 ** -124)
        tt(w("wb", 30, 58), w("wb", 0, 28), sma(BM, 28), A.add)
        tt(w("nf", 0, None, 32), behind, folded, A.is_gt)
        tt(w("nf", 30, None, 32), before, folded, A.is_ge)
        for e, a, b in SEARCH:
            row = lambda m: (T.nf[:, 32 * m + 1:32 * m + 30], T.wb[:, m + 1:m + 30], T.sma[:, NS + m:NS + m + 1])
            call = ((lambda o, x, c: S.activation(o, x, F.Sign, bias=c)) if e == "a" else
                    (lambda o, x, c: V.tensor_scalar(o, x, c, 0.0, A.add, A.is_gt)))
            op(e, lambda call=call, a=a, b=b: [call(*row(m)) for m in range(a, b)], [w("wb", 0, 58), sma(NS + a, b - a)],
               [w("nf", 32 * m + 1, 32 * m + 30) for m in range(a, b)], (b - a) * 64 * CYCLE)
        for h in range(2):
            scan(w("run", C * h, C * h + C), w("kl", C * h, C * h + C), w("nf", C * h, C * h + C), 0.0, A.add, A.max)
        ts(off(O_L2), w("run", 31, None, 32), 1024.0, A.mult, 15 + MID - 1024, A.add)
        ts(off(O_L2 + 28), w("run", 28, 866, 31), -1024.0, A.mult, 464.0 + 1024, A.add)
        ts(ni(QQ), off(O_L2, 56), 1.0 / 16, A.mult, -0.46875, A.add)
        ts(w("kd", 3, None, 4), ni(QQ), 16.0, A.mult, w("kd4", 0, 1), A.add)
        for h, got, win, cmp in ((0, "ga", w("win", 0, 464), A.is_ge), (1, "gb", w("win", MLW, 936), A.is_le)):
            for a, b in parts:
                act(w(got, a, b), by(win, part(O_L2 + 28 * h, a, b)), F.Copy)
                tt(w("tb", 512 * h + a, 512 * h + b), w(got, a, b), bank(0, b - a, a), cmp)
            quant("b", 128 * h, 128 * h + 128, w("tb", 512 * h, 512 * h + 512))
            mm(1 + h, "c", C4, "b", 128 * h, 128 * h + 128)
            nd = w("nd", WORDS * h, WORDS * h + WORDS)
            scan(nd, bank(1 + h, WORDS), w("kd", WORDS * h, WORDS * h + WORDS), 0.0, A.max, A.add)
            ts(off(O_LR + 28 * h), w("nd", WORDS * h + 3, WORDS * h + WORDS, 4), col(N4), A.add)
        tt(sma(EE), w("nd", 3, HALF, 4), tab(TE), A.subtract)
        left, right = off(O_LR), off(O_LR + 28)
        act(w("g1l"), by(w("c1l"), left), F.Identity, -0.5, 1.5)
        tt(w("b1r"), by(w("c1r"), right), w("vr"), A.is_equal)
        scan(rev("tb", 512), rev("nrr", 0), rev("b1r", 0), 0.0, A.mult, A.add)
        tt(w("b1l"), w("g1l"), bank(6), A.is_le)
        scan(flags(0), w("nrl"), w("b1l"), 0.0, A.mult, A.add)
        for h in (1, 0):
            quant("b", 128 * h, 128 * h + 128, w("tb", 512 * h, 512 * h + 512))
        mm(1, "c", C5, "b", 128, 256, "c", C5, "b", 0, 128)
        scan(w("nd", HALF), w("kd4", 0, WORDS), bank(1, WORDS), 0.0, A.add, A.max)
        DB = (3, 4, 0, 2)
        for b in range(4):
            mm(DB[b], "c", 128 * b, l_, 0, C)
            act(plane("dec", b), bank(DB[b]), F.Copy)
        tt(ni(IX, 28), w("nd", HALF + 3, None, 4), sma(EE, 28), A.subtract)
        tt(ni(IX + 28, 28), w("nd", HALF + 3, None, 4), sma(EE + 28, 28), A.add)
        ts(ni(SEL), ni(IX), 2 * ODD - 1, A.bitwise_and)
        cp(off(O_W, 56), ni(SEL))
        ts(sma(OW), ni(SEL), -float(ODD), A.add, 0.0, A.max)
        tt(sma(OWN, 28), sma(OW + 28, 28), sma(OW, 28), A.subtract)
        tt(sma(BASE, 28), sma(OWN, 28), tab(TK, 28), A.add)
        for a, b in parts:
            act(w("gw", a, b), by(w("iw"), part(O_W, a, b)), F.Copy)
        tt(w("w2r"), by(w("iw"), off(O_W + 28)), t1(RL), A.mult)
        scan(rev("c2r", 17), rev("kc2", 1), rev("w2r", 0), -MID, A.min, A.add)
        for a, b in parts:
            tt(w("w2l", a, b), w("gw", a, b), bank(7, b - a, a), A.mult)
            scan(w("c2l", 16 + a, 16 + b), w("kc2", a, b), w("w2l", a, b), -MID, A.min, A.add)
        act(w("ga"), by(w("c2r"), right), F.Identity, 1.0, MID)
        for a, b in parts:
            act(w("gb", a, b), by(w("c2l"), part(O_LR, a, b)), F.Identity, col(M15), col(MM15))
        tt(w("g2r"), w("ga"), bank(5), A.mult)
        scan(rev("h2r", 0), rev("nrr", 0), rev("g2r", 0), 0.0, A.mult, A.add)
        for a, b in parts:
            tt(w("g2l", a, b), w("gb", a, b), bank(6, b - a, a), A.mult)
            scan(w("h2l", a, b), w("nrl", a, b), w("g2l", a, b), 0.0, A.mult, A.add)
            tt(w("hh", 16 + a, 16 + b), w("h2r", a, b), w("h2l", a, b), A.subtract)
        for src, dst, n in ((16, 0, SPLIT), (0, C, SPLIT), (16 + SPLIT, SPLIT, C - SPLIT), (SPLIT, C + SPLIT, 480 - SPLIT)):
            turn(w("tt", dst, dst + n), w("hh", src, src + n))
            scan(w("ts", dst, dst + n), w("tt", dst, dst + n), w("ks", 0, n), 0.0, A.add, A.mult)
        tt(sma(AT, 28), w("ts", 15, C, 16), sma(BASE, 28), A.add)
        tt(sma(AT + 32, 28), w("ts", 479, 927, 16), sma(AT, 28), A.add)
        cp(off(O_AT), sma(AT + 32, 28))
        cp(by(w("ord"), off(O_AT)), w("rb"))
        oo = O_O + 32 * rnd
        scan(w("no"), w("kdb"), w("ord"), 0.0, A.add, A.max)
        ts(off(oo), w("no", 15, None, 16), col(NB), A.add)
        came = w("came" + n_)
        send([(came, off(oo + 20, 8), False)], "larr" + n_, "lout" + n_)
        if last:
            act(w("ordf"), w("ord"), F.Identity, 1.0, MID)
            dma("s", T.ol[:], T.ordf[0:128:16, :], [w("ordf")], [], 8 * 1792)

        def scale(e, out, src, f):
            if e == "v":
                ts(out, src, f, A.mult)
            else:
                act(out, src, F.Copy, f)
        old, new = "x64" + "ab"[rnd % 2], "x64" + "ba"[rnd % 2]
        for j, (a, n, eng) in enumerate(LAYER):
            step = lambda t, b: w(t, 4 * a + b, 4 * n, 4)
            pb = 4 * (j % 2)
            for b in range(4):
                if a:
                    scale(eng[b], step("z", b), by(plane(old, b), off(oo + (a - K) // 16, (n - a) // 16)), 1.0 / 64)
                else:
                    scale(eng[b], step("z", b), by(plane("dec", b), came), 1.0)
            quant("z", a, n, w("z", 4 * a, 4 * n))
            for b in range(4):
                scale(eng[5 + b], plane("z64", b, a, n), step("z", b), 64.0)
                mm(pb + b, "w", 128 * b, "z", a, n)
            for b in range(4):
                tt(plane(new, b, a, n), bank(pb + b, n - a), plane("z64", b, a, n), A.add)
                scale(eng[10 + b], step("xs", b), plane(new, b, a, n), 1.0 / 64)
            quant("x", a, n, w("xs", 4 * a, 4 * n))
        for j, (a, n, eng) in enumerate(LAYER):
            mm(4 + j, "v" if last else "p", 0, "x", a, n)
            if last:
                scale(eng[15], w("ysb", a, n), bank(4 + j, n - a), 1.0)
    for a, n in STORES:
        dma("s", T.oc[:, 4 * a:4 * n], T.qx[:, a:n].bitcast(dt.uint8), [codes("x", a, n)], [], 512 * (n - a) + ROWS)
        dma("a", T.y[:, a:n], T.ysb[:, a:n], [w("ysb", a, n)], [], 512 * (n - a) + ROWS)
    for k in range(4):
        dma("s" if k % 2 else "a", T.osc[4 * k:4 * k + 4, :], T["sx_"][32 * k:32 * k + 4, :], [scales("x")], [], 4 * C)
    op("g", None, stored, [], 0.0)
    emit(g, T, ops)
